import numpy as np, ml_dtypes
CORES = [1,5,17,21,33,37,49,53]
N = 8
BF = ml_dtypes.bfloat16
V, B, W, K, L, T, S, RO = 1536, 128, 1792, 128, 5, 44, 1344, 3
def ghosts(a):
    return np.concatenate([a, np.roll(a, 1, 0)[:, :, V - B:], np.roll(a, -1, 0)[:, :, :B]], axis=2)
def home(a):
    b = np.array(a[:, :, :V])
    b[:, :, V - B:] += np.roll(a, -1, 0)[:, :, V:V + B]
    b[:, :, :B] += np.roll(a, 1, 0)[:, :, V + B:]
    return b
def counts(mem):
    a = np.zeros((N, 8, W + 1), np.int64)
    np.add.at(a, (np.arange(N)[:, None, None, None], np.arange(8)[None, :, None, None], mem), 1)
    return home(a[:, :, :W])
def change(q, d, n):
    return np.clip(q + d - np.minimum(np.roll(n, -1, 1), 3), 1, 16)
def grow(vw, tl, t):
    gi = np.arange(8)[:, None]; cell = (np.arange(V) + S * t) % V
    small = vw[:, cell] < 8
    o = np.argsort(~small, axis=1, kind="stable")[:, :K]
    has = np.take_along_axis(small, o, 1); last = cell[o]
    mem = np.full((8, K, L), W); mem[:, :, 0] = np.where(has, last, W)
    size = has.astype(np.int64); tot = np.where(has, vw[gi, last], 0); go = has & (tot < T)
    for j in range(1, L):
        x = tl[gi, :, last]; nm = x >> 4
        sc = (x & 15) * vw[gi[:, :, None], nm]
        sc = np.where(np.any(nm[:, :, :, None] == mem[:, :, None, :j], axis=3), -1, sc)
        k = np.argmax(sc, axis=2)[:, :, None]
        new = np.take_along_axis(nm, k, 2)[:, :, 0]
        go = go & (np.take_along_axis(sc, k, 2)[:, :, 0] >= 0)
        mem[:, :, j] = np.where(go, new, W)
        size = size + go; tot = tot + np.where(go, vw[gi, new], 0)
        last = np.where(go, new, last); go = go & (tot < T)
    return mem, size, tot
def floats(rng):
    broad = rng.random((1, 8, 16, 1)) < 0.4; base = np.exp2(2 * rng.random((1, 8, 16, 1)) - 1)
    z = rng.standard_normal((N, 8, 16, V), dtype=np.float32)
    return np.clip(np.where(broad, np.exp2(4 * rng.random((N, 8, 16, V)) - 2), base * (1 + 0.06 * z)), 0.25, 4.0)
def weights(rng):
    n = np.arange(1, 2 * K + 1); x = rng.random((N, 128, 2 * K))
    return np.where(n < 8, 0.95 + 0.1 * x, 0.6 + 0.8 * x) * np.reciprocal(n.astype(np.float64))
def parts(rng):
    nm = rng.integers(0, W, (N, 8, 16, W)); p = rng.random(nm.shape)
    pool = rng.integers(0, W, (N, 8, 64))
    few = pool[np.arange(N)[:, None, None, None], np.arange(8)[None, :, None, None], rng.integers(0, 64, nm.shape)]
    nm = np.where(p < 0.1, few, np.where(p < 0.2, rng.integers(V, W, nm.shape), np.where(p < 0.23, np.arange(W), nm)))
    return nm, rng.integers(0, 16, nm.shape)
def volumes(rng, share):
    sm = rng.random((N, 8, V)) < share
    return np.where(sm, rng.integers(1, 8, sm.shape), rng.integers(8, 17, sm.shape)), rng.integers(-3, 5, (N, 8, RO, V)), sm
def keep(rng, sm):
    return np.where(sm[:, :, None, :], rng.integers(-1, 1, (N, 8, RO, V)), rng.integers(3, 6, (N, 8, RO, V)))
def hub(rng, nm, al, vol, dv, g, own, far):
    b = nm[:, g]
    al[:, g] = np.where((b == own) | (b == far), al[:, g], np.minimum(al[:, g], 14))
    k = np.argsort(rng.random((N, 16, W)), axis=1)
    for j, c in ((0, own), (1, far)):
        np.put_along_axis(nm[:, g], k[:, j:j + 1], c, axis=1); np.put_along_axis(al[:, g], k[:, j:j + 1], 15, axis=1)
    vol[:, g, own] = 16; dv[:, g, :, own] = 15
def pack(u, nm, al, vol, dv, wt):
    return {"u": np.ascontiguousarray(u.reshape(N, 128, V)).astype(np.float32), "nt": np.ascontiguousarray((16 * nm + al).reshape(N, 128, W)).astype(np.int32),
            "vol": np.ascontiguousarray(vol).astype(np.int32), "dv": np.ascontiguousarray(dv.reshape(N, 8, RO * V)).astype(np.int32), "wt": np.ascontiguousarray(wt).astype(np.float32)}
def setup_inputs(rng):
    nm, al = parts(rng); vol, dv, sm = volumes(rng, rng.choice(np.array([0.04, 0.15, 0.35, 0.6]), (N, 8, 1)))
    return pack(floats(rng), nm, al, vol, dv, weights(rng))
def setup_inputs_spread(rng):
    shape = (N, 8, 16, W)
    nm = np.minimum((W * rng.random(shape) ** 2).astype(np.int64), W - 1); nm[:, 1::2] = W - 1 - nm[:, 1::2]
    al = np.minimum((16 * rng.random(shape) ** 2).astype(np.int64), 15)
    vol = 1 + np.minimum((16 * rng.random((N, 8, V)) ** 2).astype(np.int64), 15); dv = rng.integers(-15, 16, (N, 8, RO, V))
    u = np.exp2(2 * rng.random((N, 8, 16, V)) - 1) * np.exp2(rng.integers(-1, 2, (N, 8, 1, V)))
    return pack(u, nm, al, vol, dv, weights(rng))
def setup_inputs_ends(rng):
    nm, al = parts(rng); p = rng.random(nm.shape); e = rng.integers(0, 2, nm.shape)
    nm = np.where(p < 0.74, e * (W - 1), nm); al = np.where(p < 0.9, 15 * e, al)
    zero = rng.random((N, 8, 1, W)) < 0.05; nm = np.where(zero, 0, nm); al = np.where(zero, 0, al)
    vol = np.where(rng.random((N, 8, V)) < 0.5, 1, 16); dv = np.where(rng.random((N, 8, RO, V)) < 0.5, -15, 15)
    hubs = (7, int(rng.integers(0, 6)))
    for g in hubs: hub(rng, nm, al, vol, dv, g, B - 1, W - 1)
    full = L - 3; chain = [60] + [V - 1, V - 3][:full] + [V - 2, W - 2]; size = [7] + [16] * full + [T - 8 - 16 * full]
    for g in range(8):
        vol[:, g, B - 2] = 16; dv[:, g, 0, B - 2] = 15
        for r in range(N):
            if g in hubs and r < N - 1: continue
            for a, b in zip(chain, chain[1:]):
                nm[r, g, :, a] = b; al[r, g, :, a] = 15
            for a, x in zip(chain, size):
                vol[r, g, a] = x; dv[r, g, 0, a] = 0
            if g not in hubs:
                nm[r, g, :, 61] = 61; vol[r, g, 61] = 1; dv[r, g, 0, 61] = -15
    wt = np.where(rng.random((N, 128, 2 * K)) < 0.5, 0.500001, 1.499999) * np.reciprocal(np.arange(1, 2 * K + 1).astype(np.float64))
    u = floats(rng); u = np.where(rng.random(u.shape) < 0.65, np.where(rng.random(u.shape) < 0.5, 0.25, 4.0), u)
    return pack(u, nm, al, vol, dv, wt)
def setup_inputs_corners(rng):
    nm, al = parts(rng); col = np.arange(W); k = np.arange(16)[:, None]; sh = int(rng.integers(0, 6))
    many = np.array([0, 1, K - 1, K, K + 1, V])[(3 * np.arange(N)[:, None] + np.arange(8)[None, :] + sh) % 6]
    draw = rng.random((N, 8, V)); way = (S * np.arange(RO) - 1) % V
    draw[:, :, way] = np.where((many == K)[:, :, None], -1.0, draw[:, :, way])
    sm = np.argsort(np.argsort(draw, axis=2), axis=2) < many[:, :, None]
    vol = np.where(sm, rng.integers(1, 8, sm.shape), rng.integers(8, 17, sm.shape)); e = rng.integers(0, 4, (N, 8, 1))
    vol = np.where(e == 1, np.where(sm, 1, 16), np.where(e == 2, np.where(sm, 7, 8), vol)); dv = keep(rng, sm)
    z = rng.integers(0, 16, (N, 8, 1, W)); one = rng.integers(0, W, (N, 8, 1, W))
    ends = np.array([0, V - 1, V, V + B - 1, V + B, W - 1])[rng.integers(0, 6, nm.shape)]
    nm = np.where(z == 0, col, np.where(z == 1, np.where(k == (col & 15), one, col), np.where(z == 2, one, np.where(z < 5, ends, nm))))
    a = rng.integers(0, 8, (N, 8, 1, W)); al = np.where(a == 0, 0, np.where(a == 1, 15, al))
    return pack(floats(rng), nm, al, vol, dv, weights(rng))
def setup_inputs_crowd(rng):
    nm, al = parts(rng); vol, dv, sm = volumes(rng, 0.5); dv = keep(rng, sm); sh = int(rng.integers(0, 4))
    hs = [int(x) for x in V - 100 + rng.permutation(80)[:8]]
    four = np.array([V - 10, V - 10 + B, 5, V + B + 5])
    for g in range(8):
        m = (g + sh) % 4
        if m < 2: hub(rng, nm, al, vol, dv, g, hs[g], hs[g] + B)
        if m == 1:
            for r in range(0, N, 2):
                nm[r, g, :, 40] = 40; vol[r, g, 40] = 5; dv[r, g, :, 40] = 0
        if m == 2: nm[:, g] = four[rng.integers(0, 4, (N, 16, W))]
    for g in range(8):
        if (g + sh) % 4 < 2:
            p = (g - 1) % 8; vol[:, p, hs[g]] = 12; dv[:, p, 0, hs[g]] = 0; dv[:, p, 1, hs[g]] = rng.integers(-2, 0, N); dv[:, p, 2:, hs[g]] = 3
    return pack(floats(rng), nm, al, vol, dv, weights(rng))
def setup_inputs_calm(rng):
    nm, al = parts(rng); vol, dv, sm = volumes(rng, 0.3); kind = (np.arange(8) + int(rng.integers(0, 4))) % 4
    late, turn = [int(g) for g in np.flatnonzero(kind == 0)]
    vol[:, late] = rng.integers(8, 17, (N, V))
    for g in range(8):
        if kind[g] >= 2:
            pool = rng.permutation(W)[:120 if kind[g] == 2 else 300]; nm[:, g] = pool[rng.integers(0, len(pool), (N, 16, W))]
    tl = 16 * nm + al; dv[:, :, 0] = 0; q = vol
    for t in range(1, RO):
        none = ((np.arange(8) == turn) & (t % 2 == 1))[None, :, None]
        vw = ghosts(q); n = counts(np.stack([grow(vw[r], tl[r], t - 1)[0] for r in range(N)]))
        h = np.minimum(np.roll(n, -1, 1), 3); goal = np.where(none, 8, rng.integers(7, 9, q.shape))
        dv[:, :, t] = np.where((rng.random(q.shape) < 0.6) | (none & (q < 8)), goal - q + h, np.where(none, 3, 0))
        q = change(q, dv[:, :, t], n)
    return pack(floats(rng), nm, al, vol, dv, weights(rng))
def check_ranges(d):
    bad = []
    for k, lo, hi in (("nt", 0, 16 * W - 1), ("vol", 1, 16), ("dv", -15, 15)):
        if np.min(d[k]) < lo or np.max(d[k]) > hi: bad.append("range of " + k)
    if not (np.min(d["u"]) >= 0.25 and np.max(d["u"]) <= 4): bad.append("range of u")
    p = np.asarray(d["wt"], np.float64) * np.arange(1, 2 * K + 1)
    if not (np.min(p) >= 0.5 and np.max(p) <= 1.5): bad.append("range of wt")
    return bad
def reference(u, nt, vol, dv, wt):
    x = u.astype(np.float64).reshape(N, 8, 16, V).transpose(0, 1, 3, 2)
    tl = nt.astype(np.int64).reshape(N, 8, 16, W); w = wt.astype(np.float64).reshape(N, 8, 16, 2 * K).transpose(0, 1, 3, 2)
    q = vol.astype(np.int64); d = dv.astype(np.int64).reshape(N, 8, RO, V)
    n = np.zeros((N, 8, V), np.int64); gi = np.arange(8)[:, None]; g3 = gi[:, :, None]
    for t in range(RO):
        q = change(q, d[:, :, t], n); vw = ghosts(q); xw = ghosts(x)
        total = np.zeros((N, 8, W + 1, 16)); named = []
        for r in range(N):
            mem, size, tot = grow(vw[r], tl[r], t); named.append(mem); there = mem < W
            m = np.minimum(np.where(there, mem, mem[:, :, :1]), W - 1)
            um = xw[r][g3, m]
            mean = np.add.reduce(np.where(there, vw[r][g3, m], 0)[..., None] * um, axis=2) * w[r][gi, np.maximum(tot, 1) - 1]
            slope = 0.5 * (np.take_along_axis(um, np.maximum(size - 1, 0)[:, :, None, None], 2)[:, :, 0] - um[:, :, 0])
            un = xw[r][g3[:, :, :, None], tl[r][g3, :, m] >> 4]
            lo = np.min(un, axis=(2, 3)); hi = np.max(un, axis=(2, 3))
            c = 0.125 * (2 * np.arange(L) - (size - 1)[:, :, None])
            est = np.clip(mean[:, :, None] + slope[:, :, None] * c[..., None], lo[:, :, None], hi[:, :, None])
            np.add.at(total[r], (g3, mem), est)
        n = counts(np.stack(named)); s = home(total[:, :, :W])
        wn = np.stack([w[r][gi, np.maximum(n[r], 1) - 1] for r in range(N)])
        x = np.where((n > 0)[..., None], s * wn, x)
    return {"y": np.ascontiguousarray(x.transpose(0, 1, 3, 2)).reshape(N, 128, V).astype(np.float32)}

def check_inputs(d):
    bad = list(check_ranges(d))
    if not bad:
        for name, y in reference(**d).items():
            for q in range(N):
                v = np.abs(np.asarray(y[q], np.float64)); s = np.sqrt(np.mean(v * v))
                if v.max() > 11 * s or s < 2.0 ** -1: bad.append('%s of rank %d is uneven or too small' % (name, q))
    return bad

@@ -1,0 +1,677 @@
+import math
+from concourse.bass import DstId, RemoteDMATransfer
+from concourse.mybir import AluOpType, ActivationFunctionType
+
+AL = AluOpType
+AF = ActivationFunctionType
+V, W, RO, STEP = 1536, 1792, 3, 1344
+F, B, I, U16 = "float32", "bfloat16", "int32", "uint16"
+SPLIT = (64, 0, 0)
+LV = 2
+UB = (LV - 1) * W
+HELP = ((), (), ())
+BIAS = (0, 0, 10, 5, 0, 0, 0, 20, 5)
+STATS = {}
+
+SCRATCH = {}
+
+
+def _sb(names, shape, dtype):
+    for n in names.split():
+        SCRATCH[n] = ("sbuf", [128] + list(shape), dtype)
+
+
+_sb("VD ntb", [W], I)
+_sb("VDb", [V], B)
+_sb("At volE", [W], B)
+_sb("Gt", [W + 16], B)
+_sb("W0 W1", [UB + 2 * W], F)
+_sb("wall", [768], F)
+_sb("S Z0", [1920], F)
+_sb("Rb0 Rb1 Rb2", [512], F)
+_sb("dvO", [112, 3], F)
+_sb("Ug", [4, 1280], F)
+_sb("Omin Omax", [1280], F)
+_sb("Zh0 Zh1 Zl0 Zl1", [8, 240], B)
+_sb("Cq", [3, 143], B)
+_sb("pid", [4], I)
+_sb("r8", [16], I)
+_sb("col", [16], F)
+_sb("rows", [3, 128], F)
+_sb("cf", [5, 128], F)
+_sb("cb", [5, 128], B)
+_sb("M16", [16], F)
+_sb("cm aBf", [8], F)
+_sb("aB", [8], B)
+_sb("Rq", [16, 128], B)
+_sb("Dq", [144], B)
+_sb("wpad", [240], B)
+_sb("selP", [8, 128], B)
+_sb("xr1 ring volN", [112], B)
+_sb("xtab", [3, 112], B)
+_sb("cid qu qa qq hh st1", [112], F)
+_sb("lane biasL dump thr", [40], F)
+_sb("smallR junk", [96], B)
+_sb("Cc", [96], F)
+_sb("Pw", [104], F)
+_sb("acc", [8], F)
+_sb("x16", [8], U16)
+_sb("cmpb XE ag Hs", [128], B)
+_sb("b16", [4, 128], U16)
+_sb("bf aT tk key sc mk wZ Mm Dd De c1", [128], F)
+_sb("Vg", [2048], B)
+_sb("eq", [4, 128], B)
+_sb("Bc", [5, 128], F)
+_sb("o16 nA16", [40], U16)
+_sb("volM OHlo", [640], B)
+_sb("OH", [40, 112], B)
+_sb("ne hc cc sm t40 mm", [40], F)
+_sb("nS", [32], F)
+_sb("EQ0 EQ1", [8, 512], B)
+_sb("Wb", [512], B)
+_sb("um prod est ec", [640], F)
+_sb("Ss tg", [4, 128], F)
+_sb("b16a", [RO, 640], U16)
+_sb("oM16 off16", [RO, 40], U16)
+_sb("z16", [RO, 8], U16)
+_sb("nO th", [RO, 40], F)
+_sb("vtO", [RO, 48], B)
+_sb("G", [RO, 640], B)
+_sb("nR", [RO, 32], F)
+_sb("nF", [RO, 112], B)
+_sb("nOff sel", [112], U16)
+for _k in range(8):
+    SCRATCH["P%d" % _k] = ("psum", [128, 512], F)
+
+SEMAPHORES = ["c_vector", "c_scalar", "c_tensor", "c_pool"] + ["d%d" % k for k in range(20)] + \
+             ["ls%d" % k for k in range(9)] + ["ar%d" % k for k in range(9)]
+
+CY = 0.83e-3 * 1.2
+PCY = 0.42e-3 * 1.2
+GA, SCA = 1.56, 3.8
+LAT_X, LAT_S, WINDOW = 0.12, 0.05, 0.1
+
+
+def rank_program(g, core, T, topo):
+    rank = T.rank_of(core)
+    if rank is None:
+        return
+    cores = list(T.cores)
+    n_r = len(cores)
+    prev, nxt = cores[(rank - 1) % n_r], cores[(rank + 1) % n_r]
+
+    def share(src):
+        r = cores.index(src)
+        nb = [cores[(r - 1) % n_r], cores[(r + 1) % n_r]]
+        out, used = {}, []
+        for d in sorted(nb, key=lambda d: len(topo.engines(src, d))):
+            e = [x for x in topo.engines(src, d) if x not in used]
+            e = e[:8] if used else e[:max(1, min(8, len(set(topo.engines(src, nb[0]) + topo.engines(src, nb[1]))) // 2))]
+            out[d] = e
+            used = used + e
+        return out
+
+    ops, log, bias = [], {}, [0.0]
+    S_ = slice
+
+    def v(name, *idx, p=None):
+        if name not in SCRATCH:
+            return {"ap": T[name][(S_(None) if p is None else p,) + idx], "r": []}
+        where, shape, _ = SCRATCH[name]
+        free = shape[1:]
+        idx = tuple(idx) + (S_(None),) * (len(free) - len(idx))
+        lo = hi = 0
+        stride = 1
+        for d, i in zip(reversed(free), reversed(idx)):
+            r = range(d)[i] if isinstance(i, slice) else [i]
+            lo += min(r[0], r[-1]) * stride
+            hi += max(r[0], r[-1]) * stride
+            stride *= d
+        if where == "psum":
+            lo, hi = 0, 511
+        return {"ap": T[name][(S_(None) if p is None else p,) + idx], "r": [(name, lo, hi + 1)]}
+
+    def c(name, a, b, s=1, p=None):
+        return v(name, S_(a, b, s), p=p)
+
+    def ind(win, off):
+        return {"ap": win["ap"].indirect(off["ap"]), "r": win["r"], "x": off["r"]}
+
+    def op(eng, dur, fn, reads, writes, kind="c", extra=None):
+        me = len(ops)
+        deps = set()
+        acc = []
+        for x in reads:
+            if isinstance(x, dict):
+                acc += [(r, r[0][0] == "P" and r[0][1:].isdigit()) for r in x["r"]] + [(r, False) for r in x.get("x", [])]
+        for x in writes:
+            acc += [(r, True) for r in x["r"]] + [(r, False) for r in x.get("x", [])]
+        for (name, lo, hi), wr in acc:
+            for (l2, h2, o, w2) in log.get(name, []):
+                if o != me and l2 < hi and lo < h2 and (wr or w2):
+                    deps.add(o)
+        for (name, lo, hi), wr in acc:
+            lst = log.setdefault(name, [])
+            if wr:
+                lst[:] = [e for e in lst if not (lo <= e[0] and e[1] <= hi)]
+            lst.append((lo, hi, me, wr))
+        if extra is not None:
+            deps.add(extra)
+        ops.append({"e": eng, "d": dur, "f": fn, "deps": deps, "k": kind, "b": bias[0], "w": [x["r"][0][0] for x in writes if x["r"]]})
+        return me
+
+    def a_(x):
+        return x["ap"] if isinstance(x, dict) else x
+
+    def vd(n, x=None, o=None):
+        if o is not None and "x" in o:
+            return 0.05 + SCA * n * CY
+        if x is not None and "x" in x:
+            return 0.05 + GA * n * CY
+        return 0.03 + max(64, n) * CY
+
+    def cp(o, x, n):
+        op("vector", vd(n, x, o), lambda q: q.tensor_copy(o["ap"], x["ap"]), [x], [o])
+
+    def tt(o, x, y, f, n):
+        op("vector", vd(n, x), lambda q: q.tensor_tensor(o["ap"], x["ap"], y["ap"], f), [x, y], [o])
+
+    def ts(o, x, s1, f1, n, s2=None, f2=None):
+        if s2 is None:
+            op("vector", vd(n, x), lambda q: q.tensor_scalar(o["ap"], x["ap"], a_(s1), None, f1), [x, s1], [o])
+        else:
+            op("vector", vd(n, x), lambda q: q.tensor_scalar(o["ap"], x["ap"], a_(s1), a_(s2), f1, f2), [x, s1, s2], [o])
+
+    def scan(o, d0, d1, init, f0, f1, n):
+        op("vector", vd(n), lambda q: q.tensor_tensor_scan(o["ap"], d0["ap"], d1["ap"], init, f0, f1), [d0, d1], [o])
+
+    def ms(o, val, n):
+        op("vector", vd(n), lambda q: q.memset(o["ap"], val), [], [o])
+
+    def act(o, x, n, f=AF.Copy, bias=None, scale=None, accum=None):
+        k = {}
+        if bias is not None:
+            k["bias"] = a_(bias)
+        if scale is not None:
+            k["scale"] = a_(scale)
+        if accum is not None:
+            k["accum_out"] = accum["ap"]
+        d = 0.07 + (GA * n if "x" in x else max(64, n)) * CY + (1.3 if f == AF.Exp and not first_exp else 0)
+        if f == AF.Exp:
+            first_exp.append(1)
+        op("scalar", d, lambda q: q.activation(o["ap"], x["ap"], f, **k), [x, bias, scale], [o] + ([accum] if accum else []))
+
+    first_exp = []
+
+    def mm(lst, after=None):
+        def f(q):
+            for (o, l, r, st, sp, _) in lst:
+                ins = q.matmul(o["ap"], l["ap"], r["ap"], st, sp)
+            return ins
+        return op("tensor", 0.06 + sum(x[5] for x in lst) * PCY, f, [x[1] for x in lst] + [x[2] for x in lst],
+                  [x[0] for x in lst], extra=after)
+
+    def iota(o, pat, base, cmul, n, flt=True):
+        k = {"allow_small_or_imprecise_dtypes": True} if flt else {}
+        op("pool", 0.13 + 2 * n * CY, lambda q: q.iota(o["ap"], pat, base, cmul, **k), [], [o])
+
+    def asel(o, x, pat, f, fill, base, cmul, n):
+        op("pool", 0.17 + 2 * n * CY, lambda q: q.affine_select(o["ap"], x["ap"], pat, f, fill, base, cmul), [x], [o])
+
+    def dma(queue, o, x, us):
+        op(queue, us, lambda q: q.dma_start(o["ap"], x["ap"]), [x], [o], kind="dma")
+
+    n_x = [0]
+
+    def exchange(to_prev, to_next, us):
+        k = n_x[0]
+        n_x[0] += 1
+        mine = share(core)
+        trs = []
+        for d, lst in ((prev, to_prev), (nxt, to_next)):
+            rid, pid, _ = topo.addr(d)
+            per = len(mine[d]) // len(lst)
+            for i, (s, o) in enumerate(lst):
+                mask = sum(1 << e for e in mine[d][i * per:(i + 1) * per])
+                trs.append(RemoteDMATransfer(dst_ids=[DstId(rid=rid, pnc=pid)], dma_engine_mask=mask,
+                                             remote_sem=T.sem["ar%d" % k], src=s["ap"], dst=o["ap"]))
+        sent = len(mine[prev]) + len(mine[nxt])
+        come = len(share(prev)[core]) + len(share(nxt)[core])
+        s = op("pool", us, lambda q: q.remote_dma_fused(trs, local_sem=T.sem["ls%d" % k]),
+               [x[0] for x in to_prev + to_next], [], kind=("ls%d" % k, sent))
+        op("ext", 0.6, None, [], [x[1] for x in to_prev + to_next], kind=("ar%d" % k, come), extra=s)
+
+    p32 = S_(0, 32)
+    bias[0] = 1000.0
+    dma("sync", c("VD", 0, V, p=S_(0, 8)), v("vol", S_(None)), 2.2)
+    dma("scalar", {"ap": c("VD", 0, V, p=S_(8, 32))["ap"], "r": [("VDx", 0, 1)]}, v("dv", S_(None)), 2.4)
+    bias[0] = 500.0
+    dma("sync", v("ntb"), v("nt", S_(None)), 5.5)
+    bias[0] = 0.0
+    dma("scalar", c("wall", 0, 256), v("wt", S_(None)), 5.0)
+    dma("scalar", c("W0", UB, UB + V), v("u", S_(None)), 9.0)
+
+    ms(v("Cq", p=p32), 1.0, 215)
+    asel(v("Cq", p=p32), v("Cq", p=p32), [[-16, 3], [-3, 143]], AL.is_equal, 0.0, -83, 16, 429)
+    asel(v("Cq", 0, p=p32), v("Cq", 0, p=p32), [[-1, 143]], AL.not_equal, 1.0, 15, 16, 143)
+    iota(c("pid", 0, 1), [[0, 1]], 0, 1, 1, False)
+    iota(v("rows", 0), [[1, 128]], 0, 0, 128)
+    iota(v("rows", 1), [[0, 8], [1, 16]], 0, 0, 128)
+    iota(v("rows", 2), [[1, 8], [0, 16]], 0, 0, 128)
+    iota(v("lane"), [[0, 5], [16, 8]], 0, 0, 40)
+    ts(c("pid", 1, 2), c("pid", 0, 1), 15, AL.bitwise_and, 1)
+    ts(c("pid", 2, 3), c("pid", 0, 1), 4, AL.arith_shift_right, 1)
+    qc, gc, kc, shc, alc, wc, pc = [c("col", k, k + 1) for k in range(7)]
+    cp(qc, c("pid", 1, 2), 1)
+    cp(gc, c("pid", 2, 3), 1)
+    cp(pc, c("pid", 0, 1), 1)
+    ts(kc, qc, -2048.0, AL.mult, 1, 32768.0, AL.add)
+    ts(shc, pc, 111.5, AL.is_gt, 1, -128.0, AL.mult)
+    ts(shc, shc, pc, AL.add, 1, 16.0, AL.add)
+    lrow, qrow, grow = v("rows", 0), v("rows", 1), v("rows", 2)
+    If, rmask, qmask, unsc, d1 = [v("cf", k) for k in range(5)]
+    unsc = v("cf", 3, S_(0, 32))
+    Ib, bo, up, negI, shm = [v("cb", k) for k in range(5)]
+    bo8 = v("cb", 1, S_(0, 128, 16))
+    ts(bo, grow, gc, AL.is_equal, 128)
+    ts(v("tk"), qrow, qc, AL.is_lt, 128)
+    tt(up, v("tk"), bo, AL.mult, 256)
+    ts(v("lane"), v("lane"), qc, AL.add, 40)
+    ts(v("biasL"), v("lane"), -1.0, AL.mult, 40, -0.5, AL.add)
+    ts(If, lrow, pc, AL.is_equal, 128)
+    ts(Ib, lrow, pc, AL.is_equal, 128)
+    ts(negI, lrow, pc, AL.is_equal, 128, -16777216.0, AL.mult)
+    ts(shm, lrow, shc, AL.is_equal, 128)
+    ts(rmask, qrow, 0.5, AL.is_gt, 128)
+    qmask = c("P0", 256, 384)
+    ts(qmask, qrow, qc, AL.is_equal, 128)
+    ts(v("M16"), v("rows", 0, S_(0, 16)), qc, AL.is_equal, 16)
+    ts(v("cm"), v("rows", 0, S_(0, 8)), gc, AL.is_equal, 8)
+    ms(d1, -2048.0, 128)
+    ms(c("Pw", 96, 104), 1e6, 8)
+    ms(c("ne", 0, 8), 1.0, 8)
+    for q in range(16):
+        act(v("Rq", q), bo, 128, scale=c("M16", q, q + 1))
+    ms(v("Dq"), 0.0, 72)
+    ts(c("Dq", 15, 143), Ib, c("M16", 0, 1), AL.mult, 64)
+    for t in range(RO):
+        x0 = (STEP * t) % V // 16
+        ts(v("xtab", t, S_(0, 96 - x0)), v("rows", 0, S_(0, 96 - x0)), float(x0), AL.add, 96)
+        if x0:
+            cp(v("xtab", t, S_(96 - x0, 96)), v("rows", 0, S_(0, x0)), 96)
+        ms(v("xtab", t, S_(96, 112)), 0.0, 16)
+    ts(v("xr1"), v("rows", 0, S_(0, 112)), 1.0, AL.add, 112)
+    cp(c("ring", 0, 8), c("xr1", 96, 104), 8)
+    cp(c("ring", 8, 104), c("xr1", 0, 96), 48)
+    cp(c("ring", 104, 112), c("xr1", 104, 112), 8)
+    for q in range(16):
+        act(c("Gt", q, W, 16), v("xr1"), 112, scale=c("M16", q, q + 1))
+    ms(c("Gt", W, W + 16), 0.0, 16)
+    ts(v("cid"), v("rows", 0, S_(0, 112)), 16.0, AL.mult, 112, qc, AL.add)
+    ts(v("dump"), v("lane"), float(W), AL.add, 40)
+    ln2 = math.log(2.0)
+    ts(c("col", 8, 9), qc, 7 * ln2, AL.mult, 1, -52 * ln2, AL.add)
+    ts(c("col", 9, 10), pc, -ln2, AL.mult, 1, 63 * ln2, AL.add)
+    act(c("col", 4, 6), c("col", 8, 10), 2, AF.Exp)
+    ts(v("t40"), v("lane"), -ln2, AL.mult, 40, 63 * ln2 + math.log(2.5), AL.add)
+    act(v("thr"), v("t40"), 40, AF.Exp)
+    ts(v("aB"), v("cm"), alc, AL.mult, 8)
+    cp(v("aBf"), v("aB"), 8)
+    for k in range(8):
+        act(v("selP", k), lrow, 128, AF.Identity, bias=c("aBf", k, k + 1), scale=0.0)
+    ms(v("wpad"), 0.0, 120)
+    ts(c("wpad", 112, 128), v("M16"), 0.0, AL.mult, 16, wc, AL.add)
+    for s in range(LV):
+        ms(v("cf", 3, S_(s, 32, LV)), 256.0 ** s, 8)
+    ms(c("Z0", 0, 96), 0.0, 96)
+    for k in range(4):
+        iota(c("Z0", 96 + 456 * k, 552 + 456 * k), [[0, 456]], 0, 0, 456)
+    for n in ("Zh1", "Zl1", "Zh0", "Zl0"):
+        for k in range(4):
+            iota(v(n, S_(2 * k, 2 * k + 2)), [[0, 480]], 0, 0, 480)
+
+    for a in (0, 768):
+        x = c("VD", a, a + 768, p=p32)
+        cp(c("VDb", a, a + 768, p=p32), {"ap": x["ap"], "r": x["r"] + [("VDx", 0, 1)]}, 768)
+    for t in range(RO):
+        bank = "P%d" % (3 + t)
+        mm([(c(bank, 0, 96), v("Cq", t, S_(15 - q, 143 - q), p=p32), c("VDb", q, V, 16, p=p32), q == 0, q == 15, 96)
+            for q in range(16)])
+        cp(v("dvO", S_(8, 104), t), c(bank, 0, 96), 96)
+    exchange([(v("dvO", S_(8, 16)), v("dvO", S_(104, 112)))], [(v("dvO", S_(96, 104)), v("dvO", S_(0, 8)))], 4.0)
+    exchange([(c("W0", UB, UB + 128), c("W0", UB + 1664, UB + W))],
+             [(c("W0", UB + 1408, UB + V), c("W0", UB + V, UB + 1664))], 2.5)
+
+    def scaled(name, a, b):
+        for s in range(1, LV):
+            act(c(name, (s - 1) * W + a, (s - 1) * W + b), c(name, UB + a, UB + b), b - a, scale=256.0 ** -s)
+    for h in range(4):
+        scaled("W0", 448 * h, 448 * h + 448)
+    exchange([(c("wall", 0, 256), c("wall", 512, 768))], [(c("wall", 0, 256), c("wall", 256, 512))], 2.5)
+    for h in range(4):
+        ts(c("VD", 448 * h, 448 * h + 448), c("ntb", 448 * h, 448 * h + 448), 15, AL.bitwise_and, 448)
+        ts(c("At", 448 * h, 448 * h + 448), c("VD", 448 * h, 448 * h + 448), 32768.0, AL.mult, 448)
+
+    def tile_names(o, off):
+        ts(o, ind(v("ntb"), off), 0.0625, AL.mult, 128, -0.46875, AL.add)
+
+    def publish(j):
+        ts(v("cf", 4, S_(0, 128, 16)), c("r8", 8, 16), 32768.0, AL.add, 8)
+        scan(v("Bc", j), rmask, d1, 0.0, AL.mult, AL.add, 128)
+        tt(v("mk"), qmask, v("Bc", j), AL.mult, 128)
+        mm([(c("P1", 128, 136), v("mk"), v("cm"), True, True, 256)])
+        ts(c("o16", 8 * j, 8 * j + 8), c("P1", 128, 136), kc, AL.subtract, 8)
+
+    def lane_major(t, j, x):
+        for s in range(LV):
+            ts(v("b16a", t, S_(5 * s + j, 640, 5 * LV)), v("b16", x, S_(s, 128, LV)), float((s - 1) * W if s else UB), AL.add, 32)
+
+    def one_round(t):
+        last = t == RO - 1
+        x0 = (STEP * t) % V // 16
+        Wt = "W%d" % (t % 2)
+        if t == 0:
+            def qv(a, b):
+                return v("dvO", S_(a, b), 0)
+        else:
+            ts(v("hh"), v("nF", t - 1), 3.0, AL.min, 112)
+            tt(v("qu"), v("qa"), v("hh"), AL.subtract, 224)
+
+            def qv(a, b):
+                return c("qu", a, b)
+        ts(c("smallR", 0, 96 - x0), qv(8 + x0, 104), 7.5, AL.is_lt, 96 - x0)
+        if x0:
+            ts(c("smallR", 96 - x0, 96), qv(8, 8 + x0), 7.5, AL.is_lt, x0)
+        ts(c("volN", 0, 96), qv(8, 104), 1.0, AL.max, 96, 16.0, AL.min)
+        ts(c("volN", 96, 104), qv(0, 8), 1.0, AL.max, 8, 16.0, AL.min)
+        ts(c("volN", 104, 112), qv(104, 112), 1.0, AL.max, 8, 16.0, AL.min)
+        if not last:
+            ts(v("qq"), qv(0, 112), 1.0, AL.max, 112, 16.0, AL.min)
+            tt(v("qa"), v("qq"), v("dvO", S_(None), t + 1), AL.add, 224)
+        mm([(c("P2", 0, 96), bo, v("smallR"), True, True, 96), (c("P2", 128, 224), up, v("smallR"), True, True, 96)])
+        scan(v("Cc"), c("P2", 0, 96), c("Z0", 0, 96), 0.0, AL.add, AL.add, 96)
+        tt(c("Pw", 0, 96), v("Cc"), c("P2", 128, 224), AL.subtract, 96)
+        for k in range(8):
+            act(v("junk"), v("Cc"), 96, AF.Sign, bias=c("biasL", k, k + 1), accum=c("acc", k, k + 1))
+        ts(v("x16"), v("acc"), -0.5, AL.mult, 8, 48.0, AL.add)
+        tt(v("cmpb"), ind(v("Pw"), v("x16")), lrow, AL.is_le, 128)
+        act(v("XE"), ind(v("xtab", t), v("x16")), 128)
+        mm([(c("P2", 256, 264), v("cmpb"), bo8, True, False, 64), (c("P2", 256, 264), v("XE"), bo8, False, True, 64)])
+        cp(c("r8", 8, 16), c("P2", 256, 264), 8)
+        publish(0)
+        ts(v("mm"), v("lane"), c("Cc", 95, 96), AL.is_lt, 40)
+        for h in range(4):
+            bank = "P%d" % (3 + h % 2)
+            mm([(c(bank, q, 448, 16), v("Rq", q), c("volN", 28 * h, 28 * h + 28), True, True, 64) for q in range(16)])
+            act(c("volE", 448 * h, 448 * h + 448), c(bank, 0, 448), 448)
+        yield
+        for j in range(1, 5):
+            off = c("o16", 8 * j - 8, 8 * j)
+            tile_names(v("b16", j - 1), off)
+            act(v("ag"), ind(v("At"), off), 128)
+            sp = SPLIT[t]
+            if sp:
+                cp(c("Vg", 0, 16 * sp), ind(v("volE"), v("b16", j - 1, S_(0, sp))), 16 * sp)
+            act(c("Vg", 16 * sp, 2048), ind(v("volE"), v("b16", j - 1, S_(sp, 128))), 2048 - 16 * sp)
+            ts(v("bf"), v("b16", j - 1), kc, AL.add, 128)
+            mm([(c("P0", 128, 256), v("bf"), If, True, True, 512), (c("P0", 0, 128), v("ag"), Ib, True, True, 128)])
+            for i in range(j):
+                tt(v("eq", i), c("P0", 128, 256), v("Bc", i), AL.is_equal, 128)
+            act(v("aT"), c("P0", 0, 128), 128)
+            mm([(c("P1", 0, 128), v("bf"), If, True, False, 512)] +
+               [(c("P1", 0, 128), negI, v("eq", i), False, i == j - 1, 128) for i in range(j)])
+            mm([(c("P2", k, 128, 16), c("Vg", k, 2048, 16), v("cb", 0, S_(0, 128, 16)), True, True, 64) for k in range(16)])
+            tt(v("tk"), c("P2", 0, 128), v("aT"), AL.mult, 128)
+            tt(v("key"), c("P1", 0, 128), v("tk"), AL.add, 128)
+            scan(v("sc"), rmask, v("key"), 0.0, AL.mult, AL.max, 128)
+            tt(c("r8", 0, 8), c("sc", 15, 128, 16), c("r8", 8, 16), AL.max, 8)
+            ts(c("r8", 8, 16), c("r8", 0, 8), 2047, AL.bitwise_and, 8)
+            publish(j)
+            lane_major(t, j - 1, j - 1)
+        nO = lambda a, b: v("nO", t, S_(a, b))
+        th = lambda a, b: v("th", t, S_(a, b))
+        vt = lambda a, b: v("vtO", t, S_(a, b))
+        Gj = lambda j: v("G", t, S_(128 * j, 128 * j + 128))
+        p112 = S_(0, 112)
+
+        def one_hot(a, b):
+            ts(c("t40", 8 * a, 8 * b), nO(8 * a, 8 * b), -float(W), AL.add, 40)
+            tt(c("t40", 8 * a, 8 * b), c("t40", 8 * a, 8 * b), th(8 * a, 8 * b), AL.mult, 64)
+            ts(c("nA16", 8 * a, 8 * b), c("t40", 8 * a, 8 * b), float(W), AL.add, 40)
+            act(v("G", t, S_(128 * a, 128 * b)), ind(v("Gt"), c("nA16", 8 * a, 8 * b)), 128 * (b - a))
+            mm([(c("P4", 8 * j, 8 * j + 8), Gj(j), bo8, True, True, 64) for j in range(a, b)])
+            cp(c("hc", 8 * a, 8 * b), c("P4", 8 * a, 8 * b), 40)
+            mm([(c("P3", 128 * (j - a), 128 * (j - a + 1)), Gj(j), Ib, True, True, 128) for j in range(a, b)])
+            act(c("OHlo", 128 * a, 128 * b), c("P3", 0, 128 * (b - a)), 128 * (b - a), AF.Sign)
+            for k in range(8):
+                for j in range(a, b):
+                    ts(v("OH", 5 * k + j), v("ring"), c("hc", 8 * j + k, 8 * j + k + 1), AL.is_equal, 56)
+
+        def volumes(a, b):
+            act(c("volM", 128 * a, 128 * b), ind(v("volE"), v("oM16", t, S_(8 * a, 8 * b))), 128 * (b - a))
+            mm([(c("P4", 64, 64 + 8 * (b - a)), c("Dq", 15 - q, 143 - q), c("volM", 128 * a + q, 128 * b, 16), q == 0, q == 15, 64)
+                for q in range(16)])
+            tt(vt(8 * a, 8 * b), c("P4", 64, 64 + 8 * (b - a)), th(8 * a, 8 * b), AL.mult, 40)
+
+        cp(nO(0, 32), c("o16", 0, 32), 32)
+        cp(v("oM16", t, S_(0, 32)), c("o16", 0, 32), 32)
+        tt(c("ne", 8, 32), nO(8, 32), nO(0, 24), AL.not_equal, 48)
+        tt(th(0, 32), c("ne", 0, 32), c("mm", 0, 32), AL.mult, 64)
+        volumes(0, 4)
+        tt(c("sm", 0, 16), vt(0, 16), vt(16, 32), AL.add, 32)
+        tt(c("sm", 16, 24), c("sm", 0, 8), c("sm", 8, 16), AL.add, 16)
+        ts(c("sm", 24, 32), c("sm", 16, 24), 43.5, AL.is_lt, 8)
+        one_hot(0, 4)
+        cp(nO(32, 40), c("o16", 32, 40), 8)
+        tt(c("sm", 32, 40), nO(32, 40), nO(24, 32), AL.subtract, 16)
+        tt(c("sm", 32, 40), c("sm", 32, 40), c("sm", 24, 32), AL.mult, 16)
+        tt(nO(32, 40), nO(24, 32), c("sm", 32, 40), AL.add, 16)
+        ts(c("ne", 32, 40), c("sm", 32, 40), 0.0, AL.not_equal, 8)
+        tt(th(32, 40), c("ne", 32, 40), c("mm", 32, 40), AL.mult, 16)
+        one_hot(4, 5)
+        cp(v("oM16", t, S_(32, 40)), nO(32, 40), 8)
+        tile_names(v("b16", 0), v("oM16", t, S_(32, 40)))
+        lane_major(t, 4, 0)
+        mm([(c("P3", 16 * ((k - 1) % 8), 16 * ((k - 1) % 8) + 16, p=p112), v("OH", 5 * k + j),
+             c("OHlo", 128 * j + 16 * k, 128 * j + 16 * k + 16), j == 0, j == 4, 64) for k in range(8) for j in range(5)])
+        act(v("Hs", p=p112), c("P3", 0, 128, p=p112), 128)
+        mm([(c("P4", 0, 112), v("Hs", p=p112), v("cb", 0, S_(0, 112), p=p112), True, True, 112)])
+        cp(c("nS", 0, 16), c("P4", 0, 16), 16)
+        cp(c("nS", 16, 32), c("P4", 96, 112), 16)
+        cp(v("nF", t, S_(16, 96)), c("P4", 16, 96), 80)
+        exchange([(c("nS", 0, 16), v("nR", t, S_(16, 32)))], [(c("nS", 16, 32), v("nR", t, S_(0, 16)))], 2.2)
+        tt(v("nF", t, S_(0, 16)), c("nS", 0, 16), v("nR", t, S_(0, 16)), AL.add, 32)
+        tt(v("nF", t, S_(96, 112)), c("nS", 16, 32), v("nR", t, S_(16, 32)), AL.add, 32)
+        volumes(4, 5)
+        tt(c("sm", 16, 24), c("sm", 16, 24), vt(32, 40), AL.add, 16)
+        ts(v("z16", t), c("sm", 16, 24), -1.0, AL.add, 8, 0.0, AL.max)
+        tt(c("sm", 0, 16), th(8, 24), th(24, 40), AL.add, 32)
+        tt(c("sm", 24, 32), c("sm", 0, 8), c("sm", 8, 16), AL.add, 16)
+        ts(vt(40, 48), c("sm", 24, 32), 0.0625, AL.mult, 8)
+        yield
+        EQ = "EQ%d" % (t % 2)
+        mm([(c("P3", 8 * j - 8, 8 * j), Gj(j), v("aB"), True, True, 64) for j in range(1, 5)])
+        cp(c("cc", 0, 32), c("P3", 0, 32), 32)
+        for k in range(8):
+            bank = "P%d" % (3 + k % 2)
+            mm([(v(bank), v("selP", k), v("G", t, S_(128, 640)), True, True, 512)])
+            for j in range(4):
+                ts(v(EQ, k, S_(128 * j, 128 * j + 128)), c(bank, 128 * j, 128 * j + 128),
+                   c("cc", 8 * j + k, 8 * j + k + 1), AL.is_equal, 128)
+        mm([(v("P3"), c("wpad", 112 - 16 * k, 240 - 16 * k), v(EQ, k), k == 0, k == 7, 512) for k in range(8)])
+        act(v("Wb"), v("P3"), 512)
+        mm([(c("P4", 0, 32), c("Dq", 15 - q, 143 - q), c("Wb", q, 512, 16), q == 0, q == 15, 64) for q in range(16)])
+        tt(c("cc", 8, 40), c("P4", 0, 32), c("thr", 0, 32), AL.is_lt, 32)
+        ms(c("cc", 0, 8), 1.0, 8)
+        tt(v("cc"), v("cc"), th(0, 40), AL.mult, 80)
+        tt(v("st1", S_(0, 40)), nO(0, 40), v("dump"), AL.subtract, 80)
+        tt(v("cc"), v("cc"), v("st1", S_(0, 40)), AL.mult, 80)
+        tt(v("cc"), v("cc"), v("dump"), AL.add, 80)
+        cp(v("off16", t), v("cc"), 40)
+        dma("sync", v("S"), v("Z0"), 5.0)
+        uw = c(Wt, UB, UB + W)
+        act(v("um"), ind(uw, v("oM16", t)), 640)
+        act(v("wZ"), ind(c("wall", 0, 256), v("z16", t)), 128)
+        mm([(c("P5", q, 512, 16), v("Rq", q), vt(0, 32), True, True, 64) for q in range(16)])
+        mm([(c("P6", q, 256, 16), v("Rq", q), vt(32, 48), True, True, 64) for q in range(16)])
+        tt(c("prod", 0, 512), v("P5"), c("um", 0, 512), AL.mult, 512)
+        tt(c("prod", 512, 640), c("P6", 0, 128), c("um", 512, 640), AL.mult, 128)
+        mm([(c("P7", 384, 512), If, c("prod", 128 * j, 128 * j + 128), j == 0, j == 4, 512) for j in range(5)])
+        tt(v("Mm"), c("P7", 384, 512), v("wZ"), AL.mult, 128)
+        tt(v("Dd"), c("um", 512, 640), c("um", 0, 128), AL.subtract, 256)
+        tt(v("De"), c("P6", 128, 256), v("Dd"), AL.mult, 128)
+        tt(c("est", 0, 128), v("Mm"), v("De"), AL.subtract, 256)
+        ts(c("P7", 256, 384), v("Dd"), 0.125, AL.mult, 128)
+        for j in range(1, 5):
+            tt(c("est", 128 * j, 128 * j + 128), c("P7", 256, 384), c("est", 128 * j - 128, 128 * j), AL.add, 128)
+        for k in range(8):
+            x = ind(c(Wt, 0, UB + W), v("b16a", t, S_(80 * k, 80 * k + 80)))
+            for h in range(2):
+                xh = ind(c(Wt, 0, UB + W), v("b16a", t, S_(80 * k + 40 * h, 80 * k + 40 * h + 40)))
+                (cp if k in HELP[t] else lambda o, x, n: act(o, x, n))(v("Ug", k % 4, S_(640 * h, 640 * h + 640)), xh, 640)
+            n = 40 * LV
+            for a in range(0, 640, n):
+                o = a + 640 * (k % 2)
+                scan(c("Omin", o, o + n), v("Ug", k % 4, S_(2 * a, 2 * a + 2 * n, 2)), v("Ug", k % 4, S_(2 * a + 1, 2 * a + 2 * n, 2)),
+                     1e29, AL.min, AL.min, n)
+                scan(v("Omax", S_(o + n - 1, o - 1 if o else None, -1)),
+                     v("Ug", k % 4, S_(2 * a + 2 * n - 2, 2 * a - 1 if a else None, -2)),
+                     v("Ug", k % 4, S_(2 * a + 2 * n - 1, 2 * a, -2)), 0.0, AL.max, AL.max, n)
+            if k % 2:
+                tt(c("P7", 16 * k - 16, 16 * k + 16), c("Omin", 39, 1280, 40), unsc, AL.mult, 64)
+                tt(c("P7", 112 + 16 * k, 144 + 16 * k), c("Omax", 0, 1280, 40), unsc, AL.mult, 64)
+        sw = v("S")
+        for j in range(5):
+            ej = c("ec", 128 * j, 128 * j + 128)
+            tt(v("c1"), c("P7", 0, 128), c("est", 128 * j, 128 * j + 128), AL.max, 128)
+            tt(ej, c("P7", 128, 256), v("c1"), AL.min, 128)
+        mid = S_(112, 128)
+        mm([(c("P5", 0, 128), c("ec", 128, 256), If, True, True, 512)])
+        for j in range(1, 5):
+            zh, zl = "Zh%d" % (j % 2), "Zl%d" % (j % 2)
+            act(v(zh, S_(None), mid), c("P5", 0, 128), 128)
+            tt(v(zl, S_(None), mid), c("P5", 0, 128), v(zh, S_(None), mid), AL.subtract, 128)
+            turn = mm([(c("P5", 0, 128), c("ec", 128 * j + 128, 128 * j + 256), If, True, True, 512)]) if j < 4 else None
+            mm([(c("P6", 0, 128), v(z, k, S_(112 - 16 * k, 240 - 16 * k)), v(EQ, k, S_(128 * j - 128, 128 * j)),
+                 k == 0 and z == zh, k == 7 and z == zl, 128) for z in (zh, zl) for k in range(8)], turn)
+            act(v("Ss", j - 1), c("P6", 0, 128), 128)
+        for j in range(5):
+            off = v("off16", t, S_(8 * j, 8 * j + 8))
+            if j == 0:
+                cp(ind(sw, off), c("ec", 0, 128), 128)
+            else:
+                tt(v("tg", j - 1), ind(sw, off), v("Ss", j - 1), AL.add, 128)
+                cp(ind(sw, off), v("tg", j - 1), 128)
+        Rb = "Rb%d" % t
+        if last:
+            exchange([(c("S", V, 1664), c(Rb, 128, 256))], [(c("S", 1664, W), c(Rb, 0, 128))], 2.6)
+        else:
+            exchange([(c("S", V, 1664), c(Rb, 128, 256)), (c("S", 0, 128), c(Rb, 384, 512))],
+                     [(c("S", 1664, W), c(Rb, 0, 128)), (c("S", 1408, V), c(Rb, 256, 384))], 3.0)
+        nf = lambda a, b: v("nF", t, S_(a, b))
+        mm([(c("P5", 0, 96), shm, nf(8, 104), True, True, 96), (c("P5", 96, 104), shm, nf(0, 8), True, True, 64),
+            (c("P5", 104, 112), shm, nf(104, 112), True, True, 64)])
+        end = 96 if last else 112
+        head = W + 16 * end - 128
+        ts(c("nOff", 0, 96), c("P5", 0, 96), 1.0, AL.max, 96, -1.0, AL.add)
+        if not last:
+            ts(c("nOff", 96, 104), c("P5", 96, 104), 1.0, AL.max, 8, 255.0, AL.add)
+            ts(c("nOff", 104, 112), c("P5", 104, 112), 1.0, AL.max, 8, 511.0, AL.add)
+        ts(c("st1", 0, 8), c("P5", 0, 8), 0.5, AL.is_gt, 8, float(head), AL.mult)
+        ts(c("st1", 8, end), c("P5", 8, end), 0.5, AL.is_gt, 104, float(W - 128), AL.mult)
+        tt(c("st1", 0, end), c("st1", 0, end), c("cid", 0, end), AL.add, 224)
+        cp(c("sel", 0, end), c("st1", 0, end), 112)
+        nxt_w = "W%d" % ((t + 1) % 2)
+
+        def weigh(a, b, at):
+            tt(c(Wt, UB + at, UB + at + 16 * (b - a)), ind(v("wall"), c("nOff", a, b)), c("S", 16 * a, 16 * b), AL.mult, 16 * (b - a))
+
+        def pick(a, b, top):
+            act(c(nxt_w, UB + 16 * a, UB + 16 * b), ind(c(Wt, UB, UB + top), c("sel", a, b)), 16 * (b - a))
+            if last:
+                dma("sync", v("y", S_(16 * a, 16 * b)), c(nxt_w, UB + 16 * a, UB + 16 * b), 2.0 + (b - a) * 0.03)
+            else:
+                scaled(nxt_w, 16 * a, 16 * b)
+        weigh(8, 48, W)
+        pick(8, 48, W + 640)
+        weigh(48, 88, W + 640)
+        pick(48, 88, W + 1280)
+        tt(c("S", 0, 128), c("S", 0, 128), c(Rb, 0, 128), AL.add, 256)
+        tt(c("S", 1408, 16 * end), c("S", 1408, 16 * end), c(Rb, 128, 16 * end - 1280), AL.add, 32 * end - 2816)
+        weigh(88, end, W + 1280)
+        weigh(0, 8, head)
+        pick(88, end, head)
+        pick(0, 8, head + 128)
+        yield
+
+    parts = [one_round(t) for t in range(RO)]
+    for k, t in enumerate((0, 0, 1, 0, 1, 2, 1, 2, 2)):
+        bias[0] = BIAS[k]
+        next(parts[t])
+
+    n = len(ops)
+    succ = [[] for _ in range(n)]
+    for i, o in enumerate(ops):
+        for d in o["deps"]:
+            succ[d].append(i)
+    prio = [0.0] * n
+    for i in range(n - 1, -1, -1):
+        prio[i] = ops[i]["d"] + max([prio[s] + LAT_X for s in succ[i]] + [0.0])
+    prio = [x + o["b"] for x, o in zip(prio, ops)]
+    left = [len(o["deps"]) for o in ops]
+    ready = [i for i in range(n) if left[i] == 0]
+    rt = [0.0] * n
+    fin = [0.0] * n
+    free, busy, order = {}, {}, []
+    while ready:
+        st = {i: max(rt[i], free.get(ops[i]["e"], 0.0)) for i in ready}
+        i0 = min(ready, key=lambda i: (st[i], -prio[i]))
+        e = ops[i0]["e"]
+        i = max([k for k in ready if ops[k]["e"] == e and st[k] <= st[i0] + min(WINDOW, ops[i0]["d"])], key=lambda k: prio[k])
+        ready.remove(i)
+        o = ops[i]
+        fin[i] = st[i] + o["d"]
+        hold = o["d"] if o["k"] == "c" else (0.0 if e == "ext" else (0.1 if o["k"] == "dma" else 0.5))
+        free[e] = st[i] + hold
+        busy[e] = busy.get(e, 0.0) + hold
+        order.append(i)
+        for s in succ[i]:
+            rt[s] = max(rt[s], fin[i] + (LAT_S if ops[s]["e"] == e else LAT_X))
+            left[s] -= 1
+            if left[s] == 0:
+                ready.append(s)
+    STATS.update({"span": max(fin), "busy": busy, "n": n, "fin": fin, "ops": ops, "order": order})
+
+    queue = {"pool": g, "vector": g.vector, "scalar": g.scalar, "tensor": g.tensor, "sync": g.sync}
+    token, count, seen, n_d = {}, {}, {}, 0
+    for i in order:
+        o = ops[i]
+        e = o["e"]
+        if e == "ext":
+            token[i] = o["k"]
+            continue
+        need = {}
+        for d in o["deps"]:
+            s, val = token[d]
+            need[s] = max(need.get(s, 0), val)
+        for s in sorted(need):
+            if seen.get((e, s), 0) < need[s]:
+                queue[e].wait_ge(T.sem[s], need[s])
+                seen[(e, s)] = need[s]
+        ins = o["f"](queue[e])
+        if o["k"] == "c":
+            count[e] = count.get(e, 0) + 1
+            token[i] = ("c_" + e, count[e])
+            ins.then_inc(T.sem["c_" + e], 1)
+        elif o["k"] == "dma":
+            token[i] = ("d%d" % n_d, 16)
+            ins.then_inc(T.sem["d%d" % n_d], 16)
+            n_d += 1
+        else:
+            token[i] = o["k"]
+    top = {}
+    for s, val in token.values():
+        top[s] = max(top.get(s, 0), val)
+    for s in sorted(top):
+        if seen.get(("pool", s), 0) < top[s]:
+            g.wait_ge(T.sem[s], top[s])

@@ -10,7 +10,8 @@ SPLIT = (64, 0, 0)
 LV = 2
 UB = (LV - 1) * W
 HELP = ((), (), ())
-BIAS = (0, 0, 10, 5, 0, 0, 0, 20, 5)
+BIAS = (0, 0, 20, 0, 0, 0, 0, 0, -10)
+TIE = (1.0, 23)
 STATS = {}
 
 SCRATCH = {}
@@ -86,10 +87,10 @@ for _k in range(8):
 SEMAPHORES = ["c_vector", "c_scalar", "c_tensor", "c_pool"] + ["d%d" % k for k in range(20)] + \
              ["ls%d" % k for k in range(9)] + ["ar%d" % k for k in range(9)]
 
-CY = 0.83e-3 * 1.2
-PCY = 0.42e-3 * 1.2
-GA, SCA = 1.56, 3.8
-LAT_X, LAT_S, WINDOW = 0.12, 0.05, 0.1
+CY = 0.83e-3 * 1.3
+PCY = 0.42e-3 * 1.3
+GA, SCA, OV = 1.56, 4.2, 0.01
+LAT_X, LAT_S, WINDOW = 0.35, 0.17, 0.1
 
 
 def rank_program(g, core, T, topo):
@@ -168,7 +169,7 @@ def rank_program(g, core, T, topo):
             return 0.05 + SCA * n * CY
         if x is not None and "x" in x:
             return 0.05 + GA * n * CY
-        return 0.03 + max(64, n) * CY
+        return OV + max(64, n) * CY
 
     def cp(o, x, n):
         op("vector", vd(n, x, o), lambda q: q.tensor_copy(o["ap"], x["ap"]), [x], [o])
@@ -617,7 +618,7 @@ def rank_program(g, core, T, topo):
     prio = [0.0] * n
     for i in range(n - 1, -1, -1):
         prio[i] = ops[i]["d"] + max([prio[s] + LAT_X for s in succ[i]] + [0.0])
-    prio = [x + o["b"] for x, o in zip(prio, ops)]
+    prio = [x + o["b"] + TIE[0] * ((k * TIE[1]) % 101) / 101.0 for k, (x, o) in enumerate(zip(prio, ops))]
     left = [len(o["deps"]) for o in ops]
     ready = [i for i in range(n) if left[i] == 0]
     rt = [0.0] * n

@@ -6,12 +6,12 @@ AL = AluOpType
 AF = ActivationFunctionType
 V, W, RO, STEP = 1536, 1792, 3, 1344
 F, B, I, U16 = "float32", "bfloat16", "int32", "uint16"
-SPLIT = (64, 0, 0)
+SPLIT = (48, 32, 32)
 LV = 2
 UB = (LV - 1) * W
-HELP = ((), (), ())
-BIAS = (0, 0, 20, 0, 0, 0, 0, 0, -10)
-TIE = (1.0, 23)
+HELP = ((0,), (0,), (0,))
+BIAS = (0, 0, -20, 0, 5, 40, -5, 5, -10)
+TIE = (0.0, 5)
 STATS = {}
 
 SCRATCH = {}
@@ -52,7 +52,9 @@ _sb("xr1 ring volN", [112], B)
 _sb("xtab", [3, 112], B)
 _sb("cid qu qa qq hh st1", [112], F)
 _sb("lane biasL dump thr", [40], F)
-_sb("smallR junk", [96], B)
+_sb("smallR", [96], B)
+_sb("junk", [8, 96], B)
+_sb("c5", [5, 128], F)
 _sb("Cc", [96], F)
 _sb("Pw", [104], F)
 _sb("acc", [8], F)
@@ -87,9 +89,9 @@ for _k in range(8):
 SEMAPHORES = ["c_vector", "c_scalar", "c_tensor", "c_pool"] + ["d%d" % k for k in range(20)] + \
              ["ls%d" % k for k in range(9)] + ["ar%d" % k for k in range(9)]
 
-CY = 0.83e-3 * 1.3
-PCY = 0.42e-3 * 1.3
-GA, SCA, OV = 1.56, 4.2, 0.01
+CY = 0.83e-3 * 1.2
+PCY = 0.42e-3 * 1.2
+GA, SCA, OV = 1.56, 3.0, 0.0
 LAT_X, LAT_S, WINDOW = 0.35, 0.17, 0.1
 
 
@@ -112,7 +114,7 @@ def rank_program(g, core, T, topo):
             used = used + e
         return out
 
-    ops, log, bias = [], {}, [0.0]
+    ops, log, bias, banks = [], {}, [0.0], {}
     S_ = slice
 
     def v(name, *idx, p=None):
@@ -123,14 +125,15 @@ def rank_program(g, core, T, topo):
         idx = tuple(idx) + (S_(None),) * (len(free) - len(idx))
         lo = hi = 0
         stride = 1
+        step = 1
+        if isinstance(idx[-1], slice) and not any(isinstance(i, slice) for i in idx[:-1]):
+            step = abs(idx[-1].step or 1)
         for d, i in zip(reversed(free), reversed(idx)):
             r = range(d)[i] if isinstance(i, slice) else [i]
             lo += min(r[0], r[-1]) * stride
             hi += max(r[0], r[-1]) * stride
             stride *= d
-        if where == "psum":
-            lo, hi = 0, 511
-        return {"ap": T[name][(S_(None) if p is None else p,) + idx], "r": [(name, lo, hi + 1)]}
+        return {"ap": T[name][(S_(None) if p is None else p,) + idx], "r": [(name, lo, hi + 1, step)]}
 
     def c(name, a, b, s=1, p=None):
         return v(name, S_(a, b, s), p=p)
@@ -144,18 +147,24 @@ def rank_program(g, core, T, topo):
         acc = []
         for x in reads:
             if isinstance(x, dict):
-                acc += [(r, r[0][0] == "P" and r[0][1:].isdigit()) for r in x["r"]] + [(r, False) for r in x.get("x", [])]
+                acc += [(r, False) for r in x["r"]] + [(r, False) for r in x.get("x", [])]
         for x in writes:
             acc += [(r, True) for r in x["r"]] + [(r, False) for r in x.get("x", [])]
-        for (name, lo, hi), wr in acc:
-            for (l2, h2, o, w2) in log.get(name, []):
-                if o != me and l2 < hi and lo < h2 and (wr or w2):
+        for name in sorted(set(r[0] for r, _ in acc if r[0] in SCRATCH and SCRATCH[r[0]][0] == "psum")):
+            turn = banks.setdefault(name, [eng, [], []])
+            if turn[0] != eng:
+                turn[:] = [eng, [], turn[1]]
+            deps.update(turn[2])
+            turn[1].append(me)
+        for (name, lo, hi, sp), wr in acc:
+            for (l2, h2, o, w2, s2) in log.get(name, []):
+                if o != me and l2 < hi and lo < h2 and (wr or w2) and not (sp == s2 and (lo - l2) % sp):
                     deps.add(o)
-        for (name, lo, hi), wr in acc:
+        for (name, lo, hi, sp), wr in acc:
             lst = log.setdefault(name, [])
             if wr:
-                lst[:] = [e for e in lst if not (lo <= e[0] and e[1] <= hi)]
-            lst.append((lo, hi, me, wr))
+                lst[:] = [e for e in lst if not (lo <= e[0] and e[1] <= hi and (sp == 1 or (sp == e[4] and (lo - e[0]) % sp == 0)))]
+            lst.append((lo, hi, me, wr, sp))
         if extra is not None:
             deps.add(extra)
         ops.append({"e": eng, "d": dur, "f": fn, "deps": deps, "k": kind, "b": bias[0], "w": [x["r"][0][0] for x in writes if x["r"]]})
@@ -245,7 +254,7 @@ def rank_program(g, core, T, topo):
     p32 = S_(0, 32)
     bias[0] = 1000.0
     dma("sync", c("VD", 0, V, p=S_(0, 8)), v("vol", S_(None)), 2.2)
-    dma("scalar", {"ap": c("VD", 0, V, p=S_(8, 32))["ap"], "r": [("VDx", 0, 1)]}, v("dv", S_(None)), 2.4)
+    dma("scalar", {"ap": c("VD", 0, V, p=S_(8, 32))["ap"], "r": [("VDx", 0, 1, 1)]}, v("dv", S_(None)), 2.4)
     bias[0] = 500.0
     dma("sync", v("ntb"), v("nt", S_(None)), 5.5)
     bias[0] = 0.0
@@ -333,7 +342,7 @@ def rank_program(g, core, T, topo):
 
     for a in (0, 768):
         x = c("VD", a, a + 768, p=p32)
-        cp(c("VDb", a, a + 768, p=p32), {"ap": x["ap"], "r": x["r"] + [("VDx", 0, 1)]}, 768)
+        cp(c("VDb", a, a + 768, p=p32), {"ap": x["ap"], "r": x["r"] + [("VDx", 0, 1, 1)]}, 768)
     for t in range(RO):
         bank = "P%d" % (3 + t)
         mm([(c(bank, 0, 96), v("Cq", t, S_(15 - q, 143 - q), p=p32), c("VDb", q, V, 16, p=p32), q == 0, q == 15, 96)
@@ -357,11 +366,14 @@ def rank_program(g, core, T, topo):
         ts(o, ind(v("ntb"), off), 0.0625, AL.mult, 128, -0.46875, AL.add)
 
     def publish(j):
-        ts(v("cf", 4, S_(0, 128, 16)), c("r8", 8, 16), 32768.0, AL.add, 8)
+        ts(v("cf", 4, S_(0, 128, 16)), c("r8", 8, 16) if j else c("P2", 256, 264), 32768.0, AL.add, 8)
+        if j == 0:
+            cp(c("r8", 8, 16), c("P2", 256, 264), 8)
         scan(v("Bc", j), rmask, d1, 0.0, AL.mult, AL.add, 128)
         tt(v("mk"), qmask, v("Bc", j), AL.mult, 128)
         mm([(c("P1", 128, 136), v("mk"), v("cm"), True, True, 256)])
-        ts(c("o16", 8 * j, 8 * j + 8), c("P1", 128, 136), kc, AL.subtract, 8)
+        if j < 4:
+            ts(c("o16", 8 * j, 8 * j + 8), c("P1", 128, 136), kc, AL.subtract, 8)
 
     def lane_major(t, j, x):
         for s in range(LV):
@@ -393,12 +405,11 @@ def rank_program(g, core, T, topo):
         scan(v("Cc"), c("P2", 0, 96), c("Z0", 0, 96), 0.0, AL.add, AL.add, 96)
         tt(c("Pw", 0, 96), v("Cc"), c("P2", 128, 224), AL.subtract, 96)
         for k in range(8):
-            act(v("junk"), v("Cc"), 96, AF.Sign, bias=c("biasL", k, k + 1), accum=c("acc", k, k + 1))
+            act(v("junk", k), v("Cc"), 96, AF.Sign, bias=c("biasL", k, k + 1), accum=c("acc", k, k + 1))
         ts(v("x16"), v("acc"), -0.5, AL.mult, 8, 48.0, AL.add)
         tt(v("cmpb"), ind(v("Pw"), v("x16")), lrow, AL.is_le, 128)
         act(v("XE"), ind(v("xtab", t), v("x16")), 128)
         mm([(c("P2", 256, 264), v("cmpb"), bo8, True, False, 64), (c("P2", 256, 264), v("XE"), bo8, False, True, 64)])
-        cp(c("r8", 8, 16), c("P2", 256, 264), 8)
         publish(0)
         ts(v("mm"), v("lane"), c("Cc", 95, 96), AL.is_lt, 40)
         for h in range(4):
@@ -463,14 +474,15 @@ def rank_program(g, core, T, topo):
         tt(c("sm", 16, 24), c("sm", 0, 8), c("sm", 8, 16), AL.add, 16)
         ts(c("sm", 24, 32), c("sm", 16, 24), 43.5, AL.is_lt, 8)
         one_hot(0, 4)
-        cp(nO(32, 40), c("o16", 32, 40), 8)
+        tt(c("sm", 24, 32), c("sm", 24, 32), c("mm", 32, 40), AL.mult, 16)
+        ts(nO(32, 40), c("P1", 128, 136), kc, AL.subtract, 8)
+        tt(c("ne", 32, 40), nO(32, 40), nO(24, 32), AL.not_equal, 16)
+        tt(th(32, 40), c("ne", 32, 40), c("sm", 24, 32), AL.mult, 16)
+        one_hot(4, 5)
         tt(c("sm", 32, 40), nO(32, 40), nO(24, 32), AL.subtract, 16)
         tt(c("sm", 32, 40), c("sm", 32, 40), c("sm", 24, 32), AL.mult, 16)
-        tt(nO(32, 40), nO(24, 32), c("sm", 32, 40), AL.add, 16)
-        ts(c("ne", 32, 40), c("sm", 32, 40), 0.0, AL.not_equal, 8)
-        tt(th(32, 40), c("ne", 32, 40), c("mm", 32, 40), AL.mult, 16)
-        one_hot(4, 5)
-        cp(v("oM16", t, S_(32, 40)), nO(32, 40), 8)
+        tt(c("sm", 32, 40), nO(24, 32), c("sm", 32, 40), AL.add, 16)
+        cp(v("oM16", t, S_(32, 40)), c("sm", 32, 40), 8)
         tile_names(v("b16", 0), v("oM16", t, S_(32, 40)))
         lane_major(t, 4, 0)
         mm([(c("P3", 16 * ((k - 1) % 8), 16 * ((k - 1) % 8) + 16, p=p112), v("OH", 5 * k + j),
@@ -544,18 +556,19 @@ def rank_program(g, core, T, topo):
         sw = v("S")
         for j in range(5):
             ej = c("ec", 128 * j, 128 * j + 128)
-            tt(v("c1"), c("P7", 0, 128), c("est", 128 * j, 128 * j + 128), AL.max, 128)
-            tt(ej, c("P7", 128, 256), v("c1"), AL.min, 128)
+            tt(v("c5", j), c("P7", 0, 128), c("est", 128 * j, 128 * j + 128), AL.max, 128)
+            tt(ej, c("P7", 128, 256), v("c5", j), AL.min, 128)
         mid = S_(112, 128)
-        mm([(c("P5", 0, 128), c("ec", 128, 256), If, True, True, 512)])
+        for j in range(1, 5):
+            mm([(c("P5", 128 * j - 128, 128 * j), c("ec", 128 * j, 128 * j + 128), If, True, True, 512)])
         for j in range(1, 5):
             zh, zl = "Zh%d" % (j % 2), "Zl%d" % (j % 2)
-            act(v(zh, S_(None), mid), c("P5", 0, 128), 128)
-            tt(v(zl, S_(None), mid), c("P5", 0, 128), v(zh, S_(None), mid), AL.subtract, 128)
-            turn = mm([(c("P5", 0, 128), c("ec", 128 * j + 128, 128 * j + 256), If, True, True, 512)]) if j < 4 else None
-            mm([(c("P6", 0, 128), v(z, k, S_(112 - 16 * k, 240 - 16 * k)), v(EQ, k, S_(128 * j - 128, 128 * j)),
-                 k == 0 and z == zh, k == 7 and z == zl, 128) for z in (zh, zl) for k in range(8)], turn)
-            act(v("Ss", j - 1), c("P6", 0, 128), 128)
+            turned, bank = c("P5", 128 * j - 128, 128 * j), "P%d" % (7 - j % 2)
+            act(v(zh, S_(None), mid), turned, 128)
+            tt(v(zl, S_(None), mid), turned, v(zh, S_(None), mid), AL.subtract, 128)
+            mm([(c(bank, 0, 128), v(z, k, S_(112 - 16 * k, 240 - 16 * k)), v(EQ, k, S_(128 * j - 128, 128 * j)),
+                 k == 0 and z == zh, k == 7 and z == zl, 128) for z in (zh, zl) for k in range(8)])
+            act(v("Ss", j - 1), c(bank, 0, 128), 128)
         for j in range(5):
             off = v("off16", t, S_(8 * j, 8 * j + 8))
             if j == 0:

@@ -1,17 +1,30 @@
 import math
+import numpy as np
 from concourse.bass import DstId, RemoteDMATransfer
-from concourse.mybir import AluOpType, ActivationFunctionType
+from concourse.mybir import AluOpType, ActivationFunctionType, AxisListType
 
 AL = AluOpType
 AF = ActivationFunctionType
 V, W, RO, STEP = 1536, 1792, 3, 1344
 F, B, I, U16 = "float32", "bfloat16", "int32", "uint16"
-SPLIT = (48, 32, 32)
-LV = 2
-UB = (LV - 1) * W
-HELP = ((0,), (0,), (0,))
-BIAS = (0, 0, -20, 0, 5, 40, -5, 5, -10)
-TIE = (0.0, 5)
+BIG = 1.5 * 2.0 ** 35
+UB = W + 8
+WT = 264
+CFG = {
+    "split": ((0, 32, 64, 96, 128),) * 3,
+    "late": (True, False, False),
+    "turns": 8,
+    "look": 0.5,
+    "lend": (100.0, 100.0, 30.0),
+    "lendv": (0.0, 50.0, 50.0),
+    "acts": 5,
+    "bias": (0, 0, 0, 0, 0, 0, 0, 0, 0),
+    "lat": (0.35, 0.17, 0.1),
+    "same": True,
+    "piece": 600,
+    "own": 1.0,
+    "vbank": ("P0", "P1", "P0"),
+}
 STATS = {}
 
 SCRATCH = {}
@@ -23,76 +36,87 @@ def _sb(names, shape, dtype):
 
 
 _sb("VD ntb", [W], I)
-_sb("VDb", [V], B)
-_sb("At volE", [W], B)
-_sb("Gt", [W + 16], B)
-_sb("W0 W1", [UB + 2 * W], F)
-_sb("wall", [768], F)
-_sb("S Z0", [1920], F)
+_sb("At", [W], B)
+_sb("Gt volE", [W + 16], B)
+_sb("Wf", [UB + W], F)
+_sb("wall", [3 * WT], F)
+_sb("S", [1920], F)
+_sb("Z0", [256], F)
 _sb("Rb0 Rb1 Rb2", [512], F)
 _sb("dvO", [112, 3], F)
 _sb("Ug", [4, 1280], F)
+_sb("Ul", [4, 512], F)
+_sb("lev", [512], B)
+_sb("un2", [32], F)
+_sb("b16a", [2, 640], U16)
 _sb("Omin Omax", [1280], F)
-_sb("Zh0 Zh1 Zl0 Zl1", [8, 240], B)
+_sb("Zp", [4, 8, 240], B)
+_sb("OL", [5, 8, 240], B)
 _sb("Cq", [3, 143], B)
 _sb("pid", [4], I)
-_sb("r8", [16], I)
 _sb("col", [16], F)
 _sb("rows", [3, 128], F)
-_sb("cf", [5, 128], F)
-_sb("cb", [5, 128], B)
+_sb("cf", [2, 128], F)
+_sb("cb", [8, 128], B)
 _sb("M16", [16], F)
 _sb("cm aBf", [8], F)
-_sb("aB", [8], B)
+_sb("aB cW", [8], B)
 _sb("Rq", [16, 128], B)
-_sb("Dq", [144], B)
+_sb("Dq Dg", [144], B)
 _sb("wpad", [240], B)
 _sb("selP", [8, 128], B)
-_sb("xr1 ring volN", [112], B)
+_sb("xr1 ring volN nA", [112], B)
+_sb("x16r qtab", [96], B)
 _sb("xtab", [3, 112], B)
-_sb("cid qu qa qq hh st1", [112], F)
+_sb("qu qa qq hh thr1 ta", [112], F)
 _sb("lane biasL dump thr", [40], F)
 _sb("smallR", [96], B)
 _sb("junk", [8, 96], B)
-_sb("c5", [5, 128], F)
 _sb("Cc", [96], F)
 _sb("Pw", [104], F)
-_sb("acc", [8], F)
+_sb("acc mm bo1 bo2", [8], F)
+_sb("xr", [16], B)
 _sb("x16", [8], U16)
-_sb("cmpb XE ag Hs", [128], B)
-_sb("b16", [4, 128], U16)
-_sb("bf aT tk key sc mk wZ Mm Dd De c1", [128], F)
+_sb("cmpb XE ag", [128], B)
+_sb("b16", [2, 5, 128], U16)
+_sb("bn wZ Mm Dd De Rlo Rhi", [128], F)
+_sb("A2", [256], F)
+_sb("KS", [256], F)
+_sb("SC MK rmask hold", [128], F)
+_sb("ka kb", [8], F)
+_sb("Bc", [5, 128], F)
 _sb("Vg", [2048], B)
 _sb("eq", [4, 128], B)
-_sb("Bc", [5, 128], F)
-_sb("o16 nA16", [40], U16)
-_sb("volM OHlo", [640], B)
+_sb("o16 nA16 off16", [2, 40], U16)
+_sb("nW th pre thm", [2, 40], F)
+_sb("volM G", [2, 640], B)
 _sb("OH", [40, 112], B)
-_sb("ne hc cc sm t40 mm", [40], F)
-_sb("nS", [32], F)
-_sb("EQ0 EQ1", [8, 512], B)
+_sb("ne ff t40", [40], F)
+_sb("hc", [5, 16], F)
+_sb("hcm", [16], B)
+_sb("Zq", [40], B)
+_sb("es", [24], F)
+_sb("ev", [2, 8], B)
+_sb("nS thB", [32], F)
+_sb("EQ", [8, 512], B)
 _sb("Wb", [512], B)
-_sb("um prod est ec", [640], F)
+_sb("um", [256], F)
+_sb("prod est ec", [640], F)
 _sb("Ss tg", [4, 128], F)
-_sb("b16a", [RO, 640], U16)
-_sb("oM16 off16", [RO, 40], U16)
-_sb("z16", [RO, 8], U16)
-_sb("nO th", [RO, 40], F)
-_sb("vtO", [RO, 48], B)
-_sb("G", [RO, 640], B)
+_sb("z16", [2, 8], U16)
 _sb("nR", [RO, 32], F)
 _sb("nF", [RO, 112], B)
-_sb("nOff sel", [112], U16)
+_sb("nOff sel", [2, 112], U16)
 for _k in range(8):
     SCRATCH["P%d" % _k] = ("psum", [128, 512], F)
 
-SEMAPHORES = ["c_vector", "c_scalar", "c_tensor", "c_pool"] + ["d%d" % k for k in range(20)] + \
+SEMAPHORES = ["c_vector", "c_scalar", "c_tensor", "c_pool"] + ["d%d" % k for k in range(28)] + \
              ["ls%d" % k for k in range(9)] + ["ar%d" % k for k in range(9)]
 
-CY = 0.83e-3 * 1.2
-PCY = 0.42e-3 * 1.2
-GA, SCA, OV = 1.56, 3.0, 0.0
-LAT_X, LAT_S, WINDOW = 0.35, 0.17, 0.1
+CY = 0.83e-3 * 1.05
+PCY = 0.42e-3 * 1.05
+GA, SCA = 1.56, 3.5
+PLAN = {}
 
 
 def rank_program(g, core, T, topo):
@@ -116,24 +140,15 @@ def rank_program(g, core, T, topo):
 
     ops, log, bias, banks = [], {}, [0.0], {}
     S_ = slice
+    ALL = S_(None)
 
     def v(name, *idx, p=None):
+        ap = T[name][(ALL if p is None else p,) + idx]
         if name not in SCRATCH:
-            return {"ap": T[name][(S_(None) if p is None else p,) + idx], "r": []}
-        where, shape, _ = SCRATCH[name]
-        free = shape[1:]
-        idx = tuple(idx) + (S_(None),) * (len(free) - len(idx))
-        lo = hi = 0
-        stride = 1
-        step = 1
-        if isinstance(idx[-1], slice) and not any(isinstance(i, slice) for i in idx[:-1]):
-            step = abs(idx[-1].step or 1)
-        for d, i in zip(reversed(free), reversed(idx)):
-            r = range(d)[i] if isinstance(i, slice) else [i]
-            lo += min(r[0], r[-1]) * stride
-            hi += max(r[0], r[-1]) * stride
-            stride *= d
-        return {"ap": T[name][(S_(None) if p is None else p,) + idx], "r": [(name, lo, hi + 1, step)]}
+            return {"ap": ap, "r": []}
+        m = np.zeros(SCRATCH[name][1][1:], bool)
+        m[idx] = True
+        return {"ap": ap, "r": [(name, int.from_bytes(np.packbits(m.reshape(-1)).tobytes(), "big"))]}
 
     def c(name, a, b, s=1, p=None):
         return v(name, S_(a, b, s), p=p)
@@ -143,7 +158,7 @@ def rank_program(g, core, T, topo):
 
     def op(eng, dur, fn, reads, writes, kind="c", extra=None):
         me = len(ops)
-        deps = set()
+        deps, soft, order_only = set(), set(), set()
         acc = []
         for x in reads:
             if isinstance(x, dict):
@@ -156,18 +171,22 @@ def rank_program(g, core, T, topo):
                 turn[:] = [eng, [], turn[1]]
             deps.update(turn[2])
             turn[1].append(me)
-        for (name, lo, hi, sp), wr in acc:
-            for (l2, h2, o, w2, s2) in log.get(name, []):
-                if o != me and l2 < hi and lo < h2 and (wr or w2) and not (sp == s2 and (lo - l2) % sp):
-                    deps.add(o)
-        for (name, lo, hi, sp), wr in acc:
+        for (name, m), wr in acc:
+            for (m2, o, w2) in log.get(name, []):
+                if o != me and (m & m2) and (wr or w2):
+                    if eng == "tensor" and ops[o]["e"] == eng:
+                        order_only.add(o)
+                    else:
+                        (soft if wr and kind == "c" and ops[o]["k"] == "c" else deps).add(o)
+        for (name, m), wr in acc:
             lst = log.setdefault(name, [])
             if wr:
-                lst[:] = [e for e in lst if not (lo <= e[0] and e[1] <= hi and (sp == 1 or (sp == e[4] and (lo - e[0]) % sp == 0)))]
-            lst.append((lo, hi, me, wr, sp))
+                lst[:] = [(e[0] & ~m, e[1], e[2]) for e in lst if e[0] & ~m]
+            lst.append((m, me, wr))
         if extra is not None:
             deps.add(extra)
-        ops.append({"e": eng, "d": dur, "f": fn, "deps": deps, "k": kind, "b": bias[0], "w": [x["r"][0][0] for x in writes if x["r"]]})
+        ops.append({"e": eng, "d": dur, "alt": {eng: (dur, fn)}, "deps": deps, "war": soft - deps, "order": order_only, "k": kind,
+                    "b": bias[0], "w": [x["r"][0][0] for x in writes if x["r"]]})
         return me
 
     def a_(x):
@@ -178,7 +197,7 @@ def rank_program(g, core, T, topo):
             return 0.05 + SCA * n * CY
         if x is not None and "x" in x:
             return 0.05 + GA * n * CY
-        return OV + max(64, n) * CY
+        return max(64, n) * CY
 
     def cp(o, x, n):
         op("vector", vd(n, x, o), lambda q: q.tensor_copy(o["ap"], x["ap"]), [x], [o])
@@ -194,6 +213,9 @@ def rank_program(g, core, T, topo):
 
     def scan(o, d0, d1, init, f0, f1, n):
         op("vector", vd(n), lambda q: q.tensor_tensor_scan(o["ap"], d0["ap"], d1["ap"], init, f0, f1), [d0, d1], [o])
+
+    def red(o, x, n):
+        op("vector", vd(n), lambda q: q.tensor_reduce(o["ap"], x["ap"], AxisListType.X, AL.add), [x], [o])
 
     def ms(o, val, n):
         op("vector", vd(n), lambda q: q.memset(o["ap"], val), [], [o])
@@ -213,13 +235,34 @@ def rank_program(g, core, T, topo):
 
     first_exp = []
 
-    def mm(lst, after=None):
-        def f(q):
-            for (o, l, r, st, sp, _) in lst:
-                ins = q.matmul(o["ap"], l["ap"], r["ap"], st, sp)
-            return ins
-        return op("tensor", 0.06 + sum(x[5] for x in lst) * PCY, f, [x[1] for x in lst] + [x[2] for x in lst],
-                  [x[0] for x in lst], extra=after)
+    def either(o, x, n, scale=1.0, lend=0.0):
+        act(o, x, n, scale=scale)
+        ops[-1]["lend"] = lend
+        ops[-1]["alt"]["vector"] = (vd(n, x), lambda q: q.tensor_scalar(o["ap"], x["ap"], scale, None, AL.mult))
+
+    def mm(lst):
+        pieces, size = [[]], 0
+        for x in lst:
+            if pieces[-1] and (size + x[5] > CFG["piece"] or x[1].get("cut")):
+                pieces.append([])
+                size = 0
+            pieces[-1].append(x)
+            size += x[5]
+        for part in pieces:
+            def f(q, part=part):
+                for (o, l, r, st, sp, _) in part:
+                    ins = q.matmul(o["ap"], l["ap"], r["ap"], st, sp)
+                return ins
+            mark = [{"r": [(b + "g", 1)]} for b in sorted(set(x[0]["r"][0][0] for x in part))]
+            shut = part[0][3] and part[-1][4]
+            op("tensor", 0.03 + sum(x[5] for x in part) * PCY, f, [x[1] for x in part] + [x[2] for x in part] + (mark if shut else []),
+               [x[0] for x in part] + ([] if shut else mark))
+
+    def cut(x):
+        return dict(x, cut=True)
+
+    def grp(o, pairs):
+        return [(o, l, r, k == 0, k == len(pairs) - 1, n) for k, (l, r, n) in enumerate(pairs)]
 
     def iota(o, pat, base, cmul, n, flt=True):
         k = {"allow_small_or_imprecise_dtypes": True} if flt else {}
@@ -249,17 +292,19 @@ def rank_program(g, core, T, topo):
         come = len(share(prev)[core]) + len(share(nxt)[core])
         s = op("pool", us, lambda q: q.remote_dma_fused(trs, local_sem=T.sem["ls%d" % k]),
                [x[0] for x in to_prev + to_next], [], kind=("ls%d" % k, sent))
-        op("ext", 0.6, None, [], [x[1] for x in to_prev + to_next], kind=("ar%d" % k, come), extra=s)
+        op("ext", 0.3, None, [], [x[1] for x in to_prev + to_next], kind=("ar%d" % k, come), extra=s)
 
     p32 = S_(0, 32)
+    mid = S_(112, 128)
     bias[0] = 1000.0
-    dma("sync", c("VD", 0, V, p=S_(0, 8)), v("vol", S_(None)), 2.2)
-    dma("scalar", {"ap": c("VD", 0, V, p=S_(8, 32))["ap"], "r": [("VDx", 0, 1, 1)]}, v("dv", S_(None)), 2.4)
+    dma("sync", c("VD", 0, V, p=S_(0, 8)), v("vol", ALL), 2.2)
+    dma("scalar", {"ap": c("VD", 0, V, p=S_(8, 32))["ap"], "r": [("VDx", 1)]}, v("dv", ALL), 2.4)
     bias[0] = 500.0
-    dma("sync", v("ntb"), v("nt", S_(None)), 5.5)
+    dma("sync", v("ntb"), v("nt", ALL), 5.5)
+    bias[0] = 400.0
+    dma("scalar", c("Wf", 0, V), v("u", ALL), 8.0)
+    dma("scalar", c("wall", 8, WT), v("wt", ALL), 8.5)
     bias[0] = 0.0
-    dma("scalar", c("wall", 0, 256), v("wt", S_(None)), 5.0)
-    dma("scalar", c("W0", UB, UB + V), v("u", S_(None)), 9.0)
 
     ms(v("Cq", p=p32), 1.0, 215)
     asel(v("Cq", p=p32), v("Cq", p=p32), [[-16, 3], [-3, 143]], AL.is_equal, 0.0, -83, 16, 429)
@@ -271,37 +316,42 @@ def rank_program(g, core, T, topo):
     iota(v("lane"), [[0, 5], [16, 8]], 0, 0, 40)
     ts(c("pid", 1, 2), c("pid", 0, 1), 15, AL.bitwise_and, 1)
     ts(c("pid", 2, 3), c("pid", 0, 1), 4, AL.arith_shift_right, 1)
-    qc, gc, kc, shc, alc, wc, pc = [c("col", k, k + 1) for k in range(7)]
+    qc, gc, shc, alc, wc, pc = [c("col", k, k + 1) for k in (0, 1, 3, 4, 5, 6)]
     cp(qc, c("pid", 1, 2), 1)
     cp(gc, c("pid", 2, 3), 1)
     cp(pc, c("pid", 0, 1), 1)
-    ts(kc, qc, -2048.0, AL.mult, 1, 32768.0, AL.add)
     ts(shc, pc, 111.5, AL.is_gt, 1, -128.0, AL.mult)
     ts(shc, shc, pc, AL.add, 1, 16.0, AL.add)
     lrow, qrow, grow = v("rows", 0), v("rows", 1), v("rows", 2)
-    If, rmask, qmask, unsc, d1 = [v("cf", k) for k in range(5)]
-    unsc = v("cf", 3, S_(0, 32))
-    Ib, bo, up, negI, shm = [v("cb", k) for k in range(5)]
+    If, unsc = v("cf", 0), v("cf", 1)
+    Ib, bo, up, negI, shm, shmK, I16, kcr = [v("cb", k) for k in range(8)]
     bo8 = v("cb", 1, S_(0, 128, 16))
+    I8 = v("cb", 0, S_(0, 128, 16))
     ts(bo, grow, gc, AL.is_equal, 128)
-    ts(v("tk"), qrow, qc, AL.is_lt, 128)
-    tt(up, v("tk"), bo, AL.mult, 256)
+    ts(v("bn"), qrow, qc, AL.is_lt, 128)
+    tt(up, v("bn"), bo, AL.mult, 256)
     ts(v("lane"), v("lane"), qc, AL.add, 40)
     ts(v("biasL"), v("lane"), -1.0, AL.mult, 40, -0.5, AL.add)
     ts(If, lrow, pc, AL.is_equal, 128)
     ts(Ib, lrow, pc, AL.is_equal, 128)
+    ts(I16, lrow, pc, AL.is_equal, 128, 16.0, AL.mult)
     ts(negI, lrow, pc, AL.is_equal, 128, -16777216.0, AL.mult)
     ts(shm, lrow, shc, AL.is_equal, 128)
-    ts(rmask, qrow, 0.5, AL.is_gt, 128)
-    qmask = c("P0", 256, 384)
-    ts(qmask, qrow, qc, AL.is_equal, 128)
+    ts(shmK, lrow, shc, AL.is_equal, 128, 4096.0, AL.mult)
+    ts(kcr, qrow, -4096.0, AL.mult, 128, 65536.0, AL.add)
     ts(v("M16"), v("rows", 0, S_(0, 16)), qc, AL.is_equal, 16)
     ts(v("cm"), v("rows", 0, S_(0, 8)), gc, AL.is_equal, 8)
-    ms(d1, -2048.0, 128)
+    ms(v("cW"), -float(W), 8)
     ms(c("Pw", 96, 104), 1e6, 8)
-    ms(c("ne", 0, 8), 1.0, 8)
+    ms(v("A2"), 0.0, 256)
+    ms(v("hold"), 0.0, 128)
+    ts(v("rmask"), qrow, 0.5, AL.is_gt, 128)
+    qmask = c("P0", 384, 512)
+    ts(qmask, qrow, qc, AL.is_equal, 128)
     for q in range(16):
         act(v("Rq", q), bo, 128, scale=c("M16", q, q + 1))
+    ms(v("Dg"), 0.0, 72)
+    cp(c("Dg", 15, 143, 16), v("cm"), 8)
     ms(v("Dq"), 0.0, 72)
     ts(c("Dq", 15, 143), Ib, c("M16", 0, 1), AL.mult, 64)
     for t in range(RO):
@@ -317,7 +367,13 @@ def rank_program(g, core, T, topo):
     for q in range(16):
         act(c("Gt", q, W, 16), v("xr1"), 112, scale=c("M16", q, q + 1))
     ms(c("Gt", W, W + 16), 0.0, 16)
-    ts(v("cid"), v("rows", 0, S_(0, 112)), 16.0, AL.mult, 112, qc, AL.add)
+    ms(c("volE", W, W + 16), 0.0, 16)
+    ms(c("Wf", W, W + 8), 0.0, 8)
+    ms(c("wall", 0, 8), 1.0, 8)
+    ms(c("S", W, 1920), 0.0, 128)
+    ms(v("Z0"), 0.0, 256)
+    ts(v("x16r"), v("rows", 0, S_(0, 96)), 16.0, AL.mult, 96)
+    ts(v("qtab"), v("rows", 0, S_(0, 96)), 0.0, AL.mult, 96, qc, AL.add)
     ts(v("dump"), v("lane"), float(W), AL.add, 40)
     ln2 = math.log(2.0)
     ts(c("col", 8, 9), qc, 7 * ln2, AL.mult, 1, -52 * ln2, AL.add)
@@ -327,250 +383,339 @@ def rank_program(g, core, T, topo):
     act(v("thr"), v("t40"), 40, AF.Exp)
     ts(v("aB"), v("cm"), alc, AL.mult, 8)
     cp(v("aBf"), v("aB"), 8)
+    cp(c("hcm", 0, 8), v("cm"), 8)
+    cp(c("hcm", 8, 16), v("aB"), 8)
     for k in range(8):
         act(v("selP", k), lrow, 128, AF.Identity, bias=c("aBf", k, k + 1), scale=0.0)
     ms(v("wpad"), 0.0, 120)
     ts(c("wpad", 112, 128), v("M16"), 0.0, AL.mult, 16, wc, AL.add)
-    for s in range(LV):
-        ms(v("cf", 3, S_(s, 32, LV)), 256.0 ** s, 8)
-    ms(c("Z0", 0, 96), 0.0, 96)
-    for k in range(4):
-        iota(c("Z0", 96 + 456 * k, 552 + 456 * k), [[0, 456]], 0, 0, 456)
-    for n in ("Zh1", "Zl1", "Zh0", "Zl0"):
-        for k in range(4):
-            iota(v(n, S_(2 * k, 2 * k + 2)), [[0, 480]], 0, 0, 480)
+    for s in range(8):
+        ms(v("cf", 1, S_(s, 128, 8)), 256.0 ** s, 16)
+        ms(c("lev", 16 * s, 16 * s + 16), 256.0 ** -s, 16)
+    cp(c("lev", 128, 256), c("lev", 0, 128), 64)
+    cp(c("lev", 256, 512), c("lev", 0, 256), 128)
+    for s in range(2):
+        ms(c("un2", s, 32, 2), 256.0 ** s, 16)
+    bias[0] = -100.0
+    for name, n in (("OL", 5), ("Zp", 4)):
+        for k in range(n):
+            for h in range(8):
+                iota(v(name, k, h), [[0, 240]], 0, 0, 240)
+    bias[0] = 0.0
 
     for a in (0, 768):
         x = c("VD", a, a + 768, p=p32)
-        cp(c("VDb", a, a + 768, p=p32), {"ap": x["ap"], "r": x["r"] + [("VDx", 0, 1, 1)]}, 768)
+        cp(c("Vg", a, a + 768, p=p32), {"ap": x["ap"], "r": x["r"] + [("VDx", 1)]}, 768)
     for t in range(RO):
         bank = "P%d" % (3 + t)
-        mm([(c(bank, 0, 96), v("Cq", t, S_(15 - q, 143 - q), p=p32), c("VDb", q, V, 16, p=p32), q == 0, q == 15, 96)
-            for q in range(16)])
+        mm(grp(c(bank, 0, 96), [(v("Cq", t, S_(15 - q, 143 - q), p=p32), c("Vg", q, V, 16, p=p32), 96) for q in range(16)]))
         cp(v("dvO", S_(8, 104), t), c(bank, 0, 96), 96)
     exchange([(v("dvO", S_(8, 16)), v("dvO", S_(104, 112)))], [(v("dvO", S_(96, 104)), v("dvO", S_(0, 8)))], 4.0)
-    exchange([(c("W0", UB, UB + 128), c("W0", UB + 1664, UB + W))],
-             [(c("W0", UB + 1408, UB + V), c("W0", UB + V, UB + 1664))], 2.5)
-
-    def scaled(name, a, b):
-        for s in range(1, LV):
-            act(c(name, (s - 1) * W + a, (s - 1) * W + b), c(name, UB + a, UB + b), b - a, scale=256.0 ** -s)
-    for h in range(4):
-        scaled("W0", 448 * h, 448 * h + 448)
-    exchange([(c("wall", 0, 256), c("wall", 512, 768))], [(c("wall", 0, 256), c("wall", 256, 512))], 2.5)
+    exchange([(c("Wf", 0, 128), c("Wf", 1664, W))], [(c("Wf", 1408, V), c("Wf", V, 1664))], 2.5)
+    def scaled(a, b):
+        act(c("Wf", UB + a, UB + b), c("Wf", a, b), b - a, scale=1.0 / 256)
+    for a, b in ((0, 512), (512, 1024), (1024, V), (V, W)):
+        scaled(a, b)
+    exchange([(c("wall", 0, WT), c("wall", 2 * WT, 3 * WT))], [(c("wall", 0, WT), c("wall", WT, 2 * WT))], 2.5)
     for h in range(4):
         ts(c("VD", 448 * h, 448 * h + 448), c("ntb", 448 * h, 448 * h + 448), 15, AL.bitwise_and, 448)
-        ts(c("At", 448 * h, 448 * h + 448), c("VD", 448 * h, 448 * h + 448), 32768.0, AL.mult, 448)
+        act_src = c("VD", 448 * h, 448 * h + 448)
+        ts(c("At", 448 * h, 448 * h + 448), act_src, 65536.0, AL.mult, 448)
 
-    def tile_names(o, off):
-        ts(o, ind(v("ntb"), off), 0.0625, AL.mult, 128, -0.46875, AL.add)
+    inner, left, right = (16, 96), (0, 16), (96, 112)
 
-    def publish(j):
-        ts(v("cf", 4, S_(0, 128, 16)), c("r8", 8, 16) if j else c("P2", 256, 264), 32768.0, AL.add, 8)
-        if j == 0:
-            cp(c("r8", 8, 16), c("P2", 256, 264), 8)
-        scan(v("Bc", j), rmask, d1, 0.0, AL.mult, AL.add, 128)
-        tt(v("mk"), qmask, v("Bc", j), AL.mult, 128)
-        mm([(c("P1", 128, 136), v("mk"), v("cm"), True, True, 256)])
-        if j < 4:
-            ts(c("o16", 8 * j, 8 * j + 8), c("P1", 128, 136), kc, AL.subtract, 8)
+    def spread_volumes(a, b, bank, pieces, x=0):
+        mm([(c(bank, x + q, x + 16 * (b - a), 16), v("Rq", q), c("volN", a, b), True, True, 64) for q in range(16)])
+        for (x, at, n) in pieces:
+            act(c("volE", at, at + n), c(bank, x, x + n), n)
 
-    def lane_major(t, j, x):
-        for s in range(LV):
-            ts(v("b16a", t, S_(5 * s + j, 640, 5 * LV)), v("b16", x, S_(s, 128, LV)), float((s - 1) * W if s else UB), AL.add, 32)
-
-    def one_round(t):
+    def lanes(t):
         last = t == RO - 1
+        e = t % 2
         x0 = (STEP * t) % V // 16
-        Wt = "W%d" % (t % 2)
         if t == 0:
             def qv(a, b):
                 return v("dvO", S_(a, b), 0)
+            ts(v("smallR"), qv(8, 104), 7.5, AL.is_lt, 96)
         else:
-            ts(v("hh"), v("nF", t - 1), 3.0, AL.min, 112)
-            tt(v("qu"), v("qa"), v("hh"), AL.subtract, 224)
-
             def qv(a, b):
                 return c("qu", a, b)
-        ts(c("smallR", 0, 96 - x0), qv(8 + x0, 104), 7.5, AL.is_lt, 96 - x0)
-        if x0:
-            ts(c("smallR", 96 - x0, 96), qv(8, 8 + x0), 7.5, AL.is_lt, x0)
-        ts(c("volN", 0, 96), qv(8, 104), 1.0, AL.max, 96, 16.0, AL.min)
-        ts(c("volN", 96, 104), qv(0, 8), 1.0, AL.max, 8, 16.0, AL.min)
-        ts(c("volN", 104, 112), qv(104, 112), 1.0, AL.max, 8, 16.0, AL.min)
-        if not last:
-            ts(v("qq"), qv(0, 112), 1.0, AL.max, 112, 16.0, AL.min)
-            tt(v("qa"), v("qq"), v("dvO", S_(None), t + 1), AL.add, 224)
-        mm([(c("P2", 0, 96), bo, v("smallR"), True, True, 96), (c("P2", 128, 224), up, v("smallR"), True, True, 96)])
-        scan(v("Cc"), c("P2", 0, 96), c("Z0", 0, 96), 0.0, AL.add, AL.add, 96)
-        tt(c("Pw", 0, 96), v("Cc"), c("P2", 128, 224), AL.subtract, 96)
-        for k in range(8):
+            tt(c("smallR", 96 - x0, 104 - x0), v("nR", t - 1, S_(8, 16)), c("thB", 8, 16), AL.is_gt, 16)
+            tt(c("smallR", 88 - x0, 96 - x0), v("nR", t - 1, S_(16, 24)), c("thB", 16, 24), AL.is_gt, 16)
+        mm([(c("P0", 0, 96), bo, v("smallR"), True, True, 96), (c("P0", 128, 224), up, v("smallR"), True, True, 96)])
+        scan(v("Cc"), c("P0", 0, 96), c("Z0", 0, 96), 0.0, AL.add, AL.add, 96)
+        na = CFG["acts"]
+        for k in range(na):
             act(v("junk", k), v("Cc"), 96, AF.Sign, bias=c("biasL", k, k + 1), accum=c("acc", k, k + 1))
+        for k in range(na, 8):
+            ts(v("junk", k), v("Cc"), c("lane", k, k + 1), AL.is_gt, 96, 2.0, AL.mult)
+        for k in range(na, 8):
+            red(c("bo2", k, k + 1), v("junk", k), 96)
+        tt(c("Pw", 0, 96), v("Cc"), c("P0", 128, 224), AL.subtract, 96)
+        if na < 8:
+            ts(c("acc", na, 8), c("bo2", na, 8), -96.0, AL.add, 8)
         ts(v("x16"), v("acc"), -0.5, AL.mult, 8, 48.0, AL.add)
+        ts(c("xr", 0, 8), v("acc"), -0.5, AL.mult, 8, 48.0 + x0, AL.add)
+        ts(c("xr", 8, 16), v("acc"), 2.0 * x0 - 95.0, AL.is_lt, 8, -96.0, AL.mult)
         tt(v("cmpb"), ind(v("Pw"), v("x16")), lrow, AL.is_le, 128)
         act(v("XE"), ind(v("xtab", t), v("x16")), 128)
-        mm([(c("P2", 256, 264), v("cmpb"), bo8, True, False, 64), (c("P2", 256, 264), v("XE"), bo8, False, True, 64)])
-        publish(0)
-        ts(v("mm"), v("lane"), c("Cc", 95, 96), AL.is_lt, 40)
-        for h in range(4):
-            bank = "P%d" % (3 + h % 2)
-            mm([(c(bank, q, 448, 16), v("Rq", q), c("volN", 28 * h, 28 * h + 28), True, True, 64) for q in range(16)])
-            act(c("volE", 448 * h, 448 * h + 448), c(bank, 0, 448), 448)
-        yield
-        for j in range(1, 5):
-            off = c("o16", 8 * j - 8, 8 * j)
-            tile_names(v("b16", j - 1), off)
-            act(v("ag"), ind(v("At"), off), 128)
-            sp = SPLIT[t]
-            if sp:
-                cp(c("Vg", 0, 16 * sp), ind(v("volE"), v("b16", j - 1, S_(0, sp))), 16 * sp)
-            act(c("Vg", 16 * sp, 2048), ind(v("volE"), v("b16", j - 1, S_(sp, 128))), 2048 - 16 * sp)
-            ts(v("bf"), v("b16", j - 1), kc, AL.add, 128)
-            mm([(c("P0", 128, 256), v("bf"), If, True, True, 512), (c("P0", 0, 128), v("ag"), Ib, True, True, 128)])
-            for i in range(j):
-                tt(v("eq", i), c("P0", 128, 256), v("Bc", i), AL.is_equal, 128)
-            act(v("aT"), c("P0", 0, 128), 128)
-            mm([(c("P1", 0, 128), v("bf"), If, True, False, 512)] +
-               [(c("P1", 0, 128), negI, v("eq", i), False, i == j - 1, 128) for i in range(j)])
-            mm([(c("P2", k, 128, 16), c("Vg", k, 2048, 16), v("cb", 0, S_(0, 128, 16)), True, True, 64) for k in range(16)])
-            tt(v("tk"), c("P2", 0, 128), v("aT"), AL.mult, 128)
-            tt(v("key"), c("P1", 0, 128), v("tk"), AL.add, 128)
-            scan(v("sc"), rmask, v("key"), 0.0, AL.mult, AL.max, 128)
-            tt(c("r8", 0, 8), c("sc", 15, 128, 16), c("r8", 8, 16), AL.max, 8)
-            ts(c("r8", 8, 16), c("r8", 0, 8), 2047, AL.bitwise_and, 8)
-            publish(j)
-            lane_major(t, j - 1, j - 1)
-        nO = lambda a, b: v("nO", t, S_(a, b))
-        th = lambda a, b: v("th", t, S_(a, b))
-        vt = lambda a, b: v("vtO", t, S_(a, b))
-        Gj = lambda j: v("G", t, S_(128 * j, 128 * j + 128))
-        p112 = S_(0, 112)
+        mm(grp(c("P0", 224, 232), [(I16, c("xr", 0, 8), 64), (I16, c("xr", 8, 16), 64), (Ib, v("cW"), 64)] +
+               [(c("Dg", 15 - q, 143 - q), c("cmpb", q, 128, 16), 64) for q in range(16)]) +
+           grp(c("P0", 232, 240), [(v("cmpb"), bo8, 64), (v("XE"), bo8, 64)]))
+        ts(v("o16", e, S_(0, 8)), c("P0", 224, 232), float(W), AL.add, 8)
+        cp(v("nW", e, S_(0, 8)), c("P0", 224, 232), 8)
+        cp(c("hold", 0, 128, 16), c("P0", 232, 240), 8)
+        scan(v("Bc", 0), v("rmask"), v("hold"), 0.0, AL.mult, AL.add, 128)
+        ts(v("mm"), c("lane", 0, 8), c("Cc", 95, 96), AL.is_lt, 8)
+        if t:
+            for (a, b), x in ((left, 0), (right, 16)):
+                ts(c("hh", a, b), v("nF", t - 1, S_(a, b)), 3.0, AL.min, 16)
+                tt(c("qu", a, b), c("qa", a, b), c("hh", a, b), AL.subtract, 32)
+        else:
+            ts(c("volN", 16, 96), qv(16, 96), 1.0, AL.max, 80, 16.0, AL.min)
+            inner_volumes()
+        for a, b in (left, right):
+            ts(c("volN", a, b), qv(a, b), 1.0, AL.max, 16, 16.0, AL.min)
+        spread_volumes(0, 16, "P1", [])
+        spread_volumes(96, 112, "P1", [(0, V, 128), (128, 0, 128), (256, 1408, 128), (384, 1664, 128)], 256)
+        if not last:
+            tt(v("qa"), v("volN"), v("dvO", ALL, t + 1), AL.add, 224)
+            ts(v("ta"), v("qa"), 10.5, AL.is_gt, 112, 1000.0, AL.mult)
+            ts(v("qq"), v("qa"), -7.5, AL.add, 112)
+            tt(v("thr1"), v("qq"), v("ta"), AL.add, 224)
 
-        def one_hot(a, b):
-            ts(c("t40", 8 * a, 8 * b), nO(8 * a, 8 * b), -float(W), AL.add, 40)
-            tt(c("t40", 8 * a, 8 * b), c("t40", 8 * a, 8 * b), th(8 * a, 8 * b), AL.mult, 64)
-            ts(c("nA16", 8 * a, 8 * b), c("t40", 8 * a, 8 * b), float(W), AL.add, 40)
-            act(v("G", t, S_(128 * a, 128 * b)), ind(v("Gt"), c("nA16", 8 * a, 8 * b)), 128 * (b - a))
-            mm([(c("P4", 8 * j, 8 * j + 8), Gj(j), bo8, True, True, 64) for j in range(a, b)])
-            cp(c("hc", 8 * a, 8 * b), c("P4", 8 * a, 8 * b), 40)
-            mm([(c("P3", 128 * (j - a), 128 * (j - a + 1)), Gj(j), Ib, True, True, 128) for j in range(a, b)])
-            act(c("OHlo", 128 * a, 128 * b), c("P3", 0, 128 * (b - a)), 128 * (b - a), AF.Sign)
+    def inner_volumes():
+        for (a, b), bank in zip(((16, 40), (40, 72), (72, 96)), CFG["vbank"]):
+            spread_volumes(a, b, bank, [(0, 16 * a - 128, 16 * (b - a))])
+
+    def lists(t):
+        last = t == RO - 1
+        e = t % 2
+        EQ = "EQ"
+        sl = lambda name, a, b: v(name, e, S_(8 * a, 8 * b))
+        Gj = lambda a, b: v("G", e, S_(128 * a, 128 * b))
+        vol = lambda a, b: v("volM", e, S_(128 * a, 128 * b))
+
+        def names(j):
+            ts(v("b16", e, j), ind(v("ntb"), sl("o16", j, j + 1)), 0.0625, AL.mult, 128, -0.46875, AL.add)
+            nj = 4 if CFG["late"][t] else 5
+            for s in range(2 if j < nj else 0):
+                ts(v("b16a", e, S_(nj * s + j, 128 * nj, 2 * nj)), v("b16", e, j, S_(s, 128, 2)), float(s * UB), AL.add, 32)
+
+        def present(a, b):
+            tt(c("t40", 8 * a, 8 * b), sl("nW", a, b), sl("th", a, b), AL.mult, 16 * (b - a))
+            ts(sl("nA16", a, b), c("t40", 8 * a, 8 * b), float(W), AL.add, 40)
+            act(Gj(a, b), ind(v("Gt"), sl("nA16", a, b)), 128 * (b - a))
+            act(vol(a, b), ind(v("volE"), sl("nA16", a, b)), 128 * (b - a))
+            mm([(c("P2", 440 + 16 * (j - a), 456 + 16 * (j - a)), Gj(j, j + 1), v("hcm"), True, True, 64) for j in range(a, b)])
+            cp(v("hc", S_(a, b)), c("P2", 440, 440 + 16 * (b - a)), 48)
+            mm([(c("P1", 128 * (j - a + 1), 128 * (j - a + 2)), Gj(j, j + 1), Ib, True, True, 128) for j in range(a, b)])
+            act(v("OL", S_(a, b), ALL, mid), c("P1", 128, 128 * (b - a + 1)), 128 * (b - a), AF.Sign)
             for k in range(8):
                 for j in range(a, b):
-                    ts(v("OH", 5 * k + j), v("ring"), c("hc", 8 * j + k, 8 * j + k + 1), AL.is_equal, 56)
+                    ts(v("OH", 5 * k + j), v("ring"), v("hc", j, S_(k, k + 1)), AL.is_equal, 56)
 
-        def volumes(a, b):
-            act(c("volM", 128 * a, 128 * b), ind(v("volE"), v("oM16", t, S_(8 * a, 8 * b))), 128 * (b - a))
-            mm([(c("P4", 64, 64 + 8 * (b - a)), c("Dq", 15 - q, 143 - q), c("volM", 128 * a + q, 128 * b, 16), q == 0, q == 15, 64)
-                for q in range(16)])
-            tt(vt(8 * a, 8 * b), c("P4", 64, 64 + 8 * (b - a)), th(8 * a, 8 * b), AL.mult, 40)
+        def tally(a, b):
+            return [(v("OL", j, k, S_(112 - 16 * ((k - 1) % 8), 240 - 16 * ((k - 1) % 8))), v("OH", 5 * k + j), 112)
+                    for j in range(a, b) for k in range(8)]
 
-        cp(nO(0, 32), c("o16", 0, 32), 32)
-        cp(v("oM16", t, S_(0, 32)), c("o16", 0, 32), 32)
-        tt(c("ne", 8, 32), nO(8, 32), nO(0, 24), AL.not_equal, 48)
-        tt(th(0, 32), c("ne", 0, 32), c("mm", 0, 32), AL.mult, 64)
-        volumes(0, 4)
-        tt(c("sm", 0, 16), vt(0, 16), vt(16, 32), AL.add, 32)
-        tt(c("sm", 16, 24), c("sm", 0, 8), c("sm", 8, 16), AL.add, 16)
-        ts(c("sm", 24, 32), c("sm", 16, 24), 43.5, AL.is_lt, 8)
-        one_hot(0, 4)
-        tt(c("sm", 24, 32), c("sm", 24, 32), c("mm", 32, 40), AL.mult, 16)
-        ts(nO(32, 40), c("P1", 128, 136), kc, AL.subtract, 8)
-        tt(c("ne", 32, 40), nO(32, 40), nO(24, 32), AL.not_equal, 16)
-        tt(th(32, 40), c("ne", 32, 40), c("sm", 24, 32), AL.mult, 16)
-        one_hot(4, 5)
-        tt(c("sm", 32, 40), nO(32, 40), nO(24, 32), AL.subtract, 16)
-        tt(c("sm", 32, 40), c("sm", 32, 40), c("sm", 24, 32), AL.mult, 16)
-        tt(c("sm", 32, 40), nO(24, 32), c("sm", 32, 40), AL.add, 16)
-        cp(v("oM16", t, S_(32, 40)), c("sm", 32, 40), 8)
-        tile_names(v("b16", 0), v("oM16", t, S_(32, 40)))
-        lane_major(t, 4, 0)
-        mm([(c("P3", 16 * ((k - 1) % 8), 16 * ((k - 1) % 8) + 16, p=p112), v("OH", 5 * k + j),
-             c("OHlo", 128 * j + 16 * k, 128 * j + 16 * k + 16), j == 0, j == 4, 64) for k in range(8) for j in range(5)])
-        act(v("Hs", p=p112), c("P3", 0, 128, p=p112), 128)
-        mm([(c("P4", 0, 112), v("Hs", p=p112), v("cb", 0, S_(0, 112), p=p112), True, True, 112)])
-        cp(c("nS", 0, 16), c("P4", 0, 16), 16)
-        cp(c("nS", 16, 32), c("P4", 96, 112), 16)
-        cp(v("nF", t, S_(16, 96)), c("P4", 16, 96), 80)
+        def equal(a, b):
+            n = 128 * (b - a)
+            per = 512 // n
+            tt(sl("pre", a, b), sl("nW", a, b), c("lane", 8 * a, 8 * b), AL.subtract, 16 * (b - a))
+            tt(sl("thm", a, b), sl("th", a, b), c("thr", 8 * a, 8 * b), AL.mult, 16 * (b - a))
+            for k0 in range(0, 8, per):
+                bank = "P%d" % (3 + (k0 // per) % 2)
+                mm([(c(bank, n * (k - k0), n * (k - k0 + 1)), v("selP", k), Gj(a, b), True, True, n) for k in range(k0, k0 + per)])
+                for k in range(k0, k0 + per):
+                    for j in range(a, b):
+                        x = n * (k - k0) + 128 * (j - a)
+                        ts(v(EQ, k, S_(128 * j - 128, 128 * j)), c(bank, x, x + 128), v("hc", j, S_(8 + k, 9 + k)), AL.is_equal, 128)
+            mm(grp(c("P3", 0, n), [(c("wpad", 112 - 16 * k, 240 - 16 * k), v(EQ, k, S_(128 * a - 128, 128 * b - 128)), n) for k in range(8)]))
+            act(c("Wb", 128 * a - 128, 128 * b - 128), c("P3", 0, n), n)
+            mm(grp(c("P4", 0, 8 * (b - a)), [(c("Dq", 15 - q, 143 - q), c("Wb", 128 * a - 128 + q, 128 * b - 128, 16), 64) for q in range(16)]))
+            f = c("ff", 8 * a, 8 * b)
+            tt(f, c("P4", 0, 8 * (b - a)), sl("thm", a, b), AL.is_lt, 32)
+            tt(f, f, sl("pre", a, b), AL.mult, 64)
+            tt(f, f, c("dump", 8 * a, 8 * b), AL.add, 64)
+            cp(sl("off16", a, b), f, 32)
+
+        names(0)
+        for j in range(1, 5):
+            off = sl("o16", j - 1, j)
+            act(v("ag"), ind(v("At"), off), 128)
+            cuts = CFG["split"][t]
+            for a, b in zip(cuts, cuts[1:]):
+                either(c("Vg", 16 * a, 16 * b), ind(v("volE"), v("b16", e, j - 1, S_(a, b))), 16 * (b - a), lend=CFG["lendv"][t])
+            cp(v("bn"), v("b16", e, j - 1), 128)
+            mm([(c("P0", 0, 128), v("bn"), If, True, True, 512)])
+            mm([(c("P1", 0, 128), v("ag"), Ib, True, True, 128)])
+            rest = grp(c("P0", 129, 384, 2), [(v("bn"), If, 512), (Ib, kcr, 128)] + [(negI, v("eq", i), 128) for i in range(j)])
+            mm(rest[:2])
+            for i in range(j):
+                tt(v("eq", i), c("P0", 0, 128), v("Bc", i), AL.is_equal, 128)
+            act(c("A2", 1, 256, 2), c("P1", 0, 128), 128)
+            mm(rest[2:])
+            held = v("Bc", j - 1, S_(0, 128, 16))
+            if j == 4:
+                mm(grp(c("P2", 224, 232), [(vol(i, i + 1), I8, 64) for i in range(4)]))
+                ts(v("bo1"), c("P2", 224, 232), 43.5, AL.is_gt, 8, 4095.0 * 4096, AL.mult)
+                ts(v("bo2"), c("P2", 224, 232), 0.5, AL.is_lt, 8, 4095.0 * 4096, AL.mult)
+                tt(v("bo1"), v("bo1"), held, AL.add, 16)
+                tt(v("bo2"), v("bo1"), v("bo2"), AL.add, 16)
+                held = v("bo2")
+            mm([(c("P0", 128 + 2 * k, 384, 32), c("Vg", k, 2048, 16), I8, True, True, 64) for k in range(16)])
+            scan(v("KS"), v("A2"), c("P0", 128, 384), 0.0, AL.mult, AL.add, 256)
+            scan(v("SC"), v("rmask"), c("KS", 1, 256, 2), 0.0, AL.mult, AL.max, 128)
+            tt(v("ka"), c("SC", 15, 128, 16), held, AL.max, 16)
+            ts(v("kb"), v("ka") if j == 4 else c("SC", 15, 128, 16), BIG, AL.add, 8, -BIG, AL.add)
+            tt(c("hold", 0, 128, 16), v("ka"), v("kb"), AL.subtract, 16)
+            scan(v("Bc", j), v("rmask"), v("hold"), 0.0, AL.mult, AL.add, 128)
+            tt(v("MK"), qmask, v("Bc", j), AL.mult, 128)
+            mm(grp(c("P0", 0, 8), [(Ib, v("cW"), 64), (v("MK"), v("cm"), 256)]))
+            ts(sl("o16", j, j + 1), c("P0", 0, 8), float(W), AL.add, 8)
+            if j == 4:
+                tt(sl("th", 4, 5), c("P0", 0, 8), sl("nW", 3, 4), AL.not_equal, 8)
+            cp(sl("nW", j, j + 1), c("P0", 0, 8), 8)
+            names(j)
+            if j == 2:
+                cp(sl("th", 0, 1), v("mm"), 8)
+                tt(c("ne", 8, 24), sl("nW", 1, 3), sl("nW", 0, 2), AL.not_equal, 32)
+                for i in (1, 2):
+                    tt(sl("th", i, i + 1), c("ne", 8 * i, 8 * i + 8), v("mm"), AL.mult, 16)
+                present(0, 3)
+                tt(c("ff", 0, 8), sl("nW", 0, 1), c("lane", 0, 8), AL.subtract, 16)
+                tt(c("ff", 0, 8), c("ff", 0, 8), v("mm"), AL.mult, 16)
+                tt(c("ff", 0, 8), c("ff", 0, 8), c("dump", 0, 8), AL.add, 16)
+                cp(sl("off16", 0, 1), c("ff", 0, 8), 8)
+            if j == 3:
+                tt(c("ne", 24, 32), sl("nW", 3, 4), sl("nW", 2, 3), AL.not_equal, 16)
+                tt(sl("th", 3, 4), c("ne", 24, 32), v("mm"), AL.mult, 16)
+                present(3, 4)
+        mm(grp(c("P2", 0, 112), tally(0, 4)))
+        cp(v("nA"), c("P2", 0, 112), 112)
+        tt(c("es", 0, 8), sl("th", 1, 2), sl("th", 2, 3), AL.add, 16)
+        tt(c("es", 0, 8), c("es", 0, 8), sl("th", 3, 4), AL.add, 16)
+        ts(c("es", 0, 8), c("es", 0, 8), 0.0625, AL.mult, 8)
+        equal(1, 4)
+        present(4, 5)
+        mm(grp(c("P2", 0, 112), [(Ib, v("nA"), 112)] + tally(4, 5)))
+        cp(c("nS", 0, 16), c("P2", 0, 16), 16)
+        cp(c("nS", 16, 32), c("P2", 96, 112), 16)
         exchange([(c("nS", 0, 16), v("nR", t, S_(16, 32)))], [(c("nS", 16, 32), v("nR", t, S_(0, 16)))], 2.2)
+        cp(v("nF", t, S_(16, 96)), c("P2", 16, 96), 80)
+        if not last:
+            x0 = (STEP * (t + 1)) % V // 16
+            tt(c("smallR", 0, 88 - x0), c("P2", 8 + x0, 96), c("thr1", 8 + x0, 96), AL.is_gt, 64)
+            tt(c("smallR", 104 - x0, 96), c("P2", 16, 8 + x0), c("thr1", 16, 8 + x0), AL.is_gt, 80)
+            tt(c("thB", 8, 16), c("thr1", 8, 16), c("nS", 8, 16), AL.subtract, 16)
+            tt(c("thB", 16, 24), c("thr1", 96, 104), c("nS", 16, 24), AL.subtract, 16)
+            ts(c("hh", 16, 96), c("P2", 16, 96), 3.0, AL.min, 80)
+            tt(c("qu", 16, 96), c("qa", 16, 96), c("hh", 16, 96), AL.subtract, 160)
+        mm(grp(c("P2", 184, 224), [(c("Dq", 15 - q, 143 - q), v("volM", e, S_(q, 640, 16)), 64) for q in range(16)]))
+        cp(v("Zq"), c("P2", 184, 224), 40)
+        mm(grp(c("P2", 112, 120), [(Ib, c("Zq", 8 * i, 8 * i + 8), 64) for i in range(5)]))
+        ts(v("z16", e), c("P2", 112, 120), 7.0, AL.add, 8)
+        ts(c("es", 8, 16), sl("th", 4, 5), 0.0625, AL.mult, 8)
+        tt(v("ev", e), c("es", 0, 8), c("es", 8, 16), AL.add, 16)
+        equal(4, 5)
+        if not last:
+            ts(c("volN", 16, 96), c("qu", 16, 96), 1.0, AL.max, 80, 16.0, AL.min)
+            inner_volumes()
+        own = lambda a, b: grp(c("P2", 344 + a, 344 + b), [(shmK, v("nF", t, S_(8 + a, 8 + b)), 80), (Ib, c("x16r", a, b), 80),
+                                                           (Ib, c("qtab", a, b), 80)])
+        mm([(c("P2", 240, 320), shm, v("nF", t, S_(16, 96)), True, True, 80)] + own(8, 88))
+        ts(v("nOff", e, S_(8, 88)), c("P2", 240, 320), 7.0, AL.add, 80)
+        ts(v("sel", e, S_(8, 88)), c("P2", 352, 432), float(W), AL.min, 80)
         tt(v("nF", t, S_(0, 16)), c("nS", 0, 16), v("nR", t, S_(0, 16)), AL.add, 32)
         tt(v("nF", t, S_(96, 112)), c("nS", 16, 32), v("nR", t, S_(16, 32)), AL.add, 32)
-        volumes(4, 5)
-        tt(c("sm", 16, 24), c("sm", 16, 24), vt(32, 40), AL.add, 16)
-        ts(v("z16", t), c("sm", 16, 24), -1.0, AL.add, 8, 0.0, AL.max)
-        tt(c("sm", 0, 16), th(8, 24), th(24, 40), AL.add, 32)
-        tt(c("sm", 24, 32), c("sm", 0, 8), c("sm", 8, 16), AL.add, 16)
-        ts(vt(40, 48), c("sm", 24, 32), 0.0625, AL.mult, 8)
-        yield
-        EQ = "EQ%d" % (t % 2)
-        mm([(c("P3", 8 * j - 8, 8 * j), Gj(j), v("aB"), True, True, 64) for j in range(1, 5)])
-        cp(c("cc", 0, 32), c("P3", 0, 32), 32)
-        for k in range(8):
-            bank = "P%d" % (3 + k % 2)
-            mm([(v(bank), v("selP", k), v("G", t, S_(128, 640)), True, True, 512)])
-            for j in range(4):
-                ts(v(EQ, k, S_(128 * j, 128 * j + 128)), c(bank, 128 * j, 128 * j + 128),
-                   c("cc", 8 * j + k, 8 * j + k + 1), AL.is_equal, 128)
-        mm([(v("P3"), c("wpad", 112 - 16 * k, 240 - 16 * k), v(EQ, k), k == 0, k == 7, 512) for k in range(8)])
-        act(v("Wb"), v("P3"), 512)
-        mm([(c("P4", 0, 32), c("Dq", 15 - q, 143 - q), c("Wb", q, 512, 16), q == 0, q == 15, 64) for q in range(16)])
-        tt(c("cc", 8, 40), c("P4", 0, 32), c("thr", 0, 32), AL.is_lt, 32)
-        ms(c("cc", 0, 8), 1.0, 8)
-        tt(v("cc"), v("cc"), th(0, 40), AL.mult, 80)
-        tt(v("st1", S_(0, 40)), nO(0, 40), v("dump"), AL.subtract, 80)
-        tt(v("cc"), v("cc"), v("st1", S_(0, 40)), AL.mult, 80)
-        tt(v("cc"), v("cc"), v("dump"), AL.add, 80)
-        cp(v("off16", t), v("cc"), 40)
-        dma("sync", v("S"), v("Z0"), 5.0)
-        uw = c(Wt, UB, UB + W)
-        act(v("um"), ind(uw, v("oM16", t)), 640)
-        act(v("wZ"), ind(c("wall", 0, 256), v("z16", t)), 128)
-        mm([(c("P5", q, 512, 16), v("Rq", q), vt(0, 32), True, True, 64) for q in range(16)])
-        mm([(c("P6", q, 256, 16), v("Rq", q), vt(32, 48), True, True, 64) for q in range(16)])
-        tt(c("prod", 0, 512), v("P5"), c("um", 0, 512), AL.mult, 512)
-        tt(c("prod", 512, 640), c("P6", 0, 128), c("um", 512, 640), AL.mult, 128)
-        mm([(c("P7", 384, 512), If, c("prod", 128 * j, 128 * j + 128), j == 0, j == 4, 512) for j in range(5)])
+
+    def border_counts(t):
+        last = t == RO - 1
+        e = t % 2
+        own = lambda a, b: grp(c("P2", 344 + a, 344 + b), [(shmK, v("nF", t, S_(8 + a, 8 + b)), 64), (Ib, c("x16r", a, b), 64),
+                                                           (Ib, c("qtab", a, b), 64)])
+        mm([(c("P2", 232, 240), shm, v("nF", t, S_(8, 16)), True, True, 64),
+            (c("P2", 320, 328), shm, v("nF", t, S_(96, 104)), True, True, 64),
+            (c("P2", 328, 336), shm, v("nF", t, S_(0, 8)), True, True, 64),
+            (c("P2", 336, 344), shm, v("nF", t, S_(104, 112)), True, True, 64)] + own(0, 8) + own(88, 96))
+        ts(v("sel", e, S_(0, 8)), c("P2", 344, 352), float(W), AL.min, 8)
+        ts(v("sel", e, S_(88, 96)), c("P2", 432, 440), float(W), AL.min, 8)
+        ts(v("nOff", e, S_(0, 8)), c("P2", 232, 240), 7.0, AL.add, 8)
+        ts(v("nOff", e, S_(88, 96)), c("P2", 320, 328), 7.0, AL.add, 8)
+        if not last:
+            ts(v("nOff", e, S_(96, 104)), c("P2", 328, 336), 7.0 + WT, AL.add, 8)
+            ts(v("nOff", e, S_(104, 112)), c("P2", 336, 344), 7.0 + 2 * WT, AL.add, 8)
+
+    def fields(t):
+        last = t == RO - 1
+        e = t % 2
+        EQ = "EQ"
+        uw = c("Wf", 0, UB)
+        sl = lambda name, a, b: v(name, e, S_(8 * a, 8 * b))
+        dma("sync", c("S", V, W), v("Z0"), 3.0)
+        for a, b in ((8, 48), (48, 88), (0, 8), (88, 96)):
+            act(c("S", 16 * a, 16 * b), ind(uw, v("sel", e, S_(a, b))), 16 * (b - a))
+        act(c("um", 0, 128), ind(uw, sl("o16", 0, 1)), 128)
+        act(c("um", 128, 256), ind(uw, sl("o16", 4, 5)), 128)
+        act(v("wZ"), ind(c("wall", 0, WT), v("z16", e)), 128)
+        for a, b in ((0, 2), (2, 4), (4, 5)):
+            tt(c("prod", 128 * a, 128 * b), ind(uw, sl("o16", a, b)), v("volM", e, S_(128 * a, 128 * b)), AL.mult, 128 * (b - a))
+        mm([(c("P6", 128 + q, 256, 16), v("Rq", q), v("ev", e), True, True, 64) for q in range(16)])
+        mm(grp(c("P7", 384, 512), [(If, c("prod", 128 * j, 128 * j + 128), 512) for j in range(5)]))
         tt(v("Mm"), c("P7", 384, 512), v("wZ"), AL.mult, 128)
-        tt(v("Dd"), c("um", 512, 640), c("um", 0, 128), AL.subtract, 256)
+        tt(v("Dd"), c("um", 128, 256), c("um", 0, 128), AL.subtract, 256)
         tt(v("De"), c("P6", 128, 256), v("Dd"), AL.mult, 128)
         tt(c("est", 0, 128), v("Mm"), v("De"), AL.subtract, 256)
         ts(c("P7", 256, 384), v("Dd"), 0.125, AL.mult, 128)
         for j in range(1, 5):
             tt(c("est", 128 * j, 128 * j + 128), c("P7", 256, 384), c("est", 128 * j - 128, 128 * j), AL.add, 128)
+        back = lambda a, b, s=1: S_(b - 1, a - 1 if a else None, -s)
+
+        def bound(src, row, a, n, o):
+            scan(c("Omin", o, o + n), v(src, row, S_(a, a + 2 * n, 2)), v(src, row, S_(a + 1, a + 2 * n, 2)), 1e29, AL.min, AL.min, n)
+            scan(v("Omax", back(o, o + n)), v(src, row, back(a, a + 2 * n - 1, 2)), v(src, row, back(a + 1, a + 2 * n, 2)),
+                 0.0, AL.max, AL.max, n)
+
+        late = CFG["late"][t]
+        nj = 4 if late else 5
+        lo, hi = (("Rlo", 0), ("Rhi", 0)) if late else (("P7", 0), ("P7", 128))
         for k in range(8):
-            x = ind(c(Wt, 0, UB + W), v("b16a", t, S_(80 * k, 80 * k + 80)))
             for h in range(2):
-                xh = ind(c(Wt, 0, UB + W), v("b16a", t, S_(80 * k + 40 * h, 80 * k + 40 * h + 40)))
-                (cp if k in HELP[t] else lambda o, x, n: act(o, x, n))(v("Ug", k % 4, S_(640 * h, 640 * h + 640)), xh, 640)
-            n = 40 * LV
-            for a in range(0, 640, n):
-                o = a + 640 * (k % 2)
-                scan(c("Omin", o, o + n), v("Ug", k % 4, S_(2 * a, 2 * a + 2 * n, 2)), v("Ug", k % 4, S_(2 * a + 1, 2 * a + 2 * n, 2)),
-                     1e29, AL.min, AL.min, n)
-                scan(v("Omax", S_(o + n - 1, o - 1 if o else None, -1)),
-                     v("Ug", k % 4, S_(2 * a + 2 * n - 2, 2 * a - 1 if a else None, -2)),
-                     v("Ug", k % 4, S_(2 * a + 2 * n - 1, 2 * a, -2)), 0.0, AL.max, AL.max, n)
+                x = ind(v("Wf"), v("b16a", e, S_(8 * nj * (2 * k + h), 8 * nj * (2 * k + h + 1))))
+                either(v("Ug", k % 4, S_(128 * nj * h, 128 * nj * (h + 1))), x, 128 * nj, lend=CFG["lend"][t])
+            for i in range(8):
+                bound("Ug", k % 4, 32 * nj * i, 16 * nj, 128 * nj * (k % 2) + 16 * nj * i)
             if k % 2:
-                tt(c("P7", 16 * k - 16, 16 * k + 16), c("Omin", 39, 1280, 40), unsc, AL.mult, 64)
-                tt(c("P7", 112 + 16 * k, 144 + 16 * k), c("Omax", 0, 1280, 40), unsc, AL.mult, 64)
+                a = 16 * k - 16
+                tt(c(lo[0], lo[1] + a, lo[1] + a + 32), c("Omin", 8 * nj - 1, 256 * nj, 8 * nj), c("un2", 0, 32), AL.mult, 64)
+                tt(c(hi[0], hi[1] + a, hi[1] + a + 32), c("Omax", 0, 256 * nj, 8 * nj), c("un2", 0, 32), AL.mult, 64)
+        if late:
+            for k in range(4):
+                tt(v("Ul", k), ind(uw, v("b16", e, 4, S_(32 * k, 32 * k + 32))), v("lev"), AL.mult, 512)
+                for i in range(4):
+                    bound("Ul", k, 128 * i, 64, 256 * k + 64 * i)
+            tt(c("P7", 0, 128), c("Omin", 7, 1024, 8), unsc, AL.mult, 256)
+            tt(c("P7", 128, 256), c("Omax", 0, 1024, 8), unsc, AL.mult, 256)
+            tt(c("P7", 0, 128), c("P7", 0, 128), v("Rlo"), AL.min, 128)
+            tt(c("P7", 128, 256), c("P7", 128, 256), v("Rhi"), AL.max, 128)
         sw = v("S")
         for j in range(5):
             ej = c("ec", 128 * j, 128 * j + 128)
-            tt(v("c5", j), c("P7", 0, 128), c("est", 128 * j, 128 * j + 128), AL.max, 128)
-            tt(ej, c("P7", 128, 256), v("c5", j), AL.min, 128)
-        mid = S_(112, 128)
+            tt(c("prod", 128 * j, 128 * j + 128), c("P7", 0, 128), c("est", 128 * j, 128 * j + 128), AL.max, 128)
+            tt(ej, c("P7", 128, 256), c("prod", 128 * j, 128 * j + 128), AL.min, 128)
         for j in range(1, 5):
             mm([(c("P5", 128 * j - 128, 128 * j), c("ec", 128 * j, 128 * j + 128), If, True, True, 512)])
         for j in range(1, 5):
-            zh, zl = "Zh%d" % (j % 2), "Zl%d" % (j % 2)
+            zh, zl = 2 * (j % 2), 2 * (j % 2) + 1
             turned, bank = c("P5", 128 * j - 128, 128 * j), "P%d" % (7 - j % 2)
-            act(v(zh, S_(None), mid), turned, 128)
-            tt(v(zl, S_(None), mid), turned, v(zh, S_(None), mid), AL.subtract, 128)
-            mm([(c(bank, 0, 128), v(z, k, S_(112 - 16 * k, 240 - 16 * k)), v(EQ, k, S_(128 * j - 128, 128 * j)),
-                 k == 0 and z == zh, k == 7 and z == zl, 128) for z in (zh, zl) for k in range(8)])
+            act(v("Zp", zh, ALL, mid), turned, 128)
+            tt(v("Zp", zl, ALL, mid), turned, v("Zp", zh, ALL, mid), AL.subtract, 128)
+            mm(grp(c(bank, 0, 128), [(v("Zp", z, k, S_(112 - 16 * k, 240 - 16 * k)), v(EQ, k, S_(128 * j - 128, 128 * j)), 128)
+                                     for z in (zh, zl) for k in range(8)]))
             act(v("Ss", j - 1), c(bank, 0, 128), 128)
         for j in range(5):
-            off = v("off16", t, S_(8 * j, 8 * j + 8))
+            off = sl("off16", j, j + 1)
             if j == 0:
                 cp(ind(sw, off), c("ec", 0, 128), 128)
             else:
@@ -582,97 +727,114 @@ def rank_program(g, core, T, topo):
         else:
             exchange([(c("S", V, 1664), c(Rb, 128, 256)), (c("S", 0, 128), c(Rb, 384, 512))],
                      [(c("S", 1664, W), c(Rb, 0, 128)), (c("S", 1408, V), c(Rb, 256, 384))], 3.0)
-        nf = lambda a, b: v("nF", t, S_(a, b))
-        mm([(c("P5", 0, 96), shm, nf(8, 104), True, True, 96), (c("P5", 96, 104), shm, nf(0, 8), True, True, 64),
-            (c("P5", 104, 112), shm, nf(104, 112), True, True, 64)])
         end = 96 if last else 112
-        head = W + 16 * end - 128
-        ts(c("nOff", 0, 96), c("P5", 0, 96), 1.0, AL.max, 96, -1.0, AL.add)
-        if not last:
-            ts(c("nOff", 96, 104), c("P5", 96, 104), 1.0, AL.max, 8, 255.0, AL.add)
-            ts(c("nOff", 104, 112), c("P5", 104, 112), 1.0, AL.max, 8, 511.0, AL.add)
-        ts(c("st1", 0, 8), c("P5", 0, 8), 0.5, AL.is_gt, 8, float(head), AL.mult)
-        ts(c("st1", 8, end), c("P5", 8, end), 0.5, AL.is_gt, 104, float(W - 128), AL.mult)
-        tt(c("st1", 0, end), c("st1", 0, end), c("cid", 0, end), AL.add, 224)
-        cp(c("sel", 0, end), c("st1", 0, end), 112)
-        nxt_w = "W%d" % ((t + 1) % 2)
 
-        def weigh(a, b, at):
-            tt(c(Wt, UB + at, UB + at + 16 * (b - a)), ind(v("wall"), c("nOff", a, b)), c("S", 16 * a, 16 * b), AL.mult, 16 * (b - a))
-
-        def pick(a, b, top):
-            act(c(nxt_w, UB + 16 * a, UB + 16 * b), ind(c(Wt, UB, UB + top), c("sel", a, b)), 16 * (b - a))
+        def weigh(a, b):
+            tt(c("Wf", 16 * a, 16 * b), ind(v("wall"), v("nOff", e, S_(a, b))), c("S", 16 * a, 16 * b), AL.mult, 16 * (b - a))
             if last:
-                dma("sync", v("y", S_(16 * a, 16 * b)), c(nxt_w, UB + 16 * a, UB + 16 * b), 2.0 + (b - a) * 0.03)
+                dma("sync", v("y", S_(16 * a, 16 * b)), c("Wf", 16 * a, 16 * b), 2.0 + (b - a) * 0.03)
             else:
-                scaled(nxt_w, 16 * a, 16 * b)
-        weigh(8, 48, W)
-        pick(8, 48, W + 640)
-        weigh(48, 88, W + 640)
-        pick(48, 88, W + 1280)
+                scaled(16 * a, 16 * b)
+        weigh(8, 48)
+        weigh(48, 88)
         tt(c("S", 0, 128), c("S", 0, 128), c(Rb, 0, 128), AL.add, 256)
         tt(c("S", 1408, 16 * end), c("S", 1408, 16 * end), c(Rb, 128, 16 * end - 1280), AL.add, 32 * end - 2816)
-        weigh(88, end, W + 1280)
-        weigh(0, 8, head)
-        pick(88, end, head)
-        pick(0, 8, head + 128)
-        yield
+        weigh(0, 8)
+        weigh(88, end)
 
-    parts = [one_round(t) for t in range(RO)]
-    for k, t in enumerate((0, 0, 1, 0, 1, 2, 1, 2, 2)):
-        bias[0] = BIAS[k]
-        next(parts[t])
+    steps = [(lanes, 0), (lists, 0), (lanes, 1), (fields, 0), (lists, 1), (lanes, 2), (fields, 1), (lists, 2), (fields, 2)]
+    for k, (f, t) in enumerate(steps):
+        bias[0] = CFG["bias"][k]
+        if f is fields:
+            border_counts(t)
+        f(t)
 
     n = len(ops)
-    succ = [[] for _ in range(n)]
-    for i, o in enumerate(ops):
-        for d in o["deps"]:
-            succ[d].append(i)
-    prio = [0.0] * n
-    for i in range(n - 1, -1, -1):
-        prio[i] = ops[i]["d"] + max([prio[s] + LAT_X for s in succ[i]] + [0.0])
-    prio = [x + o["b"] + TIE[0] * ((k * TIE[1]) % 101) / 101.0 for k, (x, o) in enumerate(zip(prio, ops))]
-    left = [len(o["deps"]) for o in ops]
-    ready = [i for i in range(n) if left[i] == 0]
-    rt = [0.0] * n
-    fin = [0.0] * n
-    free, busy, order = {}, {}, []
-    while ready:
-        st = {i: max(rt[i], free.get(ops[i]["e"], 0.0)) for i in ready}
-        i0 = min(ready, key=lambda i: (st[i], -prio[i]))
-        e = ops[i0]["e"]
-        i = max([k for k in ready if ops[k]["e"] == e and st[k] <= st[i0] + min(WINDOW, ops[i0]["d"])], key=lambda k: prio[k])
-        ready.remove(i)
-        o = ops[i]
-        fin[i] = st[i] + o["d"]
-        hold = o["d"] if o["k"] == "c" else (0.0 if e == "ext" else (0.1 if o["k"] == "dma" else 0.5))
-        free[e] = st[i] + hold
-        busy[e] = busy.get(e, 0.0) + hold
-        order.append(i)
-        for s in succ[i]:
-            rt[s] = max(rt[s], fin[i] + (LAT_S if ops[s]["e"] == e else LAT_X))
-            left[s] -= 1
-            if left[s] == 0:
-                ready.append(s)
-    STATS.update({"span": max(fin), "busy": busy, "n": n, "fin": fin, "ops": ops, "order": order})
+    if "order" not in PLAN:
+        lat_x, lat_s, window = CFG["lat"]
+        pred = [[(d, 0) for d in o["deps"]] + [(d, 1) for d in o["war"]] + [(d, 2) for d in o["order"]] for o in ops]
+        succ = [[] for _ in range(n)]
+        for i in range(n):
+            for d, kind in pred[i]:
+                succ[d].append((i, kind))
+
+        def wait(d, ed, e, kind):
+            if ed != e or ops[d]["k"] != "c":
+                return lat_x
+            return lat_s if kind == 0 or (kind == 1 and CFG["same"]) else 0.0
+
+        def schedule(prio, before, after, eng, back):
+            left_ = [len(x) for x in before]
+            ready, rt, fin, free, order = {}, [None] * n, [0.0] * n, {}, []
+            eng = list(eng)
+
+            def enter(i):
+                rt[i] = {}
+                for e in ([eng[i]] if back else ops[i]["alt"]):
+                    rt[i][e] = max([fin[d] + (wait(i, e, eng[d], k) if back else wait(d, eng[d], e, k)) for d, k in before[i]] + [0.0])
+                    ready.setdefault(e, []).append(i)
+            for i in range(n):
+                if left_[i] == 0:
+                    enter(i)
+            while len(order) < n:
+                t0, e = min((max(min(rt[i][e] for i in lst), free.get(e, 0.0)), e) for e, lst in ready.items() if lst)
+                rank_ = lambda k: prio[k] - (ops[k]["lend"] if e != ops[k]["e"] else 0.0)
+                i = max([k for k in ready[e] if rt[k][e] <= t0 + window], key=rank_)
+                if e != ops[i]["e"]:
+                    due = [k for k in ready[e] if rt[k][e] <= t0 + CFG["look"] * ops[i]["alt"][e][0] and rank_(k) > rank_(i)]
+                    if due:
+                        i = min(due, key=lambda k: rt[k][e])
+                for x in rt[i]:
+                    ready[x].remove(i)
+                o = ops[i]
+                eng[i] = e
+                d = o["alt"][e][0]
+                hold = d if o["k"] == "c" else (0.0 if e == "ext" else (0.1 if o["k"] == "dma" else 0.5))
+                st = max(t0, rt[i][e])
+                if back:
+                    st = max(rt[i][e], t0 - (d - hold))
+                fin[i] = st + d
+                free[e] = fin[i] if back else st + hold
+                order.append(i)
+                for s, k in after[i]:
+                    left_[s] -= 1
+                    if left_[s] == 0:
+                        enter(s)
+            return max(fin), fin, order, eng
+
+        eng = [o["e"] for o in ops]
+        tail = [0.0] * n
+        for i in range(n - 1, -1, -1):
+            tail[i] = ops[i]["d"] + max([tail[s] + wait(i, eng[i], eng[s], k) for s, k in succ[i]] + [0.0])
+        best = None
+        for turn in range(CFG["turns"]):
+            span, fin, order, eng = schedule([x + o["b"] - CFG["own"] * o["d"] for x, o in zip(tail, ops)], pred, succ, eng, False)
+            if best is None or span < best[0]:
+                best = (span, fin, order, eng)
+            STATS.setdefault("spans", []).append(round(span, 1))
+            tail = schedule(fin, succ, pred, eng, True)[1]
+        PLAN["order"], PLAN["eng"] = best[2], best[3]
+        STATS.update({"span": best[0], "n": n, "fin": best[1], "ops": ops})
 
     queue = {"pool": g, "vector": g.vector, "scalar": g.scalar, "tensor": g.tensor, "sync": g.sync}
     token, count, seen, n_d = {}, {}, {}, 0
-    for i in order:
+    for i in PLAN["order"]:
         o = ops[i]
-        e = o["e"]
+        e = PLAN["eng"][i]
         if e == "ext":
             token[i] = o["k"]
             continue
         need = {}
-        for d in o["deps"]:
+        for d in o["deps"] | o["war"]:
+            if d not in o["deps"] and not CFG["same"] and PLAN["eng"][d] == e and ops[d]["k"] == "c":
+                continue
             s, val = token[d]
             need[s] = max(need.get(s, 0), val)
         for s in sorted(need):
             if seen.get((e, s), 0) < need[s]:
                 queue[e].wait_ge(T.sem[s], need[s])
                 seen[(e, s)] = need[s]
-        ins = o["f"](queue[e])
+        ins = o["alt"][e][1](queue[e])
         if o["k"] == "c":
             count[e] = count.get(e, 0) + 1
             token[i] = ("c_" + e, count[e])

@@ -9,21 +9,30 @@ V, W, RO, STEP = 1536, 1792, 3, 1344
 F, B, I, U16 = "float32", "bfloat16", "int32", "uint16"
 BIG = 1.5 * 2.0 ** 35
 UB = W + 8
+TOP = 16 * 4096.0
 WT = 264
 CFG = {
-    "split": ((0, 32, 64, 96, 128),) * 3,
-    "late": (True, False, False),
-    "turns": 8,
-    "look": 0.5,
-    "lend": (100.0, 100.0, 30.0),
-    "lendv": (0.0, 50.0, 50.0),
-    "acts": 5,
-    "bias": (0, 0, 0, 0, 0, 0, 0, 0, 0),
+    "split": ((0, 64, 128), (0, 48, 128), (0, 32, 64, 96, 128)),
+    "per": ((0, 32, 64, 96, 128), (0, 32, 64, 96, 128), (0, 32, 64, 96, 112, 128)), "per4": ((0, 32, 64, 96, 128),) * 3, "lendf": 5.0, "fast": (1, 1, 0), "weigh": (8, 48, 88),
+    "turn": 128,
+    "turns": 5, "polish": 9000, "heat": 0.1, "lookt": 1.5, "gapt": 1.0, "est": 0,
+    "plain": 5,
+    "shake": 0.6,
+    "short": ((0, 0), (0, 0), (0, 0)),
+    "batch": ((0, 3, 4),) * 3,
+    "ebatch": ((1, 4),) * 3,
+    "look": 0.3,
+    "gap": 2.0,
+    "lend": (100.0, 50.0, 30.0),
+    "lendv": (0.0, 20.0, 5.0),
+    "acts": 8,
+    "lanes": (0, 0, 0), "steps": (0, 0, 0), "marks": (0, 0, 0), "equal": (0, 0, 0), "counts": (0, 0, 0), "start": (0, 0, 0),
+    "mean": (0, 0, 0), "bounds": (0, 0, 0), "sums": (0, 0, 0),
     "lat": (0.35, 0.17, 0.1),
     "same": True,
     "piece": 600,
-    "own": 1.0,
-    "vbank": ("P0", "P1", "P0"),
+    "own": 0.5,
+    "vbank": ("P1", "P0", "P1"),
 }
 STATS = {}
 
@@ -36,31 +45,27 @@ def _sb(names, shape, dtype):
 
 
 _sb("VD ntb", [W], I)
-_sb("At", [W], B)
 _sb("Gt volE", [W + 16], B)
 _sb("Wf", [UB + W], F)
-_sb("wall", [3 * WT], F)
 _sb("S", [1920], F)
+_sb("wall", [3 * WT], F)
 _sb("Z0", [256], F)
 _sb("Rb0 Rb1 Rb2", [512], F)
 _sb("dvO", [112, 3], F)
-_sb("Ug", [4, 1280], F)
-_sb("Ul", [4, 512], F)
-_sb("lev", [512], B)
-_sb("un2", [32], F)
-_sb("b16a", [2, 640], U16)
+_sb("Ug", [10240], F)
+_sb("un", [32], F)
 _sb("Omin Omax", [1280], F)
-_sb("Zp", [4, 8, 240], B)
+_sb("Zp", [8, 8, 240], B)
 _sb("OL", [5, 8, 240], B)
 _sb("Cq", [3, 143], B)
 _sb("pid", [4], I)
 _sb("col", [16], F)
 _sb("rows", [3, 128], F)
-_sb("cf", [2, 128], F)
+_sb("cf", [8, 128], F)
 _sb("cb", [8, 128], B)
 _sb("M16", [16], F)
 _sb("cm aBf", [8], F)
-_sb("aB cW", [8], B)
+_sb("cW", [8], B)
 _sb("Rq", [16, 128], B)
 _sb("Dq Dg", [144], B)
 _sb("wpad", [240], B)
@@ -68,22 +73,28 @@ _sb("selP", [8, 128], B)
 _sb("xr1 ring volN nA", [112], B)
 _sb("x16r qtab", [96], B)
 _sb("xtab", [3, 112], B)
-_sb("qu qa qq hh thr1 ta", [112], F)
+_sb("qu qa hh thr1", [112], F)
 _sb("lane biasL dump thr", [40], F)
 _sb("smallR", [96], B)
 _sb("junk", [8, 96], B)
 _sb("Cc", [96], F)
 _sb("Pw", [104], F)
-_sb("acc mm bo1 bo2", [8], F)
+_sb("acc bo2 ka kb", [8], F)
+_sb("bo", [56], F)
+_sb("dig", [3, 56], F)
+_sb("ring16", [112], B)
+_sb("q16", [16], B)
+_sb("mm", [32], F)
+_sb("row", [2, 512], B)
 _sb("xr", [16], B)
 _sb("x16", [8], U16)
-_sb("cmpb XE ag", [128], B)
+_sb("cmpb XE", [128], B)
+_sb("raw", [128], F)
 _sb("b16", [2, 5, 128], U16)
 _sb("bn wZ Mm Dd De Rlo Rhi", [128], F)
 _sb("A2", [256], F)
 _sb("KS", [256], F)
 _sb("SC MK rmask hold", [128], F)
-_sb("ka kb", [8], F)
 _sb("Bc", [5, 128], F)
 _sb("Vg", [2048], B)
 _sb("eq", [4, 128], B)
@@ -100,8 +111,7 @@ _sb("ev", [2, 8], B)
 _sb("nS thB", [32], F)
 _sb("EQ", [8, 512], B)
 _sb("Wb", [512], B)
-_sb("um", [256], F)
-_sb("prod est ec", [640], F)
+_sb("um prod ec", [640], F)
 _sb("Ss tg", [4, 128], F)
 _sb("z16", [2, 8], U16)
 _sb("nR", [RO, 32], F)
@@ -117,6 +127,93 @@ CY = 0.83e-3 * 1.05
 PCY = 0.42e-3 * 1.05
 GA, SCA = 1.56, 3.5
 PLAN = {}
+
+
+def polish(ops, order, eng, lat_x, lat_s):
+    n = len(ops)
+    eng, order, seed = list(eng), list(order), [1]
+    hard = [sorted(o["deps"] | o["war"]) for o in ops]
+    pred = [set(hard[i]) | o["order"] for i, o in enumerate(ops)]
+    succ = [[] for _ in ops]
+    for i in range(n):
+        for p in sorted(pred[i]):
+            succ[p].append(i)
+    dur = [o["alt"][e][0] for o, e in zip(ops, eng)]
+    hold = [d if o["k"] == "c" else (0.0 if e == "ext" else (0.1 if o["k"] == "dma" else 0.5)) for o, e, d in zip(ops, eng, dur)]
+
+    def waits(i):
+        return [(p, lat_s if eng[p] == eng[i] and ops[p]["k"] == "c" else lat_x) for p in hard[i]]
+    lat = [waits(i) for i in range(n)]
+
+    def draw():
+        seed[0] = (seed[0] * 1103515245 + 12345) % 2 ** 31
+        return seed[0] / 2.0 ** 31
+
+    def run(seq):
+        fin, st, why, free, last = [0.0] * n, [0.0] * n, [-1] * n, {}, {}
+        for i in seq:
+            e = eng[i]
+            s, w = free.get(e, 0.0), last.get(e, -1)
+            for p, x in lat[i]:
+                x += fin[p]
+                if x > s:
+                    s, w = x, -2 - p
+            st[i], fin[i], why[i] = s, s + dur[i], w
+            if e != "ext":
+                free[e], last[e] = s + hold[i], i
+        return max(fin), st, fin, why
+
+    def give(i, e):
+        eng[i] = e
+        dur[i] = hold[i] = ops[i]["alt"][e][0]
+        for y in [i] + succ[i]:
+            lat[y] = waits(y)
+
+    cur, st, fin, why = run(order)
+    best = (cur, fin, list(order), list(eng))
+    for _ in range(CFG["polish"]):
+        order.sort(key=lambda i: st[i])
+        pos = [0] * n
+        for k, i in enumerate(order):
+            pos[i] = k
+        i, arcs = fin.index(cur), []
+        while why[i] != -1:
+            if why[i] >= 0:
+                arcs.append((why[i], i))
+            i = why[i] if why[i] >= 0 else -2 - why[i]
+        new, flip = None, None
+        for _try in range(30):
+            k = int(draw() * len(arcs))
+            (u, x), r = arcs[k], draw()
+            if r < 0.08:
+                flip = u if len(ops[u]["alt"]) > 1 else (x if len(ops[x]["alt"]) > 1 else None)
+            elif r < 0.54:
+                while k + 1 < len(arcs) and arcs[k + 1][1] == u and draw() < 0.7:
+                    k += 1
+                    u = arcs[k][0]
+                if all(pos[p] < pos[u] for p in pred[x]):
+                    new = order[:pos[u]] + [x] + order[pos[u]:pos[x]] + order[pos[x] + 1:]
+            else:
+                while k > 0 and arcs[k - 1][0] == x and draw() < 0.7:
+                    k -= 1
+                    x = arcs[k][1]
+                if all(pos[s] > pos[x] for s in succ[u]):
+                    new = order[:pos[u]] + order[pos[u] + 1:pos[x] + 1] + [u] + order[pos[x] + 1:]
+            if new is not None or flip is not None:
+                break
+        if flip is not None:
+            old, new = eng[flip], order
+            give(flip, [e for e in ops[flip]["alt"] if e != old][0])
+        if new is None:
+            continue
+        c, s2, f2, w2 = run(new)
+        if c <= cur + CFG["heat"] * draw() ** 3:
+            cur, st, fin, why, order = c, s2, f2, w2, list(new)
+            if c < best[0]:
+                best = (c, fin, list(new), list(eng))
+        elif flip is not None:
+            give(flip, old)
+    return best
 
 
 def rank_program(g, core, T, topo):
@@ -177,7 +274,7 @@ def rank_program(g, core, T, topo):
                     if eng == "tensor" and ops[o]["e"] == eng:
                         order_only.add(o)
                     else:
-                        (soft if wr and kind == "c" and ops[o]["k"] == "c" else deps).add(o)
+                        (soft if not w2 and kind == "c" and ops[o]["k"] == "c" else deps).add(o)
         for (name, m), wr in acc:
             lst = log.setdefault(name, [])
             if wr:
@@ -186,8 +283,12 @@ def rank_program(g, core, T, topo):
         if extra is not None:
             deps.add(extra)
         ops.append({"e": eng, "d": dur, "alt": {eng: (dur, fn)}, "deps": deps, "war": soft - deps, "order": order_only, "k": kind,
-                    "b": bias[0], "w": [x["r"][0][0] for x in writes if x["r"]]})
+                    "b": bias[0], "w": [x["r"][0][0] for x in writes if x["r"]],
+                    "g": 2 if any("x" in x for x in writes) else int(any(isinstance(x, dict) and "x" in x for x in reads))})
         return me
+
+    def part(name, t):
+        bias[0] = CFG[name][t]
 
     def a_(x):
         return x["ap"] if isinstance(x, dict) else x
@@ -268,6 +369,11 @@ def rank_program(g, core, T, topo):
         k = {"allow_small_or_imprecise_dtypes": True} if flt else {}
         op("pool", 0.13 + 2 * n * CY, lambda q: q.iota(o["ap"], pat, base, cmul, **k), [], [o])
 
+    def fill(o, val, n):
+        iota(o, [[0, n]], val, 0, n)
+        ops[-1]["lend"] = CFG["lendf"]
+        ops[-1]["alt"]["vector"] = (vd(n), lambda q: q.memset(o["ap"], float(val)))
+
     def asel(o, x, pat, f, fill, base, cmul, n):
         op("pool", 0.17 + 2 * n * CY, lambda q: q.affine_select(o["ap"], x["ap"], pat, f, fill, base, cmul), [x], [o])
 
@@ -323,57 +429,65 @@ def rank_program(g, core, T, topo):
     ts(shc, pc, 111.5, AL.is_gt, 1, -128.0, AL.mult)
     ts(shc, shc, pc, AL.add, 1, 16.0, AL.add)
     lrow, qrow, grow = v("rows", 0), v("rows", 1), v("rows", 2)
-    If, unsc = v("cf", 0), v("cf", 1)
-    Ib, bo, up, negI, shm, shmK, I16, kcr = [v("cb", k) for k in range(8)]
+    If = v("cf", 0)
+    Ib, bo, up, negI, shm, shmK, I16, top = [v("cb", k) for k in range(8)]
     bo8 = v("cb", 1, S_(0, 128, 16))
     I8 = v("cb", 0, S_(0, 128, 16))
     ts(bo, grow, gc, AL.is_equal, 128)
-    ts(v("bn"), qrow, qc, AL.is_lt, 128)
-    tt(up, v("bn"), bo, AL.mult, 256)
+    ts(v("cmpb"), qrow, qc, AL.is_lt, 128)
+    tt(up, v("cmpb"), bo, AL.mult, 256)
     ts(v("lane"), v("lane"), qc, AL.add, 40)
     ts(v("biasL"), v("lane"), -1.0, AL.mult, 40, -0.5, AL.add)
     ts(If, lrow, pc, AL.is_equal, 128)
     ts(Ib, lrow, pc, AL.is_equal, 128)
-    ts(I16, lrow, pc, AL.is_equal, 128, 16.0, AL.mult)
-    ts(negI, lrow, pc, AL.is_equal, 128, -16777216.0, AL.mult)
     ts(shm, lrow, shc, AL.is_equal, 128)
-    ts(shmK, lrow, shc, AL.is_equal, 128, 4096.0, AL.mult)
-    ts(kcr, qrow, -4096.0, AL.mult, 128, 65536.0, AL.add)
+    negf, Iup, Idown = v("cf", 6), v("cf", 1), v("cf", 7)
+    for o, x, k in [(I16, Ib, 16.0), (negI, Ib, -2.0 ** 24), (shmK, shm, 4096.0), (negf, If, -1.0), (Iup, If, 2.0 ** 16),
+                    (Idown, If, -2.0 ** 20)] + [(v("cf", 1 + s), If, s / 8.0) for s in range(1, 5)]:
+        act(o, x, 128, scale=k)
+    iota(top, [[0, 8], [-4096, 16]], int(TOP), 0, 128)
+    fill(c("ne", 0, 8), 1, 8)
     ts(v("M16"), v("rows", 0, S_(0, 16)), qc, AL.is_equal, 16)
     ts(v("cm"), v("rows", 0, S_(0, 8)), gc, AL.is_equal, 8)
-    ms(v("cW"), -float(W), 8)
-    ms(c("Pw", 96, 104), 1e6, 8)
-    ms(v("A2"), 0.0, 256)
-    ms(v("hold"), 0.0, 128)
+    fill(v("cW"), -W, 8)
+    fill(c("Pw", 96, 104), 10 ** 6, 8)
+    fill(v("A2"), 0, 256)
+    fill(v("hold"), 0, 128)
     ts(v("rmask"), qrow, 0.5, AL.is_gt, 128)
     qmask = c("P0", 384, 512)
     ts(qmask, qrow, qc, AL.is_equal, 128)
     for q in range(16):
         act(v("Rq", q), bo, 128, scale=c("M16", q, q + 1))
-    ms(v("Dg"), 0.0, 72)
+    fill(v("Dg"), 0, 144)
     cp(c("Dg", 15, 143, 16), v("cm"), 8)
-    ms(v("Dq"), 0.0, 72)
+    fill(c("Dq", 0, 15), 0, 15)
     ts(c("Dq", 15, 143), Ib, c("M16", 0, 1), AL.mult, 64)
     for t in range(RO):
         x0 = (STEP * t) % V // 16
-        ts(v("xtab", t, S_(0, 96 - x0)), v("rows", 0, S_(0, 96 - x0)), float(x0), AL.add, 96)
+        iota(v("xtab", t, S_(0, 96 - x0)), [[1, 96 - x0]], x0, 0, 96 - x0)
         if x0:
-            cp(v("xtab", t, S_(96 - x0, 96)), v("rows", 0, S_(0, x0)), 96)
-        ms(v("xtab", t, S_(96, 112)), 0.0, 16)
-    ts(v("xr1"), v("rows", 0, S_(0, 112)), 1.0, AL.add, 112)
-    cp(c("ring", 0, 8), c("xr1", 96, 104), 8)
-    cp(c("ring", 8, 104), c("xr1", 0, 96), 48)
-    cp(c("ring", 104, 112), c("xr1", 104, 112), 8)
+            iota(v("xtab", t, S_(96 - x0, 96)), [[1, x0]], 0, 0, x0)
+        fill(v("xtab", t, S_(96, 112)), 0, 16)
+    iota(v("xr1"), [[1, 112]], 1, 0, 112)
+    for name, k in (("ring", 1), ("ring16", 16)):
+        for a, b, x in ((0, 8, 97), (8, 104, 1), (104, 112, 105)):
+            iota(c(name, a, b), [[k, b - a]], k * x, 0, b - a)
+    iota(v("q16"), [[1, 16]], -16, 0, 16)
+    fill(v("dig", 1), 1, 56)
+    fill(v("dig", 1, S_(0, 56, 7)), 0, 8)
+    fill(v("dig", 1, S_(3, 56, 7)), -1, 8)
+    for x, val in ((1, BIG), (2, -BIG), (4, -7.5), (5, BIG / 256), (6, 16 - BIG / 256)):
+        ms(v("dig", 0, S_(x, 56, 7)), val, 8)
     for q in range(16):
         act(c("Gt", q, W, 16), v("xr1"), 112, scale=c("M16", q, q + 1))
-    ms(c("Gt", W, W + 16), 0.0, 16)
-    ms(c("volE", W, W + 16), 0.0, 16)
-    ms(c("Wf", W, W + 8), 0.0, 8)
-    ms(c("wall", 0, 8), 1.0, 8)
-    ms(c("S", W, 1920), 0.0, 128)
-    ms(v("Z0"), 0.0, 256)
-    ts(v("x16r"), v("rows", 0, S_(0, 96)), 16.0, AL.mult, 96)
-    ts(v("qtab"), v("rows", 0, S_(0, 96)), 0.0, AL.mult, 96, qc, AL.add)
+    fill(c("Gt", W, W + 16), 0, 16)
+    fill(c("volE", W, W + 16), 0, 16)
+    fill(c("Wf", W, W + 8), 0, 8)
+    fill(c("wall", 0, 8), 1, 8)
+    fill(c("S", W, 1920), 0, 128)
+    fill(v("Z0"), 0, 256)
+    iota(v("x16r"), [[16, 96]], 0, 0, 96)
+    act(v("qtab"), v("rows", 0, S_(0, 96)), 96, AF.Identity, bias=qc, scale=0.0)
     ts(v("dump"), v("lane"), float(W), AL.add, 40)
     ln2 = math.log(2.0)
     ts(c("col", 8, 9), qc, 7 * ln2, AL.mult, 1, -52 * ln2, AL.add)
@@ -381,46 +495,44 @@ def rank_program(g, core, T, topo):
     act(c("col", 4, 6), c("col", 8, 10), 2, AF.Exp)
     ts(v("t40"), v("lane"), -ln2, AL.mult, 40, 63 * ln2 + math.log(2.5), AL.add)
     act(v("thr"), v("t40"), 40, AF.Exp)
-    ts(v("aB"), v("cm"), alc, AL.mult, 8)
-    cp(v("aBf"), v("aB"), 8)
+    ts(c("hcm", 8, 16), v("cm"), alc, AL.mult, 8)
+    cp(v("aBf"), c("hcm", 8, 16), 8)
     cp(c("hcm", 0, 8), v("cm"), 8)
-    cp(c("hcm", 8, 16), v("aB"), 8)
     for k in range(8):
         act(v("selP", k), lrow, 128, AF.Identity, bias=c("aBf", k, k + 1), scale=0.0)
-    ms(v("wpad"), 0.0, 120)
+    fill(v("wpad"), 0, 240)
     ts(c("wpad", 112, 128), v("M16"), 0.0, AL.mult, 16, wc, AL.add)
-    for s in range(8):
-        ms(v("cf", 1, S_(s, 128, 8)), 256.0 ** s, 16)
-        ms(c("lev", 16 * s, 16 * s + 16), 256.0 ** -s, 16)
-    cp(c("lev", 128, 256), c("lev", 0, 128), 64)
-    cp(c("lev", 256, 512), c("lev", 0, 256), 128)
-    for s in range(2):
-        ms(c("un2", s, 32, 2), 256.0 ** s, 16)
+    iota(v("un"), [[0, 16], [255, 2]], 1, 0, 32)
     bias[0] = -100.0
-    for name, n in (("OL", 5), ("Zp", 4)):
+    for name, n in (("OL", 5), ("Zp", 8)):
         for k in range(n):
             for h in range(8):
                 iota(v(name, k, h), [[0, 240]], 0, 0, 240)
     bias[0] = 0.0
 
-    for a in (0, 768):
-        x = c("VD", a, a + 768, p=p32)
-        cp(c("Vg", a, a + 768, p=p32), {"ap": x["ap"], "r": x["r"] + [("VDx", 1)]}, 768)
+    def both(x):
+        return {"ap": x["ap"], "r": x["r"] + [("VDx", 1), ("VDy", 1)]}
+    for a in (0, 1408):
+        for p in (S_(32, 64), S_(64, 128)):
+            ms({"ap": c("VD", a, a + 128, p=p)["ap"], "r": [("VDy", 1)]}, 0, 128)
+    exchange([(both(c("VD", 0, 128)), c("VD", 1664, W))], [(both(c("VD", 1408, V)), c("VD", V, 1664))], 4.0)
+    for a, b in ((0, 768), (768, V), (V, W)):
+        cp(c("Vg", a, b, p=p32), both(c("VD", a, b, p=p32)), b - a)
     for t in range(RO):
         bank = "P%d" % (3 + t)
         mm(grp(c(bank, 0, 96), [(v("Cq", t, S_(15 - q, 143 - q), p=p32), c("Vg", q, V, 16, p=p32), 96) for q in range(16)]))
         cp(v("dvO", S_(8, 104), t), c(bank, 0, 96), 96)
-    exchange([(v("dvO", S_(8, 16)), v("dvO", S_(104, 112)))], [(v("dvO", S_(96, 104)), v("dvO", S_(0, 8)))], 4.0)
+    for t in range(RO):
+        bank = "P%d" % (3 + t)
+        mm(grp(c(bank, 96, 112), [(v("Cq", t, S_(15 - q, 143 - q), p=p32), c("Vg", V + q, W, 16, p=p32), 64) for q in range(16)]))
+        cp(v("dvO", S_(0, 8), t), c(bank, 96, 104), 8)
+        cp(v("dvO", S_(104, 112), t), c(bank, 104, 112), 8)
     exchange([(c("Wf", 0, 128), c("Wf", 1664, W))], [(c("Wf", 1408, V), c("Wf", V, 1664))], 2.5)
     def scaled(a, b):
         act(c("Wf", UB + a, UB + b), c("Wf", a, b), b - a, scale=1.0 / 256)
     for a, b in ((0, 512), (512, 1024), (1024, V), (V, W)):
         scaled(a, b)
     exchange([(c("wall", 0, WT), c("wall", 2 * WT, 3 * WT))], [(c("wall", 0, WT), c("wall", WT, 2 * WT))], 2.5)
-    for h in range(4):
-        ts(c("VD", 448 * h, 448 * h + 448), c("ntb", 448 * h, 448 * h + 448), 15, AL.bitwise_and, 448)
-        act_src = c("VD", 448 * h, 448 * h + 448)
-        ts(c("At", 448 * h, 448 * h + 448), act_src, 65536.0, AL.mult, 448)
 
     inner, left, right = (16, 96), (0, 16), (96, 112)
 
@@ -463,29 +575,28 @@ def rank_program(g, core, T, topo):
                [(c("Dg", 15 - q, 143 - q), c("cmpb", q, 128, 16), 64) for q in range(16)]) +
            grp(c("P0", 232, 240), [(v("cmpb"), bo8, 64), (v("XE"), bo8, 64)]))
         ts(v("o16", e, S_(0, 8)), c("P0", 224, 232), float(W), AL.add, 8)
-        cp(v("nW", e, S_(0, 8)), c("P0", 224, 232), 8)
         cp(c("hold", 0, 128, 16), c("P0", 232, 240), 8)
         scan(v("Bc", 0), v("rmask"), v("hold"), 0.0, AL.mult, AL.add, 128)
-        ts(v("mm"), c("lane", 0, 8), c("Cc", 95, 96), AL.is_lt, 8)
+        ts(v("mm"), c("lane", 0, 32), c("Cc", 95, 96), AL.is_lt, 32)
         if t:
             for (a, b), x in ((left, 0), (right, 16)):
                 ts(c("hh", a, b), v("nF", t - 1, S_(a, b)), 3.0, AL.min, 16)
                 tt(c("qu", a, b), c("qa", a, b), c("hh", a, b), AL.subtract, 32)
         else:
             ts(c("volN", 16, 96), qv(16, 96), 1.0, AL.max, 80, 16.0, AL.min)
-            inner_volumes()
+            inner_volumes(("P6", "P7", "P6"))
         for a, b in (left, right):
             ts(c("volN", a, b), qv(a, b), 1.0, AL.max, 16, 16.0, AL.min)
         spread_volumes(0, 16, "P1", [])
         spread_volumes(96, 112, "P1", [(0, V, 128), (128, 0, 128), (256, 1408, 128), (384, 1664, 128)], 256)
         if not last:
             tt(v("qa"), v("volN"), v("dvO", ALL, t + 1), AL.add, 224)
-            ts(v("ta"), v("qa"), 10.5, AL.is_gt, 112, 1000.0, AL.mult)
-            ts(v("qq"), v("qa"), -7.5, AL.add, 112)
-            tt(v("thr1"), v("qq"), v("ta"), AL.add, 224)
+            ts(c("P2", 112, 224), v("qa"), -10.5, AL.add, 112, 1000.0, AL.mult)
+            ts(v("thr1"), v("qa"), -7.5, AL.add, 112)
+            tt(v("thr1"), c("P2", 112, 224), v("thr1"), AL.max, 112)
 
-    def inner_volumes():
-        for (a, b), bank in zip(((16, 40), (40, 72), (72, 96)), CFG["vbank"]):
+    def inner_volumes(banks_=CFG["vbank"]):
+        for (a, b), bank in zip(((16, 48), (48, 72), (72, 96)), banks_):
             spread_volumes(a, b, bank, [(0, 16 * a - 128, 16 * (b - a))])
 
     def lists(t):
@@ -495,12 +606,13 @@ def rank_program(g, core, T, topo):
         sl = lambda name, a, b: v(name, e, S_(8 * a, 8 * b))
         Gj = lambda a, b: v("G", e, S_(128 * a, 128 * b))
         vol = lambda a, b: v("volM", e, S_(128 * a, 128 * b))
+        bo = lambda k: c("bo", 8 * k, 8 * k + 8)
 
         def names(j):
             ts(v("b16", e, j), ind(v("ntb"), sl("o16", j, j + 1)), 0.0625, AL.mult, 128, -0.46875, AL.add)
-            nj = 4 if CFG["late"][t] else 5
-            for s in range(2 if j < nj else 0):
-                ts(v("b16a", e, S_(nj * s + j, 128 * nj, 2 * nj)), v("b16", e, j, S_(s, 128, 2)), float(s * UB), AL.add, 32)
+
+        def level(j):
+            ts(v("b16", e, j, S_(1, 128, 2)), v("b16", e, j, S_(1, 128, 2)), float(UB), AL.add, 32)
 
         def present(a, b):
             tt(c("t40", 8 * a, 8 * b), sl("nW", a, b), sl("th", a, b), AL.mult, 16 * (b - a))
@@ -509,6 +621,8 @@ def rank_program(g, core, T, topo):
             act(vol(a, b), ind(v("volE"), sl("nA16", a, b)), 128 * (b - a))
             mm([(c("P2", 440 + 16 * (j - a), 456 + 16 * (j - a)), Gj(j, j + 1), v("hcm"), True, True, 64) for j in range(a, b)])
             cp(v("hc", S_(a, b)), c("P2", 440, 440 + 16 * (b - a)), 48)
+            if a == 4 and CFG["fast"][t]:
+                return
             mm([(c("P1", 128 * (j - a + 1), 128 * (j - a + 2)), Gj(j, j + 1), Ib, True, True, 128) for j in range(a, b)])
             act(v("OL", S_(a, b), ALL, mid), c("P1", 128, 128 * (b - a + 1)), 128 * (b - a), AF.Sign)
             for k in range(8):
@@ -522,35 +636,43 @@ def rank_program(g, core, T, topo):
         def equal(a, b):
             n = 128 * (b - a)
             per = 512 // n
-            tt(sl("pre", a, b), sl("nW", a, b), c("lane", 8 * a, 8 * b), AL.subtract, 16 * (b - a))
+            a0 = 0 if a == 1 else a
+            tt(sl("pre", a0, b), sl("nW", a0, b), c("lane", 8 * a0, 8 * b), AL.subtract, 16 * (b - a0))
             tt(sl("thm", a, b), sl("th", a, b), c("thr", 8 * a, 8 * b), AL.mult, 16 * (b - a))
             for k0 in range(0, 8, per):
                 bank = "P%d" % (3 + (k0 // per) % 2)
                 mm([(c(bank, n * (k - k0), n * (k - k0 + 1)), v("selP", k), Gj(a, b), True, True, n) for k in range(k0, k0 + per)])
+                short = k0 < CFG["short"][t][a == 4]
+                if short:
+                    act(v("row", (k0 // per) % 2, S_(0, n * per)), c(bank, 0, n * per), n * per)
                 for k in range(k0, k0 + per):
                     for j in range(a, b):
                         x = n * (k - k0) + 128 * (j - a)
-                        ts(v(EQ, k, S_(128 * j - 128, 128 * j)), c(bank, x, x + 128), v("hc", j, S_(8 + k, 9 + k)), AL.is_equal, 128)
+                        src = v("row", (k0 // per) % 2, S_(x, x + 128)) if short else c(bank, x, x + 128)
+                        ts(v(EQ, k, S_(128 * j - 128, 128 * j)), src, v("hc", j, S_(8 + k, 9 + k)), AL.is_equal, 64 if short else 128)
             mm(grp(c("P3", 0, n), [(c("wpad", 112 - 16 * k, 240 - 16 * k), v(EQ, k, S_(128 * a - 128, 128 * b - 128)), n) for k in range(8)]))
             act(c("Wb", 128 * a - 128, 128 * b - 128), c("P3", 0, n), n)
             mm(grp(c("P4", 0, 8 * (b - a)), [(c("Dq", 15 - q, 143 - q), c("Wb", 128 * a - 128 + q, 128 * b - 128, 16), 64) for q in range(16)]))
-            f = c("ff", 8 * a, 8 * b)
-            tt(f, c("P4", 0, 8 * (b - a)), sl("thm", a, b), AL.is_lt, 32)
-            tt(f, f, sl("pre", a, b), AL.mult, 64)
-            tt(f, f, c("dump", 8 * a, 8 * b), AL.add, 64)
-            cp(sl("off16", a, b), f, 32)
+            tt(c("ff", 8 * a, 8 * b), c("P4", 0, 8 * (b - a)), sl("thm", a, b), AL.is_lt, 32)
+            if a0 < a:
+                cp(c("ff", 0, 8), sl("th", 0, 1), 8)
+            f = c("ff", 8 * a0, 8 * b)
+            tt(f, f, sl("pre", a0, b), AL.mult, 64)
+            tt(f, f, c("dump", 8 * a0, 8 * b), AL.add, 64)
+            cp(sl("off16", a0, b), f, 32)
 
         names(0)
         for j in range(1, 5):
             off = sl("o16", j - 1, j)
-            act(v("ag"), ind(v("At"), off), 128)
+            act(v("raw"), ind(v("ntb"), off), 128)
+            cp(v("bn"), v("b16", e, j - 1), 128)
             cuts = CFG["split"][t]
             for a, b in zip(cuts, cuts[1:]):
                 either(c("Vg", 16 * a, 16 * b), ind(v("volE"), v("b16", e, j - 1, S_(a, b))), 16 * (b - a), lend=CFG["lendv"][t])
-            cp(v("bn"), v("b16", e, j - 1), 128)
+            level(j - 1)
             mm([(c("P0", 0, 128), v("bn"), If, True, True, 512)])
-            mm([(c("P1", 0, 128), v("ag"), Ib, True, True, 128)])
-            rest = grp(c("P0", 129, 384, 2), [(v("bn"), If, 512), (Ib, kcr, 128)] + [(negI, v("eq", i), 128) for i in range(j)])
+            mm(grp(c("P1", 0, 128), [(v("raw"), Iup, 512), (v("bn"), Idown, 512)]))
+            rest = grp(c("P0", 129, 384, 2), [(v("bn"), If, 512), (Ib, top, 128)] + [(negI, v("eq", i), 128) for i in range(j)])
             mm(rest[:2])
             for i in range(j):
                 tt(v("eq", i), c("P0", 0, 128), v("Bc", i), AL.is_equal, 128)
@@ -558,47 +680,71 @@ def rank_program(g, core, T, topo):
             mm(rest[2:])
             held = v("Bc", j - 1, S_(0, 128, 16))
             if j == 4:
-                mm(grp(c("P2", 224, 232), [(vol(i, i + 1), I8, 64) for i in range(4)]))
-                ts(v("bo1"), c("P2", 224, 232), 43.5, AL.is_gt, 8, 4095.0 * 4096, AL.mult)
-                ts(v("bo2"), c("P2", 224, 232), 0.5, AL.is_lt, 8, 4095.0 * 4096, AL.mult)
-                tt(v("bo1"), v("bo1"), held, AL.add, 16)
-                tt(v("bo2"), v("bo1"), v("bo2"), AL.add, 16)
-                held = v("bo2")
-            mm([(c("P0", 128 + 2 * k, 384, 32), c("Vg", k, 2048, 16), I8, True, True, 64) for k in range(16)])
+                act(v("XE"), ind(v("volE"), off), 128)
+                mm(grp(c("P2", 224, 232), [(vol(i, i + 1), I8, 64) for i in range(3)] + [(v("XE"), I8, 64)]) +
+                   [(c("P2", 232, 240), vol(0, 1), I8, True, True, 64)])
+                ts(bo(0), c("P2", 232, 240), 0.5, AL.is_lt, 8, 4095.0 * 4096, AL.mult)
+                ts(bo(1), c("P2", 224, 232), 43.5, AL.is_gt, 8, 4095.0 * 4096, AL.mult)
+                tt(bo(2), bo(0), bo(1), AL.add, 16)
+                tt(bo(4), bo(2), held, AL.add, 16)
+                if CFG["fast"][t]:
+                    ts(bo(3), bo(2), 4095.5, AL.add, 8)
+            cuts = CFG["batch"][t]
+            part("marks", t)
+            if j in cuts:
+                a = cuts[cuts.index(j) - 1]
+                if a < 3:
+                    ts(sl("nW", a, min(j, 3)), sl("o16", a, min(j, 3)), -float(W), AL.add, 24)
+                tt(c("ne", 8 * max(a, 1), 8 * j), sl("nW", max(a, 1), j), sl("nW", max(a, 1) - 1, j - 1), AL.not_equal, 32)
+                tt(sl("th", a, j), c("ne", 8 * a, 8 * j), c("mm", 8 * a, 8 * j), AL.mult, 48)
+                present(a, j)
+            if j - 1 in CFG["ebatch"][t][1:]:
+                ecuts = CFG["ebatch"][t]
+                part("equal", t)
+                equal(ecuts[ecuts.index(j - 1) - 1], j - 1)
+            part("steps", t)
+            if j == 4:
+                held = bo(4)
+            w = CFG["turn"]
+            for a in range(0, 128, w):
+                mm([(c("P0", 128 + 2 * k, 384, 32, p=S_(a, a + w)), c("Vg", 16 * a + k, 16 * (a + w), 16), I8, True, True, min(w, 64))
+                    for k in range(16)])
             scan(v("KS"), v("A2"), c("P0", 128, 384), 0.0, AL.mult, AL.add, 256)
             scan(v("SC"), v("rmask"), c("KS", 1, 256, 2), 0.0, AL.mult, AL.max, 128)
-            tt(v("ka"), c("SC", 15, 128, 16), held, AL.max, 16)
-            ts(v("kb"), v("ka") if j == 4 else c("SC", 15, 128, 16), BIG, AL.add, 8, -BIG, AL.add)
-            tt(c("hold", 0, 128, 16), v("ka"), v("kb"), AL.subtract, 16)
+            ka = v("ka")
+            tt(ka, c("SC", 15, 128, 16), held, AL.max, 16)
+            ts(v("kb"), ka if j == 4 else c("SC", 15, 128, 16), BIG, AL.add, 8, -BIG, AL.add)
+            tt(c("hold", 0, 128, 16), ka, v("kb"), AL.subtract, 16)
+            if j == 4 and CFG["fast"][t]:
+                for x in (0, 3):
+                    tt(v("dig", 0, S_(x, 56, 7)), c("SC", 15, 128, 16), held, AL.max, 16)
+                tt(bo(5), c("SC", 15, 128, 16), bo(3), AL.is_gt, 16)
+                scan(v("dig", 2), v("dig", 1), v("dig", 0), 0.0, AL.mult, AL.add, 56)
+                tt(bo(6), v("dig", 2, S_(3, 56, 7)), v("dig", 2, S_(6, 56, 7)), AL.subtract, 16)
+                for k in range(8):
+                    ts(v("OH", 5 * k + 4), v("ring16"), v("dig", 2, S_(7 * k + 6, 7 * k + 7)), AL.is_equal, 56)
+                for k in range(8):
+                    ts(v("OL", 4, k, mid), v("q16"), c("bo", 48 + k, 49 + k), AL.is_equal, 16, c("bo", 40 + k, 41 + k), AL.mult)
             scan(v("Bc", j), v("rmask"), v("hold"), 0.0, AL.mult, AL.add, 128)
             tt(v("MK"), qmask, v("Bc", j), AL.mult, 128)
             mm(grp(c("P0", 0, 8), [(Ib, v("cW"), 64), (v("MK"), v("cm"), 256)]))
             ts(sl("o16", j, j + 1), c("P0", 0, 8), float(W), AL.add, 8)
             if j == 4:
                 tt(sl("th", 4, 5), c("P0", 0, 8), sl("nW", 3, 4), AL.not_equal, 8)
-            cp(sl("nW", j, j + 1), c("P0", 0, 8), 8)
+            if j > 2:
+                cp(sl("nW", j, j + 1), c("P0", 0, 8), 8)
             names(j)
-            if j == 2:
-                cp(sl("th", 0, 1), v("mm"), 8)
-                tt(c("ne", 8, 24), sl("nW", 1, 3), sl("nW", 0, 2), AL.not_equal, 32)
-                for i in (1, 2):
-                    tt(sl("th", i, i + 1), c("ne", 8 * i, 8 * i + 8), v("mm"), AL.mult, 16)
-                present(0, 3)
-                tt(c("ff", 0, 8), sl("nW", 0, 1), c("lane", 0, 8), AL.subtract, 16)
-                tt(c("ff", 0, 8), c("ff", 0, 8), v("mm"), AL.mult, 16)
-                tt(c("ff", 0, 8), c("ff", 0, 8), c("dump", 0, 8), AL.add, 16)
-                cp(sl("off16", 0, 1), c("ff", 0, 8), 8)
-            if j == 3:
-                tt(c("ne", 24, 32), sl("nW", 3, 4), sl("nW", 2, 3), AL.not_equal, 16)
-                tt(sl("th", 3, 4), c("ne", 24, 32), v("mm"), AL.mult, 16)
-                present(3, 4)
+        level(4)
         mm(grp(c("P2", 0, 112), tally(0, 4)))
         cp(v("nA"), c("P2", 0, 112), 112)
         tt(c("es", 0, 8), sl("th", 1, 2), sl("th", 2, 3), AL.add, 16)
         tt(c("es", 0, 8), c("es", 0, 8), sl("th", 3, 4), AL.add, 16)
         ts(c("es", 0, 8), c("es", 0, 8), 0.0625, AL.mult, 8)
-        equal(1, 4)
-        present(4, 5)
+        part("equal", t)
+        equal(CFG["ebatch"][t][-2], 4)
+        part("counts", t)
+        if not CFG["fast"][t]:
+            present(4, 5)
         mm(grp(c("P2", 0, 112), [(Ib, v("nA"), 112)] + tally(4, 5)))
         cp(c("nS", 0, 16), c("P2", 0, 16), 16)
         cp(c("nS", 16, 32), c("P2", 96, 112), 16)
@@ -612,13 +758,13 @@ def rank_program(g, core, T, topo):
             tt(c("thB", 16, 24), c("thr1", 96, 104), c("nS", 16, 24), AL.subtract, 16)
             ts(c("hh", 16, 96), c("P2", 16, 96), 3.0, AL.min, 80)
             tt(c("qu", 16, 96), c("qa", 16, 96), c("hh", 16, 96), AL.subtract, 160)
-        mm(grp(c("P2", 184, 224), [(c("Dq", 15 - q, 143 - q), v("volM", e, S_(q, 640, 16)), 64) for q in range(16)]))
-        cp(v("Zq"), c("P2", 184, 224), 40)
-        mm(grp(c("P2", 112, 120), [(Ib, c("Zq", 8 * i, 8 * i + 8), 64) for i in range(5)]))
-        ts(v("z16", e), c("P2", 112, 120), 7.0, AL.add, 8)
+        if CFG["fast"][t]:
+            present(4, 5)
         ts(c("es", 8, 16), sl("th", 4, 5), 0.0625, AL.mult, 8)
         tt(v("ev", e), c("es", 0, 8), c("es", 8, 16), AL.add, 16)
+        part("equal", t)
         equal(4, 5)
+        part("counts", t)
         if not last:
             ts(c("volN", 16, 96), c("qu", 16, 96), 1.0, AL.max, 80, 16.0, AL.min)
             inner_volumes()
@@ -656,61 +802,65 @@ def rank_program(g, core, T, topo):
         dma("sync", c("S", V, W), v("Z0"), 3.0)
         for a, b in ((8, 48), (48, 88), (0, 8), (88, 96)):
             act(c("S", 16 * a, 16 * b), ind(uw, v("sel", e, S_(a, b))), 16 * (b - a))
-        act(c("um", 0, 128), ind(uw, sl("o16", 0, 1)), 128)
-        act(c("um", 128, 256), ind(uw, sl("o16", 4, 5)), 128)
-        act(v("wZ"), ind(c("wall", 0, WT), v("z16", e)), 128)
-        for a, b in ((0, 2), (2, 4), (4, 5)):
-            tt(c("prod", 128 * a, 128 * b), ind(uw, sl("o16", a, b)), v("volM", e, S_(128 * a, 128 * b)), AL.mult, 128 * (b - a))
+        part("mean", t)
+        act(c("um", 0, 512), ind(uw, sl("o16", 0, 4)), 512)
+        act(c("um", 512, 640), ind(uw, sl("o16", 4, 5)), 128)
+        mm(grp(c("P6", 256, 288), [(c("Dq", 15 - q, 143 - q), v("volM", e, S_(q, 512, 16)), 64) for q in range(16)]))
+        cp(c("Zq", 0, 32), c("P6", 256, 288), 32)
+        mm(grp(c("P6", 288, 296), [(Ib, c("Zq", 8 * i, 8 * i + 8), 64) for i in range(4)] +
+               [(c("Dq", 15 - q, 143 - q), v("volM", e, S_(512 + q, 640, 16)), 64) for q in range(16)]))
         mm([(c("P6", 128 + q, 256, 16), v("Rq", q), v("ev", e), True, True, 64) for q in range(16)])
+        ts(v("z16", e), c("P6", 288, 296), 7.0, AL.add, 8)
+        act(v("wZ"), ind(c("wall", 0, WT), v("z16", e)), 128)
+        mm([(v("P5"), Ib, v("volM", e, S_(0, 512)), True, True, 512)])
+        for a in (0, 256):
+            tt(c("prod", a, a + 256), c("P5", a, a + 256), c("um", a, a + 256), AL.mult, 256)
+        mm([(c("P7", 128, 256), Ib, v("volM", e, S_(512, 640)), True, True, 128)] +
+           grp(c("P7", 256, 384), [(negf, c("um", 0, 128), 512), (If, c("um", 512, 640), 512)]))
+        tt(c("prod", 512, 640), c("P7", 128, 256), c("um", 512, 640), AL.mult, 128)
+        act(v("Dd"), c("P7", 256, 384), 128)
         mm(grp(c("P7", 384, 512), [(If, c("prod", 128 * j, 128 * j + 128), 512) for j in range(5)]))
-        tt(v("Mm"), c("P7", 384, 512), v("wZ"), AL.mult, 128)
-        tt(v("Dd"), c("um", 128, 256), c("um", 0, 128), AL.subtract, 256)
         tt(v("De"), c("P6", 128, 256), v("Dd"), AL.mult, 128)
-        tt(c("est", 0, 128), v("Mm"), v("De"), AL.subtract, 256)
-        ts(c("P7", 256, 384), v("Dd"), 0.125, AL.mult, 128)
-        for j in range(1, 5):
-            tt(c("est", 128 * j, 128 * j + 128), c("P7", 256, 384), c("est", 128 * j - 128, 128 * j), AL.add, 128)
+        tt(v("Mm"), c("P7", 384, 512), v("wZ"), AL.mult, 128)
+        if CFG["est"]:
+            tt(v("Mm"), v("Mm"), v("De"), AL.subtract, 256)
+        for j in (1, 2, 0, 3, 4):
+            mm(grp(c("P5", 128 * j - 128, 128 * j) if j else c("P7", 0, 128),
+                   [(v("cf", 1 + j), v("Dd"), 512)] * (j > 0) + [(negf, v("De"), 512)] * (1 - CFG["est"]) + [(If, v("Mm"), 512)]))
         back = lambda a, b, s=1: S_(b - 1, a - 1 if a else None, -s)
 
-        def bound(src, row, a, n, o):
-            scan(c("Omin", o, o + n), v(src, row, S_(a, a + 2 * n, 2)), v(src, row, S_(a + 1, a + 2 * n, 2)), 1e29, AL.min, AL.min, n)
-            scan(v("Omax", back(o, o + n)), v(src, row, back(a, a + 2 * n - 1, 2)), v(src, row, back(a + 1, a + 2 * n, 2)),
-                 0.0, AL.max, AL.max, n)
+        def bound(a, n, o):
+            scan(c("Omin", o, o + n), c("Ug", a, a + 2 * n, 2), c("Ug", a + 1, a + 2 * n, 2), 1e29, AL.min, AL.min, n)
+            scan(v("Omax", back(o, o + n)), v("Ug", back(a, a + 2 * n - 1, 2)), v("Ug", back(a + 1, a + 2 * n, 2)), 0.0, AL.max, AL.max, n)
 
-        late = CFG["late"][t]
-        nj = 4 if late else 5
-        lo, hi = (("Rlo", 0), ("Rhi", 0)) if late else (("P7", 0), ("P7", 128))
-        for k in range(8):
-            for h in range(2):
-                x = ind(v("Wf"), v("b16a", e, S_(8 * nj * (2 * k + h), 8 * nj * (2 * k + h + 1))))
-                either(v("Ug", k % 4, S_(128 * nj * h, 128 * nj * (h + 1))), x, 128 * nj, lend=CFG["lend"][t])
-            for i in range(8):
-                bound("Ug", k % 4, 32 * nj * i, 16 * nj, 128 * nj * (k % 2) + 16 * nj * i)
-            if k % 2:
-                a = 16 * k - 16
-                tt(c(lo[0], lo[1] + a, lo[1] + a + 32), c("Omin", 8 * nj - 1, 256 * nj, 8 * nj), c("un2", 0, 32), AL.mult, 64)
-                tt(c(hi[0], hi[1] + a, hi[1] + a + 32), c("Omax", 0, 256 * nj, 8 * nj), c("un2", 0, 32), AL.mult, 64)
-        if late:
-            for k in range(4):
-                tt(v("Ul", k), ind(uw, v("b16", e, 4, S_(32 * k, 32 * k + 32))), v("lev"), AL.mult, 512)
-                for i in range(4):
-                    bound("Ul", k, 128 * i, 64, 256 * k + 64 * i)
-            tt(c("P7", 0, 128), c("Omin", 7, 1024, 8), unsc, AL.mult, 256)
-            tt(c("P7", 128, 256), c("Omax", 0, 1024, 8), unsc, AL.mult, 256)
-            tt(c("P7", 0, 128), c("P7", 0, 128), v("Rlo"), AL.min, 128)
-            tt(c("P7", 128, 256), c("P7", 128, 256), v("Rhi"), AL.max, 128)
-        sw = v("S")
+        part("bounds", t)
         for j in range(5):
+            cuts = CFG["per"][t] if j < 4 else CFG["per4"][t]
+            for a, b in zip(cuts, cuts[1:]):
+                x = ind(c("Wf", 0, UB + W), v("b16", e, j, S_(a, b)))
+                either(c("Ug", 80 * a + j, 80 * b, 5), x, 16 * (b - a), lend=CFG["lend"][t])
+        for i in range(0, 128, 2):
+            bound(80 * i, 80, 40 * (i % 32))
+            if i % 32 == 30:
+                tt(c("Rlo", i - 30, i + 2), c("Omin", 39, 1280, 40), v("un"), AL.mult, 64)
+                tt(c("Rhi", i - 30, i + 2), c("Omax", 0, 1280, 40), v("un"), AL.mult, 64)
+        part("sums", t)
+        sw = c("S", 0, 1920)
+        for j in (1, 2, 0, 3, 4):
             ej = c("ec", 128 * j, 128 * j + 128)
-            tt(c("prod", 128 * j, 128 * j + 128), c("P7", 0, 128), c("est", 128 * j, 128 * j + 128), AL.max, 128)
-            tt(ej, c("P7", 128, 256), c("prod", 128 * j, 128 * j + 128), AL.min, 128)
+            x = c("P5", 128 * j - 128, 128 * j) if j else c("P7", 0, 128)
+            tt(x, x, v("Rlo"), AL.max, 128)
+            tt(ej, x, v("Rhi"), AL.min, 128)
+        for pair, bank in (((1, 2), "P3"), ((3, 4), "P4")):
+            turned = lambda j: c(bank, 128 * (j % 2), 128 * (j % 2) + 128)
+            for j in pair:
+                mm([(turned(j), c("ec", 128 * j, 128 * j + 128), If, True, True, 512)])
+            for j in pair:
+                act(v("Zp", 2 * j - 2, ALL, mid), turned(j), 128)
+            for j in pair:
+                tt(v("Zp", 2 * j - 1, ALL, mid), turned(j), v("Zp", 2 * j - 2, ALL, mid), AL.subtract, 128)
         for j in range(1, 5):
-            mm([(c("P5", 128 * j - 128, 128 * j), c("ec", 128 * j, 128 * j + 128), If, True, True, 512)])
-        for j in range(1, 5):
-            zh, zl = 2 * (j % 2), 2 * (j % 2) + 1
-            turned, bank = c("P5", 128 * j - 128, 128 * j), "P%d" % (7 - j % 2)
-            act(v("Zp", zh, ALL, mid), turned, 128)
-            tt(v("Zp", zl, ALL, mid), turned, v("Zp", zh, ALL, mid), AL.subtract, 128)
+            zh, zl, bank = 2 * j - 2, 2 * j - 1, "P%d" % (7 - j % 2)
             mm(grp(c(bank, 0, 128), [(v("Zp", z, k, S_(112 - 16 * k, 240 - 16 * k)), v(EQ, k, S_(128 * j - 128, 128 * j)), 128)
                                      for z in (zh, zl) for k in range(8)]))
             act(v("Ss", j - 1), c(bank, 0, 128), 128)
@@ -729,22 +879,25 @@ def rank_program(g, core, T, topo):
                      [(c("S", 1664, W), c(Rb, 0, 128)), (c("S", 1408, V), c(Rb, 256, 384))], 3.0)
         end = 96 if last else 112
 
-        def weigh(a, b):
-            tt(c("Wf", 16 * a, 16 * b), ind(v("wall"), v("nOff", e, S_(a, b))), c("S", 16 * a, 16 * b), AL.mult, 16 * (b - a))
+        def weigh(a, b, src):
+            tt(c("Wf", 16 * a, 16 * b), ind(v("wall"), v("nOff", e, S_(a, b))), src, AL.mult, 16 * (b - a))
             if last:
                 dma("sync", v("y", S_(16 * a, 16 * b)), c("Wf", 16 * a, 16 * b), 2.0 + (b - a) * 0.03)
             else:
                 scaled(16 * a, 16 * b)
-        weigh(8, 48)
-        weigh(48, 88)
-        tt(c("S", 0, 128), c("S", 0, 128), c(Rb, 0, 128), AL.add, 256)
-        tt(c("S", 1408, 16 * end), c("S", 1408, 16 * end), c(Rb, 128, 16 * end - 1280), AL.add, 32 * end - 2816)
-        weigh(0, 8)
-        weigh(88, end)
+        n = 16 * end - 1280
+        mm([(c("P5", 0, 128), If, c("S", 0, 128), True, True, 512)] +
+           [(c("P5", a, a + 128), If, c("S", 1280 + a, 1408 + a), True, True, 512) for a in range(128, n, 128)])
+        cuts = CFG["weigh"]
+        for a, b in zip(cuts, cuts[1:]):
+            weigh(a, b, c("S", 16 * a, 16 * b))
+        tt(c(Rb, 0, n), c("P5", 0, n), c(Rb, 0, n), AL.add, n)
+        weigh(88, end, c(Rb, 128, n))
+        weigh(0, 8, c(Rb, 0, 128))
 
     steps = [(lanes, 0), (lists, 0), (lanes, 1), (fields, 0), (lists, 1), (lanes, 2), (fields, 1), (lists, 2), (fields, 2)]
     for k, (f, t) in enumerate(steps):
-        bias[0] = CFG["bias"][k]
+        part("lanes" if f is lanes else "steps" if f is lists else "start", t)
         if f is fields:
             border_counts(t)
         f(t)
@@ -766,7 +919,7 @@ def rank_program(g, core, T, topo):
         def schedule(prio, before, after, eng, back):
             left_ = [len(x) for x in before]
             ready, rt, fin, free, order = {}, [None] * n, [0.0] * n, {}, []
-            eng = list(eng)
+            eng, idle = list(eng), [0]
 
             def enter(i):
                 rt[i] = {}
@@ -778,21 +931,50 @@ def rank_program(g, core, T, topo):
                     enter(i)
             while len(order) < n:
                 t0, e = min((max(min(rt[i][e] for i in lst), free.get(e, 0.0)), e) for e, lst in ready.items() if lst)
-                rank_ = lambda k: prio[k] - (ops[k]["lend"] if e != ops[k]["e"] else 0.0)
-                i = max([k for k in ready[e] if rt[k][e] <= t0 + window], key=rank_)
-                if e != ops[i]["e"]:
-                    due = [k for k in ready[e] if rt[k][e] <= t0 + CFG["look"] * ops[i]["alt"][e][0] and rank_(k) > rank_(i)]
+                rank_ = lambda k: prio[k] - (ops[k]["lend"] if e != ops[k]["e"] and not back else 0.0)
+                now = sorted([k for k in ready[e] if rt[k][e] <= t0 + window], key=rank_, reverse=True)
+                i = now[0]
+                look, gap = (CFG["lookt"], CFG["gapt"]) if e == "tensor" else (CFG["look"], CFG["gap"])
+                if look * ops[i]["alt"][e][0] > window:
+                    bar, far = rank_(i) + gap, t0 + look * ops[i]["alt"][e][0]
+                    soon, front = {}, []
+                    for x, lst in ready.items():
+                        for k in lst:
+                            if prio[k] > bar and rt[k][x] < far and (back or x == ops[k]["e"]):
+                                soon[k] = max(rt[k][x], free.get(x, 0.0) if x != e else 0.0)
+                                front.append(k)
+                    due = [(soon[k], k) for k in front if e in rt[k] and rt[k][e] > t0 + window and rank_(k) > bar]
+                    while front:
+                        k = front.pop()
+                        for s, kind in after[k]:
+                            if s not in soon and prio[s] > bar and all(p in soon or rt[p] == {} for p, _ in before[s]):
+                                at = max((soon[p] + ops[p]["d"] if p in soon else fin[p]) + (lat_s if eng[p] == eng[s] else lat_x)
+                                         for p, _ in before[s])
+                                if at < far:
+                                    soon[s] = at
+                                    front.append(s)
+                                    if (eng[s] if back else ops[s]["e"]) == e:
+                                        due.append((max(at, t0 + 0.05), s))
                     if due:
-                        i = min(due, key=lambda k: rt[k][e])
-                for x in rt[i]:
+                        at = min(due)[0]
+                        fit = [k for k in now if t0 + look * ops[k]["alt"][e][0] <= at]
+                        if not fit and idle[0] < 30:
+                            idle[0] += 1
+                            free[e] = max(min(at, t0 + 0.2), t0 + 0.05)
+                            continue
+                        i = (fit or now)[0]
+                idle[0] = 0
+                at_i = rt[i]
+                rt[i] = {}
+                for x in at_i:
                     ready[x].remove(i)
                 o = ops[i]
                 eng[i] = e
                 d = o["alt"][e][0]
                 hold = d if o["k"] == "c" else (0.0 if e == "ext" else (0.1 if o["k"] == "dma" else 0.5))
-                st = max(t0, rt[i][e])
+                st = max(t0, at_i[e])
                 if back:
-                    st = max(rt[i][e], t0 - (d - hold))
+                    st = max(at_i[e], t0 - (d - hold))
                 fin[i] = st + d
                 free[e] = fin[i] if back else st + hold
                 order.append(i)
@@ -808,13 +990,18 @@ def rank_program(g, core, T, topo):
             tail[i] = ops[i]["d"] + max([tail[s] + wait(i, eng[i], eng[s], k) for s, k in succ[i]] + [0.0])
         best = None
         for turn in range(CFG["turns"]):
-            span, fin, order, eng = schedule([x + o["b"] - CFG["own"] * o["d"] for x, o in zip(tail, ops)], pred, succ, eng, False)
-            if best is None or span < best[0]:
-                best = (span, fin, order, eng)
+            shake = CFG["shake"] if turn >= CFG["plain"] else 0.0
+            if shake and turn % 3 == 0:
+                tail, eng = best[4], best[3]
+            prio = [x + o["b"] - CFG["own"] * o["d"] + shake * ((k * 7919 + turn * 104729) % 1009) / 1009.0
+                    for k, (x, o) in enumerate(zip(tail, ops))]
+            span, fin, order, eng = schedule(prio, pred, succ, eng, False)
             STATS.setdefault("spans", []).append(round(span, 1))
             tail = schedule(fin, succ, pred, eng, True)[1]
-        PLAN["order"], PLAN["eng"] = best[2], best[3]
-        STATS.update({"span": best[0], "n": n, "fin": best[1], "ops": ops})
+            if best is None or span < best[0]:
+                best = (span, fin, order, eng, tail)
+        span, fin, PLAN["order"], PLAN["eng"] = polish(ops, best[2], best[3], lat_x, lat_s)
+        STATS.update({"span": span, "n": n, "fin": fin, "ops": ops})
 
     queue = {"pool": g, "vector": g.vector, "scalar": g.scalar, "tensor": g.tensor, "sync": g.sync}
     token, count, seen, n_d = {}, {}, {}, 0

@@ -6,33 +6,24 @@ from concourse.mybir import AluOpType, ActivationFunctionType, AxisListType
 AL = AluOpType
 AF = ActivationFunctionType
 V, W, RO, STEP = 1536, 1792, 3, 1344
-F, B, I, U16 = "float32", "bfloat16", "int32", "uint16"
+F, B, H, I, U16 = "float32", "bfloat16", "float16", "int32", "uint16"
 BIG = 1.5 * 2.0 ** 35
-UB = W + 8
+UB = W + 136
 TOP = 16 * 4096.0
 WT = 264
+UP = 2.0 ** 32
+RING = ((0, 104, 8), (8, 88, 8), (16, 0, 8), (24, 96, 8), (32, 8, 80))
 CFG = {
-    "split": ((0, 64, 128), (0, 48, 128), (0, 32, 64, 96, 128)),
-    "per": ((0, 32, 64, 96, 128), (0, 32, 64, 96, 128), (0, 32, 64, 96, 112, 128)), "per4": ((0, 32, 64, 96, 128),) * 3, "lendf": 5.0, "fast": (1, 1, 0), "weigh": (8, 48, 88),
-    "turn": 128,
-    "turns": 5, "polish": 9000, "heat": 0.1, "lookt": 1.5, "gapt": 1.0, "est": 0,
-    "plain": 5,
-    "shake": 0.6,
-    "short": ((0, 0), (0, 0), (0, 0)),
-    "batch": ((0, 3, 4),) * 3,
-    "ebatch": ((1, 4),) * 3,
-    "look": 0.3,
-    "gap": 2.0,
-    "lend": (100.0, 50.0, 30.0),
-    "lendv": (0.0, 20.0, 5.0),
-    "acts": 8,
-    "lanes": (0, 0, 0), "steps": (0, 0, 0), "marks": (0, 0, 0), "equal": (0, 0, 0), "counts": (0, 0, 0), "start": (0, 0, 0),
-    "mean": (0, 0, 0), "bounds": (0, 0, 0), "sums": (0, 0, 0),
-    "lat": (0.35, 0.17, 0.1),
-    "same": True,
-    "piece": 600,
-    "own": 0.5,
-    "vbank": ("P1", "P0", "P1"),
+    "split": ((0, 32, 64, 96, 128),) * 3,
+    "per": ((0, 32, 64, 96, 128),) * 3,
+    "fast": (1, 1, 0), "weigh": (8, 48, 88), "est": 1, "stages": (1, 1, 1), "silu": (1, 1, 1), "hiV": (0, 0, 1), "eqlast": (0, 0, 1, 1), "early": (1, 1, 0), "ecut": ((1, 2, 3, 4), (1, 3, 4), (1, 3, 4)), "unS": (0, 0, 0),
+    "batch": ((0, 2, 3, 4), (0, 3, 4), (0, 3, 4)),
+    "acts": (5, 8, 8),
+    "lend": (3.0, 3.0, 1.0), "lendv": (0.0, 1.0, 1.0), "lendc": 0.3,
+    "due": (77, 44, 0), "duel": (111, 72, 39), "pace": (6, 6.0, 6.8),
+    "lat": (0.35, 0.17), "piece": 600, "vbank": ("P1", "P0", "P1"),
+    "rounds": 6500, "heat": 0.35, "moves": (0.2, 0.4, 0.47, 0.72), "seed": 1, "off": 0.7, "pull": 1.5,
+    "other": ((0.7, (1.35, 1.9, 5.0, 1.0)), (0.95, (1.1, 1.15, 2.5, 1.5))),
 }
 STATS = {}
 
@@ -45,36 +36,40 @@ def _sb(names, shape, dtype):
 
 
 _sb("VD ntb", [W], I)
-_sb("Gt volE", [W + 16], B)
+_sb("St", [W], B)
+_sb("volE", [W + 16], B)
 _sb("Wf", [UB + W], F)
-_sb("S", [1920], F)
-_sb("wall", [3 * WT], F)
-_sb("Z0", [256], F)
+_sb("wall", [4 * WT], F)
+_sb("Z0", [96], F)
 _sb("Rb0 Rb1 Rb2", [512], F)
 _sb("dvO", [112, 3], F)
 _sb("Ug", [10240], F)
+_sb("Omin Omax", [2304], F)
 _sb("un", [32], F)
-_sb("Omin Omax", [1280], F)
-_sb("Zp", [8, 8, 240], B)
-_sb("OL", [5, 8, 240], B)
+_sb("un8", [128], F)
+_sb("lev", [512], F)
+_sb("Zp", [8, 4, 3, 16], B)
+_sb("OL", [5, 4, 3, 16], B)
 _sb("Cq", [3, 143], B)
 _sb("pid", [4], I)
 _sb("col", [16], F)
 _sb("rows", [3, 128], F)
-_sb("cf", [8, 128], F)
-_sb("cb", [8, 128], B)
+_sb("cf", [6, 128], F)
+_sb("cb", [9, 128], B)
+_sb("top", [256], B)
 _sb("M16", [16], F)
 _sb("cm aBf", [8], F)
 _sb("cW", [8], B)
+_sb("wb", [32], B)
 _sb("Rq", [16, 128], B)
 _sb("Dq Dg", [144], B)
 _sb("wpad", [240], B)
 _sb("selP", [8, 128], B)
-_sb("xr1 ring volN nA", [112], B)
-_sb("x16r qtab", [96], B)
+_sb("ring ring16 volN nA", [112], B)
+_sb("rq", [3, 16], F)
 _sb("xtab", [3, 112], B)
 _sb("qu qa hh thr1", [112], F)
-_sb("lane biasL dump thr", [40], F)
+_sb("lane lane1 biasL dump thr", [40], F)
 _sb("smallR", [96], B)
 _sb("junk", [8, 96], B)
 _sb("Cc", [96], F)
@@ -82,32 +77,31 @@ _sb("Pw", [104], F)
 _sb("acc bo2 ka kb", [8], F)
 _sb("bo", [56], F)
 _sb("dig", [3, 56], F)
-_sb("ring16", [112], B)
 _sb("q16", [16], B)
 _sb("mm", [32], F)
-_sb("row", [2, 512], B)
 _sb("xr", [16], B)
 _sb("x16", [8], U16)
 _sb("cmpb XE", [128], B)
 _sb("raw", [128], F)
 _sb("b16", [2, 5, 128], U16)
-_sb("bn wZ Mm Dd De Rlo Rhi", [128], F)
+_sb("wZ Mm Dd De Rlo Rhi", [128], F)
 _sb("A2", [256], F)
 _sb("KS", [256], F)
-_sb("SC MK rmask hold", [128], F)
-_sb("Bc", [5, 128], F)
+_sb("SC rmask qmask", [128], F)
+_sb("bn MK hold", [128], H)
+_sb("Ih", [2, 128], H)
+_sb("cmh", [2, 8], H)
+_sb("Bc", [4, 128], F)
 _sb("Vg", [2048], B)
 _sb("eq", [4, 128], B)
 _sb("o16 nA16 off16", [2, 40], U16)
-_sb("nW th pre thm", [2, 40], F)
-_sb("volM G", [2, 640], B)
+_sb("nW th pre", [2, 40], F)
+_sb("G", [2, 640], B)
 _sb("OH", [40, 112], B)
 _sb("ne ff t40", [40], F)
 _sb("hc", [5, 16], F)
 _sb("hcm", [16], B)
 _sb("Zq", [40], B)
-_sb("es", [24], F)
-_sb("ev", [2, 8], B)
 _sb("nS thB", [32], F)
 _sb("EQ", [8, 512], B)
 _sb("Wb", [512], B)
@@ -116,11 +110,11 @@ _sb("Ss tg", [4, 128], F)
 _sb("z16", [2, 8], U16)
 _sb("nR", [RO, 32], F)
 _sb("nF", [RO, 112], B)
-_sb("nOff sel", [2, 112], U16)
+_sb("nOff", [2, 120], U16)
 for _k in range(8):
     SCRATCH["P%d" % _k] = ("psum", [128, 512], F)
 
-SEMAPHORES = ["c_vector", "c_scalar", "c_tensor", "c_pool"] + ["d%d" % k for k in range(28)] + \
+SEMAPHORES = ["c_vector", "c_scalar", "c_tensor", "c_pool"] + ["d%d" % k for k in range(12)] + \
              ["ls%d" % k for k in range(9)] + ["ar%d" % k for k in range(9)]
 
 CY = 0.83e-3 * 1.05
@@ -129,91 +123,175 @@ GA, SCA = 1.56, 3.5
 PLAN = {}
 
 
-def polish(ops, order, eng, lat_x, lat_s):
+def place(x, a, b):
+    lo, hi = 0, len(b) - 1
+    while lo < hi:
+        mid = (lo + hi) // 2
+        if b[mid] > x:
+            hi = mid
+        else:
+            lo = mid + 1
+    return lo
+
+
+def plan(ops):
     n = len(ops)
-    eng, order, seed = list(eng), list(order), [1]
-    hard = [sorted(o["deps"] | o["war"]) for o in ops]
-    pred = [set(hard[i]) | o["order"] for i, o in enumerate(ops)]
+    lat_x, lat_s = CFG["lat"]
+    comp = [o["k"] == "c" for o in ops]
+    pred = [[(d, 0) for d in sorted(o["deps"])] + [(d, 1) for d in sorted(o["order"] - o["deps"])] for o in ops]
+    anc = [0] * n
+    for i in range(n):
+        far = 0
+        for d, k in pred[i]:
+            far |= anc[d]
+        pred[i] = [(d, k) for d, k in pred[i] if not far >> d & 1]
+        for d, k in pred[i]:
+            far |= 1 << d
+        anc[i] = far
     succ = [[] for _ in ops]
     for i in range(n):
-        for p in sorted(pred[i]):
-            succ[p].append(i)
-    dur = [o["alt"][e][0] for o, e in zip(ops, eng)]
-    hold = [d if o["k"] == "c" else (0.0 if e == "ext" else (0.1 if o["k"] == "dma" else 0.5)) for o, e, d in zip(ops, eng, dur)]
-
-    def waits(i):
-        return [(p, lat_s if eng[p] == eng[i] and ops[p]["k"] == "c" else lat_x) for p in hard[i]]
-    lat = [waits(i) for i in range(n)]
+        for d, k in pred[i]:
+            succ[d].append((i, k))
+    alts = [[(e, a[0], a[0] if comp[i] else (0.0 if e == "ext" else (0.1 if o["k"] == "dma" else 0.5))) for e, a in o["alt"].items()]
+            for i, o in enumerate(ops)]
+    seed = [CFG["seed"]]
 
     def draw():
         seed[0] = (seed[0] * 1103515245 + 12345) % 2 ** 31
         return seed[0] / 2.0 ** 31
 
-    def run(seq):
-        fin, st, why, free, last = [0.0] * n, [0.0] * n, [-1] * n, {}, {}
-        for i in seq:
-            e = eng[i]
-            s, w = free.get(e, 0.0), last.get(e, -1)
-            for p, x in lat[i]:
-                x += fin[p]
-                if x > s:
-                    s, w = x, -2 - p
-            st[i], fin[i], why[i] = s, s + dur[i], w
-            if e != "ext":
-                free[e], last[e] = s + hold[i], i
-        return max(fin), st, fin, why
+    def lay(key, before, after, eng, back, free):
+        key = list(key)
+        for i in (range(n - 1, -1, -1) if back else range(n)):
+            for p, k in before[i]:
+                if key[p] >= key[i]:
+                    key[i] = key[p] + 1e-6
+        st, fin, eng, gaps = [0.0] * n, [0.0] * n, list(eng), {}
+        for i in sorted(range(n), key=lambda i: key[i]):
+            best = None
+            for e, d, h in alts[i]:
+                shy = 0.0
+                if e != eng[i]:
+                    if not free or not free[i]:
+                        continue
+                    shy = free[i] if e == "vector" else free[i] - CFG["pull"]
+                r = 0.0
+                for p, k in before[i]:
+                    x = fin[p] + (0.0 if k else (lat_s if eng[p] == e and comp[i if back else p] else lat_x))
+                    if x > r:
+                        r = x
+                at = -1
+                if h:
+                    if e not in gaps:
+                        gaps[e] = ([0.0], [1e9])
+                    a, b = gaps[e]
+                    if back:
+                        r += d - h
+                    at = len(b) - 1 if r >= a[-1] else place(r, a, b)
+                    while (a[at] if a[at] > r else r) + h > b[at] + 1e-9:
+                        at += 1
+                    if a[at] > r:
+                        r = a[at]
+                    if back:
+                        r -= d - h
+                if best is None or r + d + shy < best[0]:
+                    best = (r + d + shy, e, r, d, h, at)
+            _, e, r, d, h, at = best
+            eng[i], st[i], fin[i] = e, r, r + d
+            if h:
+                a, b = gaps[e]
+                x = r + d - h if back else r
+                lo, hi = x - a[at] > 0.04, b[at] - x - h > 0.04
+                if lo and hi:
+                    a.insert(at + 1, x + h)
+                    b.insert(at, x)
+                elif lo:
+                    b[at] = x
+                elif hi:
+                    a[at] = x + h
+                else:
+                    del a[at], b[at]
+        return max(fin), st, fin, eng
 
-    def give(i, e):
-        eng[i] = e
-        dur[i] = hold[i] = ops[i]["alt"][e][0]
-        for y in [i] + succ[i]:
-            lat[y] = waits(y)
+    def both(key, eng, free):
+        span, st, fin, eng = lay(key, pred, succ, eng, False, free)
+        t, _, f2, _ = lay([-x for x in fin], succ, pred, eng, True, None)
+        return [span, st, fin, eng, [t - x for x in f2]]
 
-    cur, st, fin, why = run(order)
-    best = (cur, fin, list(order), list(eng))
-    for _ in range(CFG["polish"]):
-        order.sort(key=lambda i: st[i])
-        pos = [0] * n
-        for k, i in enumerate(order):
-            pos[i] = k
-        i, arcs = fin.index(cur), []
-        while why[i] != -1:
-            if why[i] >= 0:
-                arcs.append((why[i], i))
-            i = why[i] if why[i] >= 0 else -2 - why[i]
-        new, flip = None, None
-        for _try in range(30):
-            k = int(draw() * len(arcs))
-            (u, x), r = arcs[k], draw()
-            if r < 0.08:
-                flip = u if len(ops[u]["alt"]) > 1 else (x if len(ops[x]["alt"]) > 1 else None)
-            elif r < 0.54:
-                while k + 1 < len(arcs) and arcs[k + 1][1] == u and draw() < 0.7:
-                    k += 1
-                    u = arcs[k][0]
-                if all(pos[p] < pos[u] for p in pred[x]):
-                    new = order[:pos[u]] + [x] + order[pos[u]:pos[x]] + order[pos[x] + 1:]
-            else:
-                while k > 0 and arcs[k - 1][0] == x and draw() < 0.7:
-                    k -= 1
-                    x = arcs[k][1]
-                if all(pos[s] > pos[x] for s in succ[u]):
-                    new = order[:pos[u]] + order[pos[u] + 1:pos[x] + 1] + [u] + order[pos[x] + 1:]
-            if new is not None or flip is not None:
-                break
-        if flip is not None:
-            old, new = eng[flip], order
-            give(flip, [e for e in ops[flip]["alt"] if e != old][0])
-        if new is None:
-            continue
-        c, s2, f2, w2 = run(new)
-        if c <= cur + CFG["heat"] * draw() ** 3:
-            cur, st, fin, why, order = c, s2, f2, w2, list(new)
-            if c < best[0]:
-                best = (c, fin, list(new), list(eng))
-        elif flip is not None:
-            give(flip, old)
-    return best
+    def slow(o, d, speed):
+        if o["k"] == "c":
+            return d * speed[0] * (1.0, speed[1] / GA, speed[2] / SCA)[o["g"]]
+        return d * (speed[3] if o["e"] == "pool" else 1.0)
+    other = [(w, [{e: slow(o, a[0], speed) for e, a in o["alt"].items()} for o in ops]) for w, speed in CFG["other"]]
+
+    def worth(x):
+        order, eng, total = sorted(range(n), key=lambda i: (x[1][i], i)), x[3], x[0]
+        for w, dur in other:
+            fin, free = [0.0] * n, {}
+            for i in order:
+                e = eng[i]
+                r = free.get(e, 0.0)
+                for p, k in pred[i]:
+                    y = fin[p] + (0.0 if k else (lat_s if eng[p] == e and comp[p] else lat_x))
+                    if y > r:
+                        r = y
+                fin[i] = r + dur[i][e]
+                if e != "ext":
+                    free[e] = fin[i] if comp[i] else r + (0.1 if ops[i]["k"] == "dma" else 0.5)
+            total += w * max(fin)
+        return total / (1 + len(other))
+
+    tail = [0.0] * n
+    for i in range(n - 1, -1, -1):
+        tail[i] = ops[i]["d"] + max([tail[s] + (0.0 if k else lat_x) for s, k in succ[i]] + [ops[i].get("due", 0.0)])
+    kinds = sorted(set(o["w"] for o in ops))
+    kind = [kinds.index(o["w"]) for o in ops]
+    parts = sorted(set(o["p"] for o in ops))
+    part = [parts.index(o["p"]) for o in ops]
+    two = [i for i in range(n) if len(alts[i]) > 1]
+    cur = both([-x - o["b"] for x, o in zip(tail, ops)], [o["e"] for o in ops], [o.get("lend", 0.0) + 1e-3 for o in ops])
+    for _ in range(3):
+        new = both(cur[4], cur[3], None)
+        if new[0] <= cur[0]:
+            cur = new
+    cur.append(worth(cur))
+    best, rounds, m = cur, CFG["rounds"], CFG["moves"]
+    STATS["spans"] = [round(cur[0], 1)]
+    for it in range(rounds):
+        mix = draw()
+        base = [mix * x + (1 - mix) * y for x, y in zip(cur[1], cur[4])] if draw() < 0.5 else cur[4]
+        at, wide, amp = draw() * max(cur[2]), 3 + 20 * draw() ** 2, 0.2 + draw()
+        r, key, free, eng = draw(), base, None, cur[3]
+        if r < m[0]:
+            sh = [amp * 3 * (draw() - 0.5) if draw() < 0.2 else 0.0 for _ in kinds]
+            key = [x + sh[k] if at < x < at + wide else x for x, k in zip(base, kind)]
+        elif r < m[1]:
+            key = [x + amp * (draw() - 0.5) if at < x < at + wide else x for x in base]
+        elif r < m[2]:
+            sh = [amp * 8 * (draw() - 0.5) if draw() < 0.1 else 0.0 for _ in parts]
+            key = [x + sh[k] for x, k in zip(base, part)]
+        elif r < m[3]:
+            bar = 2.0 * draw() ** 2 + 1e-3
+            free = [bar if at < x < at + wide else 0.0 for x in base]
+        else:
+            eng = list(eng)
+            off = "vector" if draw() < CFG["off"] else ""
+            near = [i for i in two if at < base[i] < at + wide and (eng[i] == off or not off)]
+            for _ in range(1 + int(2 * draw())):
+                if near:
+                    i = near[int(draw() * len(near))]
+                    eng[i] = [a[0] for a in alts[i] if a[0] != eng[i]][0]
+        new = both(key, eng, free)
+        if new[0] <= cur[0] + 1.0:
+            new.append(worth(new))
+            if new[5] <= cur[5] + CFG["heat"] * (1 - it / rounds) * draw() ** 2:
+                cur = new
+                if new[5] < best[5]:
+                    best = new
+        if it % max(1, rounds // 8) == 0:
+            STATS["spans"].append((round(cur[0], 1), round(cur[5], 1)))
+    STATS.update({"span": max(best[2]), "n": n, "fin": best[2], "ops": ops})
+    return sorted(range(n), key=lambda i: (best[1][i], i)), best[3]
 
 
 def rank_program(g, core, T, topo):
@@ -235,7 +313,7 @@ def rank_program(g, core, T, topo):
             used = used + e
         return out
 
-    ops, log, bias, banks = [], {}, [0.0], {}
+    ops, log, tag, banks = [], {}, [0.0, ("start", -1)], {}
     S_ = slice
     ALL = S_(None)
 
@@ -253,9 +331,10 @@ def rank_program(g, core, T, topo):
     def ind(win, off):
         return {"ap": win["ap"].indirect(off["ap"]), "r": win["r"], "x": off["r"]}
 
-    def op(eng, dur, fn, reads, writes, kind="c", extra=None):
+    def op(eng, dur, fn, reads, writes, kind="c", extra=None, two=False):
         me = len(ops)
-        deps, soft, order_only = set(), set(), set()
+        who = me if two else eng
+        deps, order_only = set(), set()
         acc = []
         for x in reads:
             if isinstance(x, dict):
@@ -263,18 +342,15 @@ def rank_program(g, core, T, topo):
         for x in writes:
             acc += [(r, True) for r in x["r"]] + [(r, False) for r in x.get("x", [])]
         for name in sorted(set(r[0] for r, _ in acc if r[0] in SCRATCH and SCRATCH[r[0]][0] == "psum")):
-            turn = banks.setdefault(name, [eng, [], []])
-            if turn[0] != eng:
-                turn[:] = [eng, [], turn[1]]
+            turn = banks.setdefault(name, [who, [], []])
+            if turn[0] != who:
+                turn[:] = [who, [], turn[1]]
             deps.update(turn[2])
             turn[1].append(me)
         for (name, m), wr in acc:
             for (m2, o, w2) in log.get(name, []):
                 if o != me and (m & m2) and (wr or w2):
-                    if eng == "tensor" and ops[o]["e"] == eng:
-                        order_only.add(o)
-                    else:
-                        (soft if not w2 and kind == "c" and ops[o]["k"] == "c" else deps).add(o)
+                    (order_only if eng == "tensor" and ops[o]["e"] == eng else deps).add(o)
         for (name, m), wr in acc:
             lst = log.setdefault(name, [])
             if wr:
@@ -282,13 +358,13 @@ def rank_program(g, core, T, topo):
             lst.append((m, me, wr))
         if extra is not None:
             deps.add(extra)
-        ops.append({"e": eng, "d": dur, "alt": {eng: (dur, fn)}, "deps": deps, "war": soft - deps, "order": order_only, "k": kind,
-                    "b": bias[0], "w": [x["r"][0][0] for x in writes if x["r"]],
+        ops.append({"e": eng, "d": dur, "alt": {eng: (dur, fn)}, "deps": deps, "order": order_only, "k": kind, "b": tag[0], "p": tag[1],
+                    "w": ([x["r"][0][0] for x in writes if x["r"]] + [""])[0],
                     "g": 2 if any("x" in x for x in writes) else int(any(isinstance(x, dict) and "x" in x for x in reads))})
         return me
 
     def part(name, t):
-        bias[0] = CFG[name][t]
+        tag[1] = (name, t)
 
     def a_(x):
         return x["ap"] if isinstance(x, dict) else x
@@ -304,7 +380,7 @@ def rank_program(g, core, T, topo):
         op("vector", vd(n, x, o), lambda q: q.tensor_copy(o["ap"], x["ap"]), [x], [o])
 
     def tt(o, x, y, f, n):
-        op("vector", vd(n, x), lambda q: q.tensor_tensor(o["ap"], x["ap"], y["ap"], f), [x, y], [o])
+        op("vector", vd(n, x, o), lambda q: q.tensor_tensor(o["ap"], x["ap"], y["ap"], f), [x, y], [o])
 
     def ts(o, x, s1, f1, n, s2=None, f2=None):
         if s2 is None:
@@ -321,6 +397,8 @@ def rank_program(g, core, T, topo):
     def ms(o, val, n):
         op("vector", vd(n), lambda q: q.memset(o["ap"], val), [], [o])
 
+    first_exp = []
+
     def act(o, x, n, f=AF.Copy, bias=None, scale=None, accum=None):
         k = {}
         if bias is not None:
@@ -334,12 +412,34 @@ def rank_program(g, core, T, topo):
             first_exp.append(1)
         op("scalar", d, lambda q: q.activation(o["ap"], x["ap"], f, **k), [x, bias, scale], [o] + ([accum] if accum else []))
 
-    first_exp = []
+    def flex(first, o, x, n, scale=1.0, bias=None, relu=False, half=False, lend=None):
+        k = {"scale": a_(scale)}
+        if bias is not None:
+            k["bias"] = a_(bias)
+        f = AF.Relu if relu else (AF.Copy if bias is None else AF.Identity)
+        if relu:
+            on_v = lambda q: q.tensor_scalar(o["ap"], x["ap"], 0.0, None, AL.max)
+        elif bias is None:
+            on_v = lambda q: q.tensor_scalar(o["ap"], x["ap"], a_(scale), None, AL.mult)
+        else:
+            on_v = lambda q: q.tensor_scalar(o["ap"], x["ap"], a_(scale), a_(bias), AL.mult, AL.add)
+        alt = {"scalar": (0.07 + (GA * n if "x" in x else max(64, n)) * CY, lambda q: q.activation(o["ap"], x["ap"], f, **k)),
+               "vector": (vd(n // 2 if half else n, x), on_v)}
+        op(first, alt[first][0], alt[first][1], [x, scale, bias], [o], two=True)
+        ops[-1]["alt"] = alt
+        ops[-1]["lend"] = CFG["lendc"] if lend is None else lend
 
-    def either(o, x, n, scale=1.0, lend=0.0):
-        act(o, x, n, scale=scale)
-        ops[-1]["lend"] = lend
-        ops[-1]["alt"]["vector"] = (vd(n, x), lambda q: q.tensor_scalar(o["ap"], x["ap"], scale, None, AL.mult))
+    def put(o, x, either):
+        cp(o, x, 128)
+        if either:
+            ops[-1]["alt"]["scalar"] = (0.07 + SCA * 128 * CY, lambda q: q.activation(o["ap"], x["ap"], AF.Silu))
+            ops[-1]["lend"] = 0.3
+
+    def fs(*a, **k):
+        flex("scalar", *a, **k)
+
+    def fv(*a, **k):
+        flex("vector", *a, **k)
 
     def mm(lst):
         pieces, size = [[]], 0
@@ -349,15 +449,15 @@ def rank_program(g, core, T, topo):
                 size = 0
             pieces[-1].append(x)
             size += x[5]
-        for part in pieces:
-            def f(q, part=part):
-                for (o, l, r, st, sp, _) in part:
+        for piece in pieces:
+            def f(q, piece=piece):
+                for (o, l, r, st, sp, _) in piece:
                     ins = q.matmul(o["ap"], l["ap"], r["ap"], st, sp)
                 return ins
-            mark = [{"r": [(b + "g", 1)]} for b in sorted(set(x[0]["r"][0][0] for x in part))]
-            shut = part[0][3] and part[-1][4]
-            op("tensor", 0.03 + sum(x[5] for x in part) * PCY, f, [x[1] for x in part] + [x[2] for x in part] + (mark if shut else []),
-               [x[0] for x in part] + ([] if shut else mark))
+            mark = [{"r": [(b + "g", 1)]} for b in sorted(set(x[0]["r"][0][0] for x in piece))]
+            shut = piece[0][3] and piece[-1][4]
+            op("tensor", 0.03 + sum(x[5] for x in piece) * PCY, f, [x[1] for x in piece] + [x[2] for x in piece] + (mark if shut else []),
+               [x[0] for x in piece] + ([] if shut else mark))
 
     def cut(x):
         return dict(x, cut=True)
@@ -371,7 +471,7 @@ def rank_program(g, core, T, topo):
 
     def fill(o, val, n):
         iota(o, [[0, n]], val, 0, n)
-        ops[-1]["lend"] = CFG["lendf"]
+        ops[-1]["lend"] = 0.5
         ops[-1]["alt"]["vector"] = (vd(n), lambda q: q.memset(o["ap"], float(val)))
 
     def asel(o, x, pat, f, fill, base, cmul, n):
@@ -401,16 +501,15 @@ def rank_program(g, core, T, topo):
         op("ext", 0.3, None, [], [x[1] for x in to_prev + to_next], kind=("ar%d" % k, come), extra=s)
 
     p32 = S_(0, 32)
-    mid = S_(112, 128)
-    bias[0] = 1000.0
+    tag[0] = 1000.0
     dma("sync", c("VD", 0, V, p=S_(0, 8)), v("vol", ALL), 2.2)
     dma("scalar", {"ap": c("VD", 0, V, p=S_(8, 32))["ap"], "r": [("VDx", 1)]}, v("dv", ALL), 2.4)
-    bias[0] = 500.0
+    tag[0] = 500.0
     dma("sync", v("ntb"), v("nt", ALL), 5.5)
-    bias[0] = 400.0
+    tag[0] = 400.0
     dma("scalar", c("Wf", 0, V), v("u", ALL), 8.0)
-    dma("scalar", c("wall", 8, WT), v("wt", ALL), 8.5)
-    bias[0] = 0.0
+    dma("scalar", c("wall", WT + 8, 2 * WT), v("wt", ALL), 8.5)
+    tag[0] = 0.0
 
     ms(v("Cq", p=p32), 1.0, 215)
     asel(v("Cq", p=p32), v("Cq", p=p32), [[-16, 3], [-3, 143]], AL.is_equal, 0.0, -83, 16, 429)
@@ -422,7 +521,7 @@ def rank_program(g, core, T, topo):
     iota(v("lane"), [[0, 5], [16, 8]], 0, 0, 40)
     ts(c("pid", 1, 2), c("pid", 0, 1), 15, AL.bitwise_and, 1)
     ts(c("pid", 2, 3), c("pid", 0, 1), 4, AL.arith_shift_right, 1)
-    qc, gc, shc, alc, wc, pc = [c("col", k, k + 1) for k in (0, 1, 3, 4, 5, 6)]
+    qc, gc, below, shc, alc, wc, pc, lnw, twice, less, most = [c("col", k, k + 1) for k in range(11)]
     cp(qc, c("pid", 1, 2), 1)
     cp(gc, c("pid", 2, 3), 1)
     cp(pc, c("pid", 0, 1), 1)
@@ -430,85 +529,122 @@ def rank_program(g, core, T, topo):
     ts(shc, shc, pc, AL.add, 1, 16.0, AL.add)
     lrow, qrow, grow = v("rows", 0), v("rows", 1), v("rows", 2)
     If = v("cf", 0)
-    Ib, bo, up, negI, shm, shmK, I16, top = [v("cb", k) for k in range(8)]
+    Ib, bo, up, negI, shm, I16, selV, selE, selQ = [v("cb", k) for k in range(9)]
     bo8 = v("cb", 1, S_(0, 128, 16))
     I8 = v("cb", 0, S_(0, 128, 16))
     ts(bo, grow, gc, AL.is_equal, 128)
     ts(v("cmpb"), qrow, qc, AL.is_lt, 128)
     tt(up, v("cmpb"), bo, AL.mult, 256)
     ts(v("lane"), v("lane"), qc, AL.add, 40)
-    ts(v("biasL"), v("lane"), -1.0, AL.mult, 40, -0.5, AL.add)
+    fv(v("biasL"), v("lane"), 40, -1.0, -0.5)
     ts(If, lrow, pc, AL.is_equal, 128)
     ts(Ib, lrow, pc, AL.is_equal, 128)
     ts(shm, lrow, shc, AL.is_equal, 128)
-    negf, Iup, Idown = v("cf", 6), v("cf", 1), v("cf", 7)
-    for o, x, k in [(I16, Ib, 16.0), (negI, Ib, -2.0 ** 24), (shmK, shm, 4096.0), (negf, If, -1.0), (Iup, If, 2.0 ** 16),
-                    (Idown, If, -2.0 ** 20)] + [(v("cf", 1 + s), If, s / 8.0) for s in range(1, 5)]:
-        act(o, x, 128, scale=k)
-    iota(top, [[0, 8], [-4096, 16]], int(TOP), 0, 128)
+    negf = v("cf", 1)
+    ts(v("Ih", 0), lrow, pc, AL.is_equal, 128)
+    ts(v("Ih", 1), lrow, pc, AL.is_equal, 128, -16.0, AL.mult)
+    for o, k in [(I16, 16.0), (negI, -2.0 ** 24)]:
+        fs(o, Ib, 128, k, half=True)
+    for o, k in [(negf, -1.0)] + [(v("cf", 1 + s), s / 8.0) for s in range(1, 5)]:
+        fs(o, If, 128, k)
+    fill(c("top", 0, 256, 2), 0, 128)
+    iota(c("top", 1, 256, 2), [[0, 8], [-4096, 16]], int(TOP), 0, 128)
     fill(c("ne", 0, 8), 1, 8)
     ts(v("M16"), v("rows", 0, S_(0, 16)), qc, AL.is_equal, 16)
     ts(v("cm"), v("rows", 0, S_(0, 8)), gc, AL.is_equal, 8)
+    row = lambda k: c("M16", k, k + 1)
     fill(v("cW"), -W, 8)
+    iota(c("wb", 0, 24), [[WT, 3], [0, 8]], WT, 0, 24)
+    fill(c("wb", 24, 32), WT, 8)
     fill(c("Pw", 96, 104), 10 ** 6, 8)
     fill(v("A2"), 0, 256)
-    fill(v("hold"), 0, 128)
+    ts(v("hold"), qrow, 0.0, AL.mult, 128)
     ts(v("rmask"), qrow, 0.5, AL.is_gt, 128)
-    qmask = c("P0", 384, 512)
-    ts(qmask, qrow, qc, AL.is_equal, 128)
-    for q in range(16):
-        act(v("Rq", q), bo, 128, scale=c("M16", q, q + 1))
+    ts(v("SC"), qrow, qc, AL.is_lt, 128)
+    ts(v("wZ"), qrow, qc, AL.is_equal, 128, 2.0 ** 60, AL.mult)
+    tt(v("SC"), v("SC"), v("wZ"), AL.add, 256)
+    tt(v("qmask"), v("SC"), v("rmask"), AL.mult, 256)
+    fv(c("qmask", 1, 128, 16), c("qmask", 1, 128, 16), 8, 2.0 ** -60)
+    fv(most, row(0), 1, -984.0, 1000.0)
+    fv(less, row(0), 1, 1.0, -1.0)
+    cp(v("cmh", 0), v("cm"), 8)
+    ts(v("cmh", 1), v("cm"), less, AL.mult, 8)
     fill(v("Dg"), 0, 144)
     cp(c("Dg", 15, 143, 16), v("cm"), 8)
+    for q in range(16):
+        fv(v("Rq", q), c("Dg", 15, 143), 128, row(q), half=True)
     fill(c("Dq", 0, 15), 0, 15)
-    ts(c("Dq", 15, 143), Ib, c("M16", 0, 1), AL.mult, 64)
+    fv(c("Dq", 15, 143), Ib, 128, row(0), half=True)
     for t in range(RO):
         x0 = (STEP * t) % V // 16
         iota(v("xtab", t, S_(0, 96 - x0)), [[1, 96 - x0]], x0, 0, 96 - x0)
         if x0:
             iota(v("xtab", t, S_(96 - x0, 96)), [[1, x0]], 0, 0, x0)
         fill(v("xtab", t, S_(96, 112)), 0, 16)
-    iota(v("xr1"), [[1, 112]], 1, 0, 112)
-    for name, k in (("ring", 1), ("ring16", 16)):
-        for a, b, x in ((0, 8, 97), (8, 104, 1), (104, 112, 105)):
-            iota(c(name, a, b), [[k, b - a]], k * x, 0, b - a)
-    iota(v("q16"), [[1, 16]], -16, 0, 16)
-    fill(v("dig", 1), 1, 56)
-    fill(v("dig", 1, S_(0, 56, 7)), 0, 8)
-    fill(v("dig", 1, S_(3, 56, 7)), -1, 8)
-    for x, val in ((1, BIG), (2, -BIG), (4, -7.5), (5, BIG / 256), (6, 16 - BIG / 256)):
-        ms(v("dig", 0, S_(x, 56, 7)), val, 8)
+    for a, x, n in RING:
+        iota(c("ring", a, a + n), [[1, n]], x + 1, 0, n)
+    if max(CFG["fast"]):
+        fs(v("ring16"), v("ring"), 112, 16.0, half=True)
+        iota(v("q16"), [[1, 16]], -16, 0, 16)
+        fill(v("dig", 1), 1, 56)
+        fill(v("dig", 1, S_(0, 56, 7)), 0, 8)
+        fill(v("dig", 1, S_(3, 56, 7)), -1, 8)
+        for x, val in ((1, BIG), (2, -BIG), (4, -7.5), (5, BIG / 256), (6, 16 - BIG / 256)):
+            ms(v("dig", 0, S_(x, 56, 7)), val, 8)
+    q16f = v("rows", 0, S_(0, 16))
+    fv(v("rq", 0), q16f, 16, row(4), row(2))
+    tt(v("rq", 1), v("rq", 0), q16f, AL.mult, 32)
+    fv(v("rq", 2), v("rq", 1), 16, 1.0, row(3))
     for q in range(16):
-        act(c("Gt", q, W, 16), v("xr1"), 112, scale=c("M16", q, q + 1))
-    fill(c("Gt", W, W + 16), 0, 16)
+        fv(c("St", q, W, 16), v("ring"), 112, row(1), v("rq", 2, S_(q, q + 1)), half=True)
+    fs(selV, bo, 128, row(0), half=True)
+    ts(selE, bo, row(3), AL.mult, 64, 0.0625, AL.mult)
+    ts(v("raw"), qrow, row(3), AL.mult, 128, -1.0, AL.mult)
+    fv(twice, row(2), 1, 2.0)
+    fv(v("raw"), v("raw"), 128, 1.0, twice)
+    tt(v("raw"), v("raw"), qrow, AL.mult, 256)
+    ts(v("raw"), v("raw"), row(3), AL.add, 128, row(4), AL.subtract)
+    ts(below, gc, 0.5, AL.is_lt, 1, 8.0, AL.mult)
+    ts(below, below, gc, AL.add, 1, -1.0, AL.add)
+    ts(v("Mm"), grow, below, AL.is_equal, 128)
+    tt(selQ, v("raw"), v("Mm"), AL.mult, 256)
     fill(c("volE", W, W + 16), 0, 16)
-    fill(c("Wf", W, W + 8), 0, 8)
+    fill(c("Wf", W, UB), 0, UB - W)
     fill(c("wall", 0, 8), 1, 8)
-    fill(c("S", W, 1920), 0, 128)
-    fill(v("Z0"), 0, 256)
-    iota(v("x16r"), [[16, 96]], 0, 0, 96)
-    act(v("qtab"), v("rows", 0, S_(0, 96)), 96, AF.Identity, bias=qc, scale=0.0)
-    ts(v("dump"), v("lane"), float(W), AL.add, 40)
+    ms(c("wall", WT, WT + 8), 0.5, 8)
+    fill(v("Z0"), 0, 96)
+    fv(v("lane1"), v("lane"), 40, 1.0, 1.0)
+    fv(v("dump"), v("lane"), 40, 1.0, W + 1.0)
     ln2 = math.log(2.0)
-    ts(c("col", 8, 9), qc, 7 * ln2, AL.mult, 1, -52 * ln2, AL.add)
-    ts(c("col", 9, 10), pc, -ln2, AL.mult, 1, 63 * ln2, AL.add)
-    act(c("col", 4, 6), c("col", 8, 10), 2, AF.Exp)
-    ts(v("t40"), v("lane"), -ln2, AL.mult, 40, 63 * ln2 + math.log(2.5), AL.add)
+    fv(lnw, pc, 1, -ln2, 63 * ln2)
+    act(wc, lnw, 1, AF.Exp)
+    fv(v("t40"), v("lane"), 40, -ln2, 63 * ln2 + math.log(2.5))
     act(v("thr"), v("t40"), 40, AF.Exp)
-    ts(c("hcm", 8, 16), v("cm"), alc, AL.mult, 8)
-    cp(v("aBf"), c("hcm", 8, 16), 8)
-    cp(c("hcm", 0, 8), v("cm"), 8)
+    fv(alc, row(1), 1, 16.0, row(2))
+    fv(v("aBf"), v("cm"), 8, alc)
+    fv(c("hcm", 8, 16), v("aBf"), 8)
+    fv(c("hcm", 0, 8), v("cm"), 8, row(1))
     for k in range(8):
-        act(v("selP", k), lrow, 128, AF.Identity, bias=c("aBf", k, k + 1), scale=0.0)
+        fs(v("selP", k), Ib, 128, 0.0, c("aBf", k, k + 1), half=True)
     fill(v("wpad"), 0, 240)
-    ts(c("wpad", 112, 128), v("M16"), 0.0, AL.mult, 16, wc, AL.add)
-    iota(v("un"), [[0, 16], [255, 2]], 1, 0, 32)
-    bias[0] = -100.0
+    fv(c("wpad", 112, 128), v("M16"), 16, 0.0, wc)
+    for k in range(2):
+        ms(c("un", k, 32, 2), UP * 256.0 ** k, 16)
+    if max(CFG["stages"]) > 1:
+        for k in range(8):
+            ms(c("un8", k, 128, 8), UP * 256.0 ** k, 16)
+            ms(c("lev", 16 * k, 16 * k + 16), 256.0 ** -k, 16)
+        for a in (128, 256):
+            fs(c("lev", a, 2 * a), c("lev", 0, a), a)
     for name, n in (("OL", 5), ("Zp", 8)):
-        for k in range(n):
-            for h in range(8):
-                iota(v(name, k, h), [[0, 240]], 0, 0, 240)
-    bias[0] = 0.0
+        iota(v(name, ALL, ALL, 1), [[0, 4 * n], [0, 16]], 0, 0, 64 * n)
+    data = (ALL, S_(0, 3, 2))
+
+    def half(name, j, k):
+        return v(name, j, k // 2, S_(k % 2, k % 2 + 2))
+
+    def pair(bank, a, x, y):
+        return c(bank, x, y, p=S_(32 * a, 32 * a + 32))
 
     def both(x):
         return {"ap": x["ap"], "r": x["r"] + [("VDx", 1), ("VDy", 1)]}
@@ -518,45 +654,55 @@ def rank_program(g, core, T, topo):
     exchange([(both(c("VD", 0, 128)), c("VD", 1664, W))], [(both(c("VD", 1408, V)), c("VD", V, 1664))], 4.0)
     for a, b in ((0, 768), (768, V), (V, W)):
         cp(c("Vg", a, b, p=p32), both(c("VD", a, b, p=p32)), b - a)
-    for t in range(RO):
+
+    def wrap(t, a, b):
         bank = "P%d" % (3 + t)
-        mm(grp(c(bank, 0, 96), [(v("Cq", t, S_(15 - q, 143 - q), p=p32), c("Vg", q, V, 16, p=p32), 96) for q in range(16)]))
-        cp(v("dvO", S_(8, 104), t), c(bank, 0, 96), 96)
+        mm(grp(c(bank, a, b), [(v("Cq", t, S_(15 - q, 143 - q), p=p32), c("Vg", 16 * a + q, 16 * b, 16, p=p32), max(64, b - a))
+                               for q in range(16)]))
+        if (t, a) == (0, 0):
+            ts(v("smallR"), c(bank, 0, 96), 7.5, AL.is_lt, 96)
+        for r, x, n in RING:
+            if a <= x < b:
+                cp(v("dvO", S_(r, r + n), t), c(bank, x, x + n), n)
     for t in range(RO):
-        bank = "P%d" % (3 + t)
-        mm(grp(c(bank, 96, 112), [(v("Cq", t, S_(15 - q, 143 - q), p=p32), c("Vg", V + q, W, 16, p=p32), 64) for q in range(16)]))
-        cp(v("dvO", S_(0, 8), t), c(bank, 96, 104), 8)
-        cp(v("dvO", S_(104, 112), t), c(bank, 104, 112), 8)
+        wrap(t, 0, 96)
+    for bank, x, a, b, r in (("P6", 0, 128, 640, 512), ("P7", 0, 640, 1152, 1024), ("P6", 0, 1152, 1408, 1536), ("P7", 0, 0, 128, 256),
+                             ("P6", 256, 1408, V, 128), ("P7", 128, V, 1664, 384), ("P7", 256, 1664, W, 0)):
+        mm(grp(c(bank, x, x + b - a), [(Ib, c("St", r, r + b - a), b - a), (v("Cq", 0, S_(15, 143), p=p32), c("Vg", a, b, p=p32), b - a)]))
+        if a != V:
+            a, x = (V, 128) if a == 1664 else (a, x)
+            ts(c("volE", a, b), c(bank, x, x + b - a), row(0), AL.max, b - a, most, AL.min)
+    for t in range(RO):
+        wrap(t, 96, 112)
     exchange([(c("Wf", 0, 128), c("Wf", 1664, W))], [(c("Wf", 1408, V), c("Wf", V, 1664))], 2.5)
+
     def scaled(a, b):
-        act(c("Wf", UB + a, UB + b), c("Wf", a, b), b - a, scale=1.0 / 256)
+        fs(c("Wf", UB + a, UB + b), c("Wf", a, b), b - a, 1.0 / 256, lend=2.0)
     for a, b in ((0, 512), (512, 1024), (1024, V), (V, W)):
         scaled(a, b)
-    exchange([(c("wall", 0, WT), c("wall", 2 * WT, 3 * WT))], [(c("wall", 0, WT), c("wall", WT, 2 * WT))], 2.5)
+    fs(c("wall", 8, WT), c("wall", WT + 8, 2 * WT), 256, 1.0 / UP)
+    fs(c("wall", WT + 8, 2 * WT), c("wall", WT + 8, 2 * WT), 256, 1.0 / UP)
+    exchange([(c("wall", WT, 2 * WT), c("wall", 3 * WT, 4 * WT))], [(c("wall", WT, 2 * WT), c("wall", 2 * WT, 3 * WT))], 2.5)
 
-    inner, left, right = (16, 96), (0, 16), (96, 112)
-
-    def spread_volumes(a, b, bank, pieces, x=0):
-        mm([(c(bank, x + q, x + 16 * (b - a), 16), v("Rq", q), c("volN", a, b), True, True, 64) for q in range(16)])
-        for (x, at, n) in pieces:
-            act(c("volE", at, at + n), c(bank, x, x + n), n)
+    def spread_volumes(a, b, bank):
+        n = 16 * (b - a)
+        mm([(c(bank, 0, n), Ib, c("St", 16 * a, 16 * b), True, False, n)] +
+           [(c(bank, q, n, 16), v("Rq", q), c("volN", a, b), False, q == 15, 64) for q in range(16)])
+        if a:
+            fs(c("volE", 16 * a - 384, 16 * b - 384), c(bank, 0, n), n, lend=1.0)
+        else:
+            for r, x, _ in RING[:4]:
+                act(c("volE", 16 * x, 16 * x + 128), c(bank, 16 * r, 16 * r + 128), 128)
 
     def lanes(t):
         last = t == RO - 1
         e = t % 2
         x0 = (STEP * t) % V // 16
-        if t == 0:
-            def qv(a, b):
-                return v("dvO", S_(a, b), 0)
-            ts(v("smallR"), qv(8, 104), 7.5, AL.is_lt, 96)
-        else:
-            def qv(a, b):
-                return c("qu", a, b)
-            tt(c("smallR", 96 - x0, 104 - x0), v("nR", t - 1, S_(8, 16)), c("thB", 8, 16), AL.is_gt, 16)
-            tt(c("smallR", 88 - x0, 96 - x0), v("nR", t - 1, S_(16, 24)), c("thB", 16, 24), AL.is_gt, 16)
+        if t:
+            tt(c("smallR", 88 - x0, 104 - x0), v("nR", t - 1, S_(8, 24)), c("thB", 8, 24), AL.is_gt, 32)
         mm([(c("P0", 0, 96), bo, v("smallR"), True, True, 96), (c("P0", 128, 224), up, v("smallR"), True, True, 96)])
-        scan(v("Cc"), c("P0", 0, 96), c("Z0", 0, 96), 0.0, AL.add, AL.add, 96)
-        na = CFG["acts"]
+        scan(v("Cc"), c("P0", 0, 96), v("Z0"), 0.0, AL.add, AL.add, 96)
+        na = CFG["acts"][t]
         for k in range(na):
             act(v("junk", k), v("Cc"), 96, AF.Sign, bias=c("biasL", k, k + 1), accum=c("acc", k, k + 1))
         for k in range(na, 8):
@@ -567,11 +713,12 @@ def rank_program(g, core, T, topo):
         if na < 8:
             ts(c("acc", na, 8), c("bo2", na, 8), -96.0, AL.add, 8)
         ts(v("x16"), v("acc"), -0.5, AL.mult, 8, 48.0, AL.add)
-        ts(c("xr", 0, 8), v("acc"), -0.5, AL.mult, 8, 48.0 + x0, AL.add)
-        ts(c("xr", 8, 16), v("acc"), 2.0 * x0 - 95.0, AL.is_lt, 8, -96.0, AL.mult)
+        fv(c("xr", 0, 8), v("acc"), 8, -0.5, 48.0 + x0)
+        if x0:
+            ts(c("xr", 8, 16), v("acc"), 2.0 * x0 - 95.0, AL.is_lt, 8, -96.0, AL.mult)
         tt(v("cmpb"), ind(v("Pw"), v("x16")), lrow, AL.is_le, 128)
-        act(v("XE"), ind(v("xtab", t), v("x16")), 128)
-        mm(grp(c("P0", 224, 232), [(I16, c("xr", 0, 8), 64), (I16, c("xr", 8, 16), 64), (Ib, v("cW"), 64)] +
+        fs(v("XE"), ind(v("xtab", t), v("x16")), 128)
+        mm(grp(c("P0", 224, 232), [(I16, c("xr", 0, 8), 64)] + [(I16, c("xr", 8, 16), 64)] * (x0 > 0) + [(Ib, v("cW"), 64)] +
                [(c("Dg", 15 - q, 143 - q), c("cmpb", q, 128, 16), 64) for q in range(16)]) +
            grp(c("P0", 232, 240), [(v("cmpb"), bo8, 64), (v("XE"), bo8, 64)]))
         ts(v("o16", e, S_(0, 8)), c("P0", 224, 232), float(W), AL.add, 8)
@@ -579,33 +726,23 @@ def rank_program(g, core, T, topo):
         scan(v("Bc", 0), v("rmask"), v("hold"), 0.0, AL.mult, AL.add, 128)
         ts(v("mm"), c("lane", 0, 32), c("Cc", 95, 96), AL.is_lt, 32)
         if t:
-            for (a, b), x in ((left, 0), (right, 16)):
-                ts(c("hh", a, b), v("nF", t - 1, S_(a, b)), 3.0, AL.min, 16)
-                tt(c("qu", a, b), c("qa", a, b), c("hh", a, b), AL.subtract, 32)
+            ts(c("hh", 0, 32), v("nF", t - 1, S_(0, 32)), 3.0, AL.min, 32)
+            tt(c("qu", 0, 32), c("qa", 0, 32), c("hh", 0, 32), AL.subtract, 64)
+            ts(c("volN", 0, 32), c("qu", 0, 32), 1.0, AL.max, 32, 16.0, AL.min)
+            spread_volumes(0, 32, "P1")
         else:
-            ts(c("volN", 16, 96), qv(16, 96), 1.0, AL.max, 80, 16.0, AL.min)
-            inner_volumes(("P6", "P7", "P6"))
-        for a, b in (left, right):
-            ts(c("volN", a, b), qv(a, b), 1.0, AL.max, 16, 16.0, AL.min)
-        spread_volumes(0, 16, "P1", [])
-        spread_volumes(96, 112, "P1", [(0, V, 128), (128, 0, 128), (256, 1408, 128), (384, 1664, 128)], 256)
+            ts(v("volN"), v("dvO", ALL, 0), 1.0, AL.max, 112, 16.0, AL.min)
         if not last:
             tt(v("qa"), v("volN"), v("dvO", ALL, t + 1), AL.add, 224)
-            ts(c("P2", 112, 224), v("qa"), -10.5, AL.add, 112, 1000.0, AL.mult)
-            ts(v("thr1"), v("qa"), -7.5, AL.add, 112)
+            fv(c("P2", 112, 224), v("qa"), 112, 1000.0, -10500.0)
+            fv(v("thr1"), v("qa"), 112, 1.0, -7.5)
             tt(v("thr1"), c("P2", 112, 224), v("thr1"), AL.max, 112)
-
-    def inner_volumes(banks_=CFG["vbank"]):
-        for (a, b), bank in zip(((16, 48), (48, 72), (72, 96)), banks_):
-            spread_volumes(a, b, bank, [(0, 16 * a - 128, 16 * (b - a))])
 
     def lists(t):
         last = t == RO - 1
         e = t % 2
-        EQ = "EQ"
         sl = lambda name, a, b: v(name, e, S_(8 * a, 8 * b))
         Gj = lambda a, b: v("G", e, S_(128 * a, 128 * b))
-        vol = lambda a, b: v("volM", e, S_(128 * a, 128 * b))
         bo = lambda k: c("bo", 8 * k, 8 * k + 8)
 
         def names(j):
@@ -617,45 +754,45 @@ def rank_program(g, core, T, topo):
         def present(a, b):
             tt(c("t40", 8 * a, 8 * b), sl("nW", a, b), sl("th", a, b), AL.mult, 16 * (b - a))
             ts(sl("nA16", a, b), c("t40", 8 * a, 8 * b), float(W), AL.add, 40)
-            act(Gj(a, b), ind(v("Gt"), sl("nA16", a, b)), 128 * (b - a))
-            act(vol(a, b), ind(v("volE"), sl("nA16", a, b)), 128 * (b - a))
+            fs(Gj(a, b), ind(v("volE"), sl("nA16", a, b)), 128 * (b - a), lend=1.0)
+            tt(sl("pre", a, b), c("t40", 8 * a, 8 * b), c("lane1", 8 * a, 8 * b), AL.subtract, 16 * (b - a))
             mm([(c("P2", 440 + 16 * (j - a), 456 + 16 * (j - a)), Gj(j, j + 1), v("hcm"), True, True, 64) for j in range(a, b)])
-            cp(v("hc", S_(a, b)), c("P2", 440, 440 + 16 * (b - a)), 48)
+            fs(v("hc", S_(a, b)), c("P2", 440, 440 + 16 * (b - a)), 48)
             if a == 4 and CFG["fast"][t]:
                 return
-            mm([(c("P1", 128 * (j - a + 1), 128 * (j - a + 2)), Gj(j, j + 1), Ib, True, True, 128) for j in range(a, b)])
-            act(v("OL", S_(a, b), ALL, mid), c("P1", 128, 128 * (b - a + 1)), 128 * (b - a), AF.Sign)
+            mm([(c("P1", 128 * (j - a + 1), 128 * (j - a + 2)), Gj(j, j + 1), selQ, True, True, 128) for j in range(a, b)])
+            fs(v("OL", S_(a, b), *data), c("P1", 128, 128 * (b - a + 1)), 128 * (b - a), relu=True)
             for k in range(8):
                 for j in range(a, b):
                     ts(v("OH", 5 * k + j), v("ring"), v("hc", j, S_(k, k + 1)), AL.is_equal, 56)
 
-        def tally(a, b):
-            return [(v("OL", j, k, S_(112 - 16 * ((k - 1) % 8), 240 - 16 * ((k - 1) % 8))), v("OH", 5 * k + j), 112)
-                    for j in range(a, b) for k in range(8)]
+        def tally(a, b, first=None):
+            out = []
+            for h in range(4):
+                out += grp(pair("P2", h, 0, 112), ([(v("cb", 0, S_(32 * h, 32 * h + 32)), first, 112)] if first else []) +
+                           [(half("OL", j, m), v("OH", 5 * ((m + 1) % 8) + j), 112) for j in range(a, b) for m in (2 * h, 2 * h + 1)])
+            return out
 
         def equal(a, b):
             n = 128 * (b - a)
             per = 512 // n
-            a0 = 0 if a == 1 else a
-            tt(sl("pre", a0, b), sl("nW", a0, b), c("lane", 8 * a0, 8 * b), AL.subtract, 16 * (b - a0))
-            tt(sl("thm", a, b), sl("th", a, b), c("thr", 8 * a, 8 * b), AL.mult, 16 * (b - a))
             for k0 in range(0, 8, per):
                 bank = "P%d" % (3 + (k0 // per) % 2)
                 mm([(c(bank, n * (k - k0), n * (k - k0 + 1)), v("selP", k), Gj(a, b), True, True, n) for k in range(k0, k0 + per)])
-                short = k0 < CFG["short"][t][a == 4]
-                if short:
-                    act(v("row", (k0 // per) % 2, S_(0, n * per)), c(bank, 0, n * per), n * per)
                 for k in range(k0, k0 + per):
                     for j in range(a, b):
                         x = n * (k - k0) + 128 * (j - a)
-                        src = v("row", (k0 // per) % 2, S_(x, x + 128)) if short else c(bank, x, x + 128)
-                        ts(v(EQ, k, S_(128 * j - 128, 128 * j)), src, v("hc", j, S_(8 + k, 9 + k)), AL.is_equal, 64 if short else 128)
-            mm(grp(c("P3", 0, n), [(c("wpad", 112 - 16 * k, 240 - 16 * k), v(EQ, k, S_(128 * a - 128, 128 * b - 128)), n) for k in range(8)]))
-            act(c("Wb", 128 * a - 128, 128 * b - 128), c("P3", 0, n), n)
+                        ts(v("EQ", k, S_(128 * j - 128, 128 * j)), c(bank, x, x + 128), v("hc", j, S_(8 + k, 9 + k)), AL.is_equal, 128)
+
+        def first(a, b):
+            n = 128 * (b - a)
+            a0 = 0 if a == 1 else a
+            mm(grp(c("P3", 0, n), [(c("wpad", 112 - 16 * k, 240 - 16 * k), v("EQ", k, S_(128 * a - 128, 128 * b - 128)), n) for k in range(8)]))
+            fs(c("Wb", 128 * a - 128, 128 * b - 128), c("P3", 0, n), n)
             mm(grp(c("P4", 0, 8 * (b - a)), [(c("Dq", 15 - q, 143 - q), c("Wb", 128 * a - 128 + q, 128 * b - 128, 16), 64) for q in range(16)]))
-            tt(c("ff", 8 * a, 8 * b), c("P4", 0, 8 * (b - a)), sl("thm", a, b), AL.is_lt, 32)
+            tt(c("ff", 8 * a, 8 * b), c("P4", 0, 8 * (b - a)), c("thr", 8 * a, 8 * b), AL.is_lt, 32)
             if a0 < a:
-                cp(c("ff", 0, 8), sl("th", 0, 1), 8)
+                fv(c("ff", 0, 8), sl("th", 0, 1), 8)
             f = c("ff", 8 * a0, 8 * b)
             tt(f, f, sl("pre", a0, b), AL.mult, 64)
             tt(f, f, c("dump", 8 * a0, 8 * b), AL.add, 64)
@@ -664,31 +801,35 @@ def rank_program(g, core, T, topo):
         names(0)
         for j in range(1, 5):
             off = sl("o16", j - 1, j)
-            act(v("raw"), ind(v("ntb"), off), 128)
-            cp(v("bn"), v("b16", e, j - 1), 128)
+            fs(v("raw"), ind(v("ntb"), off), 128)
+            ts(v("bn"), v("b16", e, j - 1), 1.0, AL.mult, 64)
             cuts = CFG["split"][t]
             for a, b in zip(cuts, cuts[1:]):
-                either(c("Vg", 16 * a, 16 * b), ind(v("volE"), v("b16", e, j - 1, S_(a, b))), 16 * (b - a), lend=CFG["lendv"][t])
+                fs(c("Vg", 16 * a, 16 * b), ind(v("volE"), v("b16", e, j - 1, S_(a, b))), 16 * (b - a), lend=CFG["lendv"][t])
             level(j - 1)
-            mm([(c("P0", 0, 128), v("bn"), If, True, True, 512)])
-            mm(grp(c("P1", 0, 128), [(v("raw"), Iup, 512), (v("bn"), Idown, 512)]))
-            rest = grp(c("P0", 129, 384, 2), [(v("bn"), If, 512), (Ib, top, 128)] + [(negI, v("eq", i), 128) for i in range(j)])
-            mm(rest[:2])
+            named = c("P1", 128, 256) if CFG["eqlast"][j - 1] else c("P0", 0, 128)
+            mm([(named, v("bn"), v("Ih", 0), True, True, 128)])
+            mm(grp(c("P1", 0, 128), [(v("raw"), If, 512), (v("bn"), v("Ih", 1), 128)]))
+            odd, late = c("P0", 129, 384, 2), bool(CFG["eqlast"][j - 1])
+            listed = [(odd, negI, v("eq", i), False, late and i == j - 1, 128) for i in range(j)]
+            turn = [(c("P0", 128 + 2 * k, 384, 32), c("Vg", k, 2048, 16), I8, False, not late and k == 15, 64) for k in range(16)]
+            mm([(c("P0", 128, 384), Ib, v("top"), True, False, 256), (odd, v("bn"), v("Ih", 0), False, False, 128)])
             for i in range(j):
-                tt(v("eq", i), c("P0", 0, 128), v("Bc", i), AL.is_equal, 128)
-            act(c("A2", 1, 256, 2), c("P1", 0, 128), 128)
-            mm(rest[2:])
+                tt(v("eq", i), named, v("Bc", i), AL.is_equal, 128)
+            fs(c("A2", 1, 256, 2), c("P1", 0, 128), 128, 2.0 ** 16)
+            if not late:
+                mm(listed)
             held = v("Bc", j - 1, S_(0, 128, 16))
             if j == 4:
-                act(v("XE"), ind(v("volE"), off), 128)
-                mm(grp(c("P2", 224, 232), [(vol(i, i + 1), I8, 64) for i in range(3)] + [(v("XE"), I8, 64)]) +
-                   [(c("P2", 232, 240), vol(0, 1), I8, True, True, 64)])
+                fs(v("XE"), ind(v("volE"), off), 128)
+                mm(grp(c("P2", 224, 232), [(Gj(i, i + 1), I8, 64) for i in range(3)] + [(v("XE"), I8, 64)]) +
+                   [(c("P2", 232, 240), Gj(0, 1), I8, True, True, 64)])
                 ts(bo(0), c("P2", 232, 240), 0.5, AL.is_lt, 8, 4095.0 * 4096, AL.mult)
                 ts(bo(1), c("P2", 224, 232), 43.5, AL.is_gt, 8, 4095.0 * 4096, AL.mult)
                 tt(bo(2), bo(0), bo(1), AL.add, 16)
                 tt(bo(4), bo(2), held, AL.add, 16)
                 if CFG["fast"][t]:
-                    ts(bo(3), bo(2), 4095.5, AL.add, 8)
+                    fv(bo(3), bo(2), 8, 1.0, 4095.5)
             cuts = CFG["batch"][t]
             part("marks", t)
             if j in cuts:
@@ -698,127 +839,109 @@ def rank_program(g, core, T, topo):
                 tt(c("ne", 8 * max(a, 1), 8 * j), sl("nW", max(a, 1), j), sl("nW", max(a, 1) - 1, j - 1), AL.not_equal, 32)
                 tt(sl("th", a, j), c("ne", 8 * a, 8 * j), c("mm", 8 * a, 8 * j), AL.mult, 48)
                 present(a, j)
-            if j - 1 in CFG["ebatch"][t][1:]:
-                ecuts = CFG["ebatch"][t]
-                part("equal", t)
-                equal(ecuts[ecuts.index(j - 1) - 1], j - 1)
-            part("steps", t)
+                if j == 3 and CFG["early"][t]:
+                    mm(tally(0, 3))
+                    fs(v("nA"), c("P2", 0, 112), 112)
+            part("step%d" % j, t)
             if j == 4:
                 held = bo(4)
-            w = CFG["turn"]
-            for a in range(0, 128, w):
-                mm([(c("P0", 128 + 2 * k, 384, 32, p=S_(a, a + w)), c("Vg", 16 * a + k, 16 * (a + w), 16), I8, True, True, min(w, 64))
-                    for k in range(16)])
+            mm(turn)
+            if late:
+                mm(listed)
             scan(v("KS"), v("A2"), c("P0", 128, 384), 0.0, AL.mult, AL.add, 256)
             scan(v("SC"), v("rmask"), c("KS", 1, 256, 2), 0.0, AL.mult, AL.max, 128)
-            ka = v("ka")
-            tt(ka, c("SC", 15, 128, 16), held, AL.max, 16)
-            ts(v("kb"), ka if j == 4 else c("SC", 15, 128, 16), BIG, AL.add, 8, -BIG, AL.add)
+            ka, won = v("ka"), c("SC", 15, 128, 16)
+            tt(ka, won, held, AL.max, 16)
+            ts(v("kb"), ka if j == 4 else won, BIG, AL.add, 8, -BIG, AL.add)
             tt(c("hold", 0, 128, 16), ka, v("kb"), AL.subtract, 16)
             if j == 4 and CFG["fast"][t]:
                 for x in (0, 3):
-                    tt(v("dig", 0, S_(x, 56, 7)), c("SC", 15, 128, 16), held, AL.max, 16)
-                tt(bo(5), c("SC", 15, 128, 16), bo(3), AL.is_gt, 16)
+                    tt(v("dig", 0, S_(x, 56, 7)), won, held, AL.max, 16)
+                tt(bo(5), won, bo(3), AL.is_gt, 16)
                 scan(v("dig", 2), v("dig", 1), v("dig", 0), 0.0, AL.mult, AL.add, 56)
                 tt(bo(6), v("dig", 2, S_(3, 56, 7)), v("dig", 2, S_(6, 56, 7)), AL.subtract, 16)
                 for k in range(8):
                     ts(v("OH", 5 * k + 4), v("ring16"), v("dig", 2, S_(7 * k + 6, 7 * k + 7)), AL.is_equal, 56)
                 for k in range(8):
-                    ts(v("OL", 4, k, mid), v("q16"), c("bo", 48 + k, 49 + k), AL.is_equal, 16, c("bo", 40 + k, 41 + k), AL.mult)
-            scan(v("Bc", j), v("rmask"), v("hold"), 0.0, AL.mult, AL.add, 128)
-            tt(v("MK"), qmask, v("Bc", j), AL.mult, 128)
-            mm(grp(c("P0", 0, 8), [(Ib, v("cW"), 64), (v("MK"), v("cm"), 256)]))
+                    m = (k - 1) % 8
+                    ts(v("OL", 4, m // 2, 2 * (m % 2)), v("q16"), c("bo", 48 + k, 49 + k), AL.is_equal, 16, c("bo", 40 + k, 41 + k), AL.mult)
+            scan(v("MK"), v("qmask"), v("hold"), 0.0, AL.mult, AL.add, 128)
+            if j < 4:
+                scan(v("Bc", j), v("rmask"), v("hold"), 0.0, AL.mult, AL.add, 128)
+            mm(grp(c("P0", 0, 8), [(Ib, v("cW"), 64), (v("hold"), v("cmh", 1), 64), (v("MK"), v("cmh", 0), 64)]))
             ts(sl("o16", j, j + 1), c("P0", 0, 8), float(W), AL.add, 8)
+            ops[-1]["due"] = CFG["duel"][t] + (4 - j) * CFG["pace"][t]
             if j == 4:
                 tt(sl("th", 4, 5), c("P0", 0, 8), sl("nW", 3, 4), AL.not_equal, 8)
             if j > 2:
                 cp(sl("nW", j, j + 1), c("P0", 0, 8), 8)
             names(j)
-        level(4)
-        mm(grp(c("P2", 0, 112), tally(0, 4)))
-        cp(v("nA"), c("P2", 0, 112), 112)
-        tt(c("es", 0, 8), sl("th", 1, 2), sl("th", 2, 3), AL.add, 16)
-        tt(c("es", 0, 8), c("es", 0, 8), sl("th", 3, 4), AL.add, 16)
-        ts(c("es", 0, 8), c("es", 0, 8), 0.0625, AL.mult, 8)
+        if CFG["stages"][t] == 1:
+            level(4)
+        mm(tally(3, 4, v("nA")) if CFG["early"][t] else tally(0, 4))
+        fs(v("nA"), c("P2", 0, 112), 112)
         part("equal", t)
-        equal(CFG["ebatch"][t][-2], 4)
+        cuts = CFG["ecut"][t]
+        for a, b in zip(cuts, cuts[1:]):
+            equal(a, b)
+        first(1, 4)
         part("counts", t)
         if not CFG["fast"][t]:
             present(4, 5)
-        mm(grp(c("P2", 0, 112), [(Ib, v("nA"), 112)] + tally(4, 5)))
-        cp(c("nS", 0, 16), c("P2", 0, 16), 16)
-        cp(c("nS", 16, 32), c("P2", 96, 112), 16)
-        exchange([(c("nS", 0, 16), v("nR", t, S_(16, 32)))], [(c("nS", 16, 32), v("nR", t, S_(0, 16)))], 2.2)
-        cp(v("nF", t, S_(16, 96)), c("P2", 16, 96), 80)
+        mm(tally(4, 5, v("nA")))
+        cp(v("nS"), c("P2", 0, 32), 32)
+        exchange([(c("nS", 16, 32), v("nR", t, S_(0, 16)))], [(c("nS", 0, 16), v("nR", t, S_(16, 32)))], 2.2)
+        cp(v("nF", t, S_(32, 112)), c("P2", 32, 112), 80)
         if not last:
             x0 = (STEP * (t + 1)) % V // 16
-            tt(c("smallR", 0, 88 - x0), c("P2", 8 + x0, 96), c("thr1", 8 + x0, 96), AL.is_gt, 64)
-            tt(c("smallR", 104 - x0, 96), c("P2", 16, 8 + x0), c("thr1", 16, 8 + x0), AL.is_gt, 80)
-            tt(c("thB", 8, 16), c("thr1", 8, 16), c("nS", 8, 16), AL.subtract, 16)
-            tt(c("thB", 16, 24), c("thr1", 96, 104), c("nS", 16, 24), AL.subtract, 16)
-            ts(c("hh", 16, 96), c("P2", 16, 96), 3.0, AL.min, 80)
-            tt(c("qu", 16, 96), c("qa", 16, 96), c("hh", 16, 96), AL.subtract, 160)
+            tt(c("smallR", 0, 88 - x0), c("P2", 24 + x0, 112), c("thr1", 24 + x0, 112), AL.is_gt, 64)
+            tt(c("smallR", 104 - x0, 96), c("P2", 32, 24 + x0), c("thr1", 32, 24 + x0), AL.is_gt, 80)
+            ts(c("hh", 32, 112), c("P2", 32, 112), 3.0, AL.min, 80)
+            tt(c("thB", 8, 24), c("thr1", 8, 24), c("nS", 8, 24), AL.subtract, 32)
+            tt(c("qu", 32, 112), c("qa", 32, 112), c("hh", 32, 112), AL.subtract, 160)
         if CFG["fast"][t]:
             present(4, 5)
-        ts(c("es", 8, 16), sl("th", 4, 5), 0.0625, AL.mult, 8)
-        tt(v("ev", e), c("es", 0, 8), c("es", 8, 16), AL.add, 16)
-        part("equal", t)
+        part("equal4", t)
         equal(4, 5)
+        first(4, 5)
         part("counts", t)
         if not last:
-            ts(c("volN", 16, 96), c("qu", 16, 96), 1.0, AL.max, 80, 16.0, AL.min)
-            inner_volumes()
-        own = lambda a, b: grp(c("P2", 344 + a, 344 + b), [(shmK, v("nF", t, S_(8 + a, 8 + b)), 80), (Ib, c("x16r", a, b), 80),
-                                                           (Ib, c("qtab", a, b), 80)])
-        mm([(c("P2", 240, 320), shm, v("nF", t, S_(16, 96)), True, True, 80)] + own(8, 88))
+            ts(c("volN", 32, 112), c("qu", 32, 112), 1.0, AL.max, 80, 16.0, AL.min)
+            for (a, b), bank in zip(((32, 64), (64, 96), (96, 112)), CFG["vbank"]):
+                spread_volumes(a, b, bank)
+        mm([(c("P2", 240, 320), shm, v("nF", t, S_(32, 112)), True, True, 80)])
         ts(v("nOff", e, S_(8, 88)), c("P2", 240, 320), 7.0, AL.add, 80)
-        ts(v("sel", e, S_(8, 88)), c("P2", 352, 432), float(W), AL.min, 80)
-        tt(v("nF", t, S_(0, 16)), c("nS", 0, 16), v("nR", t, S_(0, 16)), AL.add, 32)
-        tt(v("nF", t, S_(96, 112)), c("nS", 16, 32), v("nR", t, S_(16, 32)), AL.add, 32)
+        tt(v("nF", t, S_(0, 32)), v("nS"), v("nR", t), AL.add, 64)
 
     def border_counts(t):
-        last = t == RO - 1
-        e = t % 2
-        own = lambda a, b: grp(c("P2", 344 + a, 344 + b), [(shmK, v("nF", t, S_(8 + a, 8 + b)), 64), (Ib, c("x16r", a, b), 64),
-                                                           (Ib, c("qtab", a, b), 64)])
-        mm([(c("P2", 232, 240), shm, v("nF", t, S_(8, 16)), True, True, 64),
-            (c("P2", 320, 328), shm, v("nF", t, S_(96, 104)), True, True, 64),
-            (c("P2", 328, 336), shm, v("nF", t, S_(0, 8)), True, True, 64),
-            (c("P2", 336, 344), shm, v("nF", t, S_(104, 112)), True, True, 64)] + own(0, 8) + own(88, 96))
-        ts(v("sel", e, S_(0, 8)), c("P2", 344, 352), float(W), AL.min, 8)
-        ts(v("sel", e, S_(88, 96)), c("P2", 432, 440), float(W), AL.min, 8)
-        ts(v("nOff", e, S_(0, 8)), c("P2", 232, 240), 7.0, AL.add, 8)
-        ts(v("nOff", e, S_(88, 96)), c("P2", 320, 328), 7.0, AL.add, 8)
-        if not last:
-            ts(v("nOff", e, S_(96, 104)), c("P2", 328, 336), 7.0 + WT, AL.add, 8)
-            ts(v("nOff", e, S_(104, 112)), c("P2", 336, 344), 7.0 + 2 * WT, AL.add, 8)
+        out = []
+        for k, r in enumerate((8, 24, 0, 16)):
+            out += grp(c("P2", 320 + 8 * k, 328 + 8 * k), [(shm, v("nF", t, S_(r, r + 8)), 64), (Ib, c("wb", 8 * k, 8 * k + 8), 64)])
+        mm(out)
+        ts(v("nOff", t % 2, S_(88, 120)), c("P2", 320, 352), 7.0, AL.add, 32)
 
     def fields(t):
         last = t == RO - 1
         e = t % 2
-        EQ = "EQ"
-        uw = c("Wf", 0, UB)
+        uw = c("Wf", 0, W)
         sl = lambda name, a, b: v(name, e, S_(8 * a, 8 * b))
-        dma("sync", c("S", V, W), v("Z0"), 3.0)
-        for a, b in ((8, 48), (48, 88), (0, 8), (88, 96)):
-            act(c("S", 16 * a, 16 * b), ind(uw, v("sel", e, S_(a, b))), 16 * (b - a))
         part("mean", t)
-        act(c("um", 0, 512), ind(uw, sl("o16", 0, 4)), 512)
-        act(c("um", 512, 640), ind(uw, sl("o16", 4, 5)), 128)
-        mm(grp(c("P6", 256, 288), [(c("Dq", 15 - q, 143 - q), v("volM", e, S_(q, 512, 16)), 64) for q in range(16)]))
-        cp(c("Zq", 0, 32), c("P6", 256, 288), 32)
+        fs(c("um", 0, 512), ind(uw, sl("o16", 0, 4)), 512, lend=CFG["lend"][t])
+        fs(c("um", 512, 640), ind(uw, sl("o16", 4, 5)), 128)
+        mm(grp(c("P6", 256, 288), [(c("Dq", 15 - q, 143 - q), v("G", e, S_(q, 512, 16)), 64) for q in range(16)]))
+        fs(c("Zq", 0, 32), c("P6", 256, 288), 32)
         mm(grp(c("P6", 288, 296), [(Ib, c("Zq", 8 * i, 8 * i + 8), 64) for i in range(4)] +
-               [(c("Dq", 15 - q, 143 - q), v("volM", e, S_(512 + q, 640, 16)), 64) for q in range(16)]))
-        mm([(c("P6", 128 + q, 256, 16), v("Rq", q), v("ev", e), True, True, 64) for q in range(16)])
+               [(c("Dq", 15 - q, 143 - q), v("G", e, S_(512 + q, 640, 16)), 64) for q in range(16)]))
+        mm(grp(c("P6", 128, 256), [(selE, v("G", e, S_(128 * j, 128 * j + 128)), 128) for j in range(1, 5)]))
         ts(v("z16", e), c("P6", 288, 296), 7.0, AL.add, 8)
-        act(v("wZ"), ind(c("wall", 0, WT), v("z16", e)), 128)
-        mm([(v("P5"), Ib, v("volM", e, S_(0, 512)), True, True, 512)])
+        fs(v("wZ"), ind(c("wall", 0, WT), v("z16", e)), 128, UP * UP)
+        mm([(v("P5"), selV, v("G", e, S_(0, 512)), True, True, 512)])
         for a in (0, 256):
             tt(c("prod", a, a + 256), c("P5", a, a + 256), c("um", a, a + 256), AL.mult, 256)
-        mm([(c("P7", 128, 256), Ib, v("volM", e, S_(512, 640)), True, True, 128)] +
+        mm([(c("P7", 128, 256), selV, v("G", e, S_(512, 640)), True, True, 128)] +
            grp(c("P7", 256, 384), [(negf, c("um", 0, 128), 512), (If, c("um", 512, 640), 512)]))
         tt(c("prod", 512, 640), c("P7", 128, 256), c("um", 512, 640), AL.mult, 128)
-        act(v("Dd"), c("P7", 256, 384), 128)
+        fs(v("Dd"), c("P7", 256, 384), 128, UP)
         mm(grp(c("P7", 384, 512), [(If, c("prod", 128 * j, 128 * j + 128), 512) for j in range(5)]))
         tt(v("De"), c("P6", 128, 256), v("Dd"), AL.mult, 128)
         tt(v("Mm"), c("P7", 384, 512), v("wZ"), AL.mult, 128)
@@ -834,175 +957,89 @@ def rank_program(g, core, T, topo):
             scan(v("Omax", back(o, o + n)), v("Ug", back(a, a + 2 * n - 1, 2)), v("Ug", back(a + 1, a + 2 * n, 2)), 0.0, AL.max, AL.max, n)
 
         part("bounds", t)
-        for j in range(5):
-            cuts = CFG["per"][t] if j < 4 else CFG["per4"][t]
+        m = 6 - CFG["stages"][t]
+        for j in range(m):
+            cuts = CFG["per"][t]
             for a, b in zip(cuts, cuts[1:]):
-                x = ind(c("Wf", 0, UB + W), v("b16", e, j, S_(a, b)))
-                either(c("Ug", 80 * a + j, 80 * b, 5), x, 16 * (b - a), lend=CFG["lend"][t])
+                fs(c("Ug", 16 * m * a + j, 16 * m * b, m), ind(v("Wf"), v("b16", e, j, S_(a, b))), 16 * (b - a), lend=CFG["lend"][t])
+        part("scans", t)
         for i in range(0, 128, 2):
-            bound(80 * i, 80, 40 * (i % 32))
-            if i % 32 == 30:
-                tt(c("Rlo", i - 30, i + 2), c("Omin", 39, 1280, 40), v("un"), AL.mult, 64)
-                tt(c("Rhi", i - 30, i + 2), c("Omax", 0, 1280, 40), v("un"), AL.mult, 64)
+            bound(16 * m * i, 16 * m, 8 * m * (i % 32))
+            if i % 32 == 30 and CFG["unS"][t]:
+                for h in range(2):
+                    fs(c("Rlo", i - 30 + h, i + 2, 2), c("Omin", 8 * m * (h + 1) - 1, 256 * m, 16 * m), 16, UP * 256.0 ** h)
+                    fs(c("Rhi", i - 30 + h, i + 2, 2), c("Omax", 8 * m * h, 256 * m, 16 * m), 16, UP * 256.0 ** h)
+            elif i % 32 == 30:
+                tt(c("Rlo", i - 30, i + 2), c("Omin", 8 * m - 1, 256 * m, 8 * m), v("un"), AL.mult, 64)
+                tt(c("Rhi", i - 30, i + 2), c("Omax", 0, 256 * m, 8 * m), v("un"), AL.mult, 64)
+        if m == 4:
+            part("late", t)
+            for a in range(0, 128, 32):
+                tt(c("Ug", 8192 + 16 * a, 8704 + 16 * a), ind(uw, v("b16", e, 4, S_(a, a + 32))), v("lev"), AL.mult, 512)
+            for i in range(0, 128, 8):
+                bound(8192 + 16 * i, 64, 1280 + 8 * i)
+            for o, src, x, y, f in (("Rlo", "Omin", 1287, 256, AL.min), ("Rhi", "Omax", 1280, 384, AL.max)):
+                tt(c("P6", y, y + 128), c(src, x, 2304, 8), v("un8"), AL.mult, 256)
+                tt(v(o), c("P6", y, y + 128), v(o), f, 128)
         part("sums", t)
-        sw = c("S", 0, 1920)
+        sw = c("Wf", 0, UB)
         for j in (1, 2, 0, 3, 4):
-            ej = c("ec", 128 * j, 128 * j + 128)
             x = c("P5", 128 * j - 128, 128 * j) if j else c("P7", 0, 128)
             tt(x, x, v("Rlo"), AL.max, 128)
-            tt(ej, x, v("Rhi"), AL.min, 128)
-        for pair, bank in (((1, 2), "P3"), ((3, 4), "P4")):
+            tt(c("ec", 128 * j, 128 * j + 128), x, v("Rhi"), AL.min, 128)
+        for two, bank in zip(((1, 2), (3, 4)), ("P0", "P1") if last else ("P3", "P4")):
             turned = lambda j: c(bank, 128 * (j % 2), 128 * (j % 2) + 128)
-            for j in pair:
+            for j in two:
                 mm([(turned(j), c("ec", 128 * j, 128 * j + 128), If, True, True, 512)])
-            for j in pair:
-                act(v("Zp", 2 * j - 2, ALL, mid), turned(j), 128)
-            for j in pair:
-                tt(v("Zp", 2 * j - 1, ALL, mid), turned(j), v("Zp", 2 * j - 2, ALL, mid), AL.subtract, 128)
+            for j in two:
+                (cp if CFG["hiV"][t] else act)(v("Zp", 2 * j - 2, *data), turned(j), 128)
+            for j in two:
+                tt(v("Zp", 2 * j - 1, *data), turned(j), v("Zp", 2 * j - 2, *data), AL.subtract, 128)
         for j in range(1, 5):
             zh, zl, bank = 2 * j - 2, 2 * j - 1, "P%d" % (7 - j % 2)
-            mm(grp(c(bank, 0, 128), [(v("Zp", z, k, S_(112 - 16 * k, 240 - 16 * k)), v(EQ, k, S_(128 * j - 128, 128 * j)), 128)
-                                     for z in (zh, zl) for k in range(8)]))
-            act(v("Ss", j - 1), c(bank, 0, 128), 128)
+            for h in range(4):
+                mm(grp(pair(bank, h, 0, 128), [(half("Zp", z, k), v("EQ", k, S_(128 * j - 128, 128 * j)), 128)
+                                               for z in (zh, zl) for k in (2 * h, 2 * h + 1)]))
+            fs(v("Ss", j - 1), c(bank, 0, 128), 128)
         for j in range(5):
             off = sl("off16", j, j + 1)
-            if j == 0:
-                cp(ind(sw, off), c("ec", 0, 128), 128)
-            else:
+            if j:
                 tt(v("tg", j - 1), ind(sw, off), v("Ss", j - 1), AL.add, 128)
-                cp(ind(sw, off), v("tg", j - 1), 128)
+            put(ind(sw, off), v("tg", j - 1) if j else c("ec", 0, 128), CFG["silu"][t])
         Rb = "Rb%d" % t
         if last:
-            exchange([(c("S", V, 1664), c(Rb, 128, 256))], [(c("S", 1664, W), c(Rb, 0, 128))], 2.6)
+            exchange([(c("Wf", V, 1664), c(Rb, 128, 256))], [(c("Wf", 1664, W), c(Rb, 0, 128))], 2.6)
         else:
-            exchange([(c("S", V, 1664), c(Rb, 128, 256)), (c("S", 0, 128), c(Rb, 384, 512))],
-                     [(c("S", 1664, W), c(Rb, 0, 128)), (c("S", 1408, V), c(Rb, 256, 384))], 3.0)
+            exchange([(c("Wf", V, 1664), c(Rb, 128, 256)), (c("Wf", 0, 128), c(Rb, 384, 512))],
+                     [(c("Wf", 1664, W), c(Rb, 0, 128)), (c("Wf", 1408, V), c(Rb, 256, 384))], 3.0)
         end = 96 if last else 112
+        part("weigh", t)
 
-        def weigh(a, b, src):
-            tt(c("Wf", 16 * a, 16 * b), ind(v("wall"), v("nOff", e, S_(a, b))), src, AL.mult, 16 * (b - a))
+        def weigh(a, b, src, x):
+            tt(c("Wf", 16 * a, 16 * b), ind(v("wall"), v("nOff", e, S_(x, x + b - a))), src, AL.mult, 16 * (b - a))
+            ops[-1]["due"] = CFG["due"][t]
             if last:
                 dma("sync", v("y", S_(16 * a, 16 * b)), c("Wf", 16 * a, 16 * b), 2.0 + (b - a) * 0.03)
             else:
                 scaled(16 * a, 16 * b)
         n = 16 * end - 1280
-        mm([(c("P5", 0, 128), If, c("S", 0, 128), True, True, 512)] +
-           [(c("P5", a, a + 128), If, c("S", 1280 + a, 1408 + a), True, True, 512) for a in range(128, n, 128)])
+        mm([(c("P5", 0, 128), If, c("Wf", 0, 128), True, True, 512)] +
+           [(c("P5", a, a + 128), If, c("Wf", 1280 + a, 1408 + a), True, True, 512) for a in range(128, n, 128)])
         cuts = CFG["weigh"]
         for a, b in zip(cuts, cuts[1:]):
-            weigh(a, b, c("S", 16 * a, 16 * b))
+            weigh(a, b, c("Wf", 16 * a, 16 * b), a)
         tt(c(Rb, 0, n), c("P5", 0, n), c(Rb, 0, n), AL.add, n)
-        weigh(88, end, c(Rb, 128, n))
-        weigh(0, 8, c(Rb, 0, 128))
+        weigh(88, end, c(Rb, 128, n), 88)
+        weigh(0, 8, c(Rb, 0, 128), 112)
 
-    steps = [(lanes, 0), (lists, 0), (lanes, 1), (fields, 0), (lists, 1), (lanes, 2), (fields, 1), (lists, 2), (fields, 2)]
-    for k, (f, t) in enumerate(steps):
-        part("lanes" if f is lanes else "steps" if f is lists else "start", t)
+    for f, t in [(lanes, 0), (lists, 0), (lanes, 1), (fields, 0), (lists, 1), (lanes, 2), (fields, 1), (lists, 2), (fields, 2)]:
+        part("lanes" if f is lanes else "step0" if f is lists else "start", t)
         if f is fields:
             border_counts(t)
         f(t)
 
-    n = len(ops)
     if "order" not in PLAN:
-        lat_x, lat_s, window = CFG["lat"]
-        pred = [[(d, 0) for d in o["deps"]] + [(d, 1) for d in o["war"]] + [(d, 2) for d in o["order"]] for o in ops]
-        succ = [[] for _ in range(n)]
-        for i in range(n):
-            for d, kind in pred[i]:
-                succ[d].append((i, kind))
-
-        def wait(d, ed, e, kind):
-            if ed != e or ops[d]["k"] != "c":
-                return lat_x
-            return lat_s if kind == 0 or (kind == 1 and CFG["same"]) else 0.0
-
-        def schedule(prio, before, after, eng, back):
-            left_ = [len(x) for x in before]
-            ready, rt, fin, free, order = {}, [None] * n, [0.0] * n, {}, []
-            eng, idle = list(eng), [0]
-
-            def enter(i):
-                rt[i] = {}
-                for e in ([eng[i]] if back else ops[i]["alt"]):
-                    rt[i][e] = max([fin[d] + (wait(i, e, eng[d], k) if back else wait(d, eng[d], e, k)) for d, k in before[i]] + [0.0])
-                    ready.setdefault(e, []).append(i)
-            for i in range(n):
-                if left_[i] == 0:
-                    enter(i)
-            while len(order) < n:
-                t0, e = min((max(min(rt[i][e] for i in lst), free.get(e, 0.0)), e) for e, lst in ready.items() if lst)
-                rank_ = lambda k: prio[k] - (ops[k]["lend"] if e != ops[k]["e"] and not back else 0.0)
-                now = sorted([k for k in ready[e] if rt[k][e] <= t0 + window], key=rank_, reverse=True)
-                i = now[0]
-                look, gap = (CFG["lookt"], CFG["gapt"]) if e == "tensor" else (CFG["look"], CFG["gap"])
-                if look * ops[i]["alt"][e][0] > window:
-                    bar, far = rank_(i) + gap, t0 + look * ops[i]["alt"][e][0]
-                    soon, front = {}, []
-                    for x, lst in ready.items():
-                        for k in lst:
-                            if prio[k] > bar and rt[k][x] < far and (back or x == ops[k]["e"]):
-                                soon[k] = max(rt[k][x], free.get(x, 0.0) if x != e else 0.0)
-                                front.append(k)
-                    due = [(soon[k], k) for k in front if e in rt[k] and rt[k][e] > t0 + window and rank_(k) > bar]
-                    while front:
-                        k = front.pop()
-                        for s, kind in after[k]:
-                            if s not in soon and prio[s] > bar and all(p in soon or rt[p] == {} for p, _ in before[s]):
-                                at = max((soon[p] + ops[p]["d"] if p in soon else fin[p]) + (lat_s if eng[p] == eng[s] else lat_x)
-                                         for p, _ in before[s])
-                                if at < far:
-                                    soon[s] = at
-                                    front.append(s)
-                                    if (eng[s] if back else ops[s]["e"]) == e:
-                                        due.append((max(at, t0 + 0.05), s))
-                    if due:
-                        at = min(due)[0]
-                        fit = [k for k in now if t0 + look * ops[k]["alt"][e][0] <= at]
-                        if not fit and idle[0] < 30:
-                            idle[0] += 1
-                            free[e] = max(min(at, t0 + 0.2), t0 + 0.05)
-                            continue
-                        i = (fit or now)[0]
-                idle[0] = 0
-                at_i = rt[i]
-                rt[i] = {}
-                for x in at_i:
-                    ready[x].remove(i)
-                o = ops[i]
-                eng[i] = e
-                d = o["alt"][e][0]
-                hold = d if o["k"] == "c" else (0.0 if e == "ext" else (0.1 if o["k"] == "dma" else 0.5))
-                st = max(t0, at_i[e])
-                if back:
-                    st = max(at_i[e], t0 - (d - hold))
-                fin[i] = st + d
-                free[e] = fin[i] if back else st + hold
-                order.append(i)
-                for s, k in after[i]:
-                    left_[s] -= 1
-                    if left_[s] == 0:
-                        enter(s)
-            return max(fin), fin, order, eng
-
-        eng = [o["e"] for o in ops]
-        tail = [0.0] * n
-        for i in range(n - 1, -1, -1):
-            tail[i] = ops[i]["d"] + max([tail[s] + wait(i, eng[i], eng[s], k) for s, k in succ[i]] + [0.0])
-        best = None
-        for turn in range(CFG["turns"]):
-            shake = CFG["shake"] if turn >= CFG["plain"] else 0.0
-            if shake and turn % 3 == 0:
-                tail, eng = best[4], best[3]
-            prio = [x + o["b"] - CFG["own"] * o["d"] + shake * ((k * 7919 + turn * 104729) % 1009) / 1009.0
-                    for k, (x, o) in enumerate(zip(tail, ops))]
-            span, fin, order, eng = schedule(prio, pred, succ, eng, False)
-            STATS.setdefault("spans", []).append(round(span, 1))
-            tail = schedule(fin, succ, pred, eng, True)[1]
-            if best is None or span < best[0]:
-                best = (span, fin, order, eng, tail)
-        span, fin, PLAN["order"], PLAN["eng"] = polish(ops, best[2], best[3], lat_x, lat_s)
-        STATS.update({"span": span, "n": n, "fin": fin, "ops": ops})
-
+        PLAN["order"], PLAN["eng"] = plan(ops)
     queue = {"pool": g, "vector": g.vector, "scalar": g.scalar, "tensor": g.tensor, "sync": g.sync}
     token, count, seen, n_d = {}, {}, {}, 0
     for i in PLAN["order"]:
@@ -1012,9 +1049,7 @@ def rank_program(g, core, T, topo):
             token[i] = o["k"]
             continue
         need = {}
-        for d in o["deps"] | o["war"]:
-            if d not in o["deps"] and not CFG["same"] and PLAN["eng"][d] == e and ops[d]["k"] == "c":
-                continue
+        for d in o["deps"]:
             s, val = token[d]
             need[s] = max(need.get(s, 0), val)
         for s in sorted(need):
@@ -1032,9 +1067,9 @@ def rank_program(g, core, T, topo):
             n_d += 1
         else:
             token[i] = o["k"]
-    top = {}
+    most_ = {}
     for s, val in token.values():
-        top[s] = max(top.get(s, 0), val)
-    for s in sorted(top):
-        if seen.get(("pool", s), 0) < top[s]:
-            g.wait_ge(T.sem[s], top[s])
+        most_[s] = max(most_.get(s, 0), val)
+    for s in sorted(most_):
+        if seen.get(("pool", s), 0) < most_[s]:
+            g.wait_ge(T.sem[s], most_[s])

import math
import numpy as np
from concourse.bass import DstId, RemoteDMATransfer
from concourse.mybir import AluOpType, ActivationFunctionType, AxisListType

AL = AluOpType
AF = ActivationFunctionType
V, W, RO, STEP = 1536, 1792, 3, 1344
F, B, H, I, U16 = "float32", "bfloat16", "float16", "int32", "uint16"
BIG = 1.5 * 2.0 ** 35
UB = W + 136
TOP = 16 * 4096.0
WT = 264
UP = 2.0 ** 32
RING = ((0, 104, 8), (8, 88, 8), (16, 0, 8), (24, 96, 8), (32, 8, 80))
CFG = {
    "split": ((0, 32, 64, 96, 128),) * 3,
    "per": ((0, 32, 64, 96, 128),) * 3,
    "fast": (1, 1, 0), "weigh": (8, 48, 88), "est": 1, "stages": (1, 1, 1), "silu": (1, 1, 1), "hiV": (0, 0, 1), "eqlast": (0, 0, 1, 1), "early": (1, 1, 0), "ecut": ((1, 2, 3, 4), (1, 3, 4), (1, 3, 4)), "unS": (0, 0, 0),
    "batch": ((0, 2, 3, 4), (0, 3, 4), (0, 3, 4)),
    "acts": (5, 8, 8),
    "lend": (3.0, 3.0, 1.0), "lendv": (0.0, 1.0, 1.0), "lendc": 0.3,
    "due": (77, 44, 0), "duel": (111, 72, 39), "pace": (6, 6.0, 6.8),
    "lat": (0.35, 0.17), "piece": 600, "vbank": ("P1", "P0", "P1"),
    "rounds": 6500, "heat": 0.35, "moves": (0.2, 0.4, 0.47, 0.72), "seed": 1, "off": 0.7, "pull": 1.5,
    "other": ((0.7, (1.35, 1.9, 5.0, 1.0)), (0.95, (1.1, 1.15, 2.5, 1.5))),
}
STATS = {}

SCRATCH = {}


def _sb(names, shape, dtype):
    for n in names.split():
        SCRATCH[n] = ("sbuf", [128] + list(shape), dtype)


_sb("VD ntb", [W], I)
_sb("St", [W], B)
_sb("volE", [W + 16], B)
_sb("Wf", [UB + W], F)
_sb("wall", [4 * WT], F)
_sb("Z0", [96], F)
_sb("Rb0 Rb1 Rb2", [512], F)
_sb("dvO", [112, 3], F)
_sb("Ug", [10240], F)
_sb("Omin Omax", [2304], F)
_sb("un", [32], F)
_sb("un8", [128], F)
_sb("lev", [512], F)
_sb("Zp", [8, 4, 3, 16], B)
_sb("OL", [5, 4, 3, 16], B)
_sb("Cq", [3, 143], B)
_sb("pid", [4], I)
_sb("col", [16], F)
_sb("rows", [3, 128], F)
_sb("cf", [6, 128], F)
_sb("cb", [9, 128], B)
_sb("top", [256], B)
_sb("M16", [16], F)
_sb("cm aBf", [8], F)
_sb("cW", [8], B)
_sb("wb", [32], B)
_sb("Rq", [16, 128], B)
_sb("Dq Dg", [144], B)
_sb("wpad", [240], B)
_sb("selP", [8, 128], B)
_sb("ring ring16 volN nA", [112], B)
_sb("rq", [3, 16], F)
_sb("xtab", [3, 112], B)
_sb("qu qa hh thr1", [112], F)
_sb("lane lane1 biasL dump thr", [40], F)
_sb("smallR", [96], B)
_sb("junk", [8, 96], B)
_sb("Cc", [96], F)
_sb("Pw", [104], F)
_sb("acc bo2 ka kb", [8], F)
_sb("bo", [56], F)
_sb("dig", [3, 56], F)
_sb("q16", [16], B)
_sb("mm", [32], F)
_sb("xr", [16], B)
_sb("x16", [8], U16)
_sb("cmpb XE", [128], B)
_sb("raw", [128], F)
_sb("b16", [2, 5, 128], U16)
_sb("wZ Mm Dd De Rlo Rhi", [128], F)
_sb("A2", [256], F)
_sb("KS", [256], F)
_sb("SC rmask qmask", [128], F)
_sb("bn MK hold", [128], H)
_sb("Ih", [2, 128], H)
_sb("cmh", [2, 8], H)
_sb("Bc", [4, 128], F)
_sb("Vg", [2048], B)
_sb("eq", [4, 128], B)
_sb("o16 nA16 off16", [2, 40], U16)
_sb("nW th pre", [2, 40], F)
_sb("G", [2, 640], B)
_sb("OH", [40, 112], B)
_sb("ne ff t40", [40], F)
_sb("hc", [5, 16], F)
_sb("hcm", [16], B)
_sb("Zq", [40], B)
_sb("nS thB", [32], F)
_sb("EQ", [8, 512], B)
_sb("Wb", [512], B)
_sb("um prod ec", [640], F)
_sb("Ss tg", [4, 128], F)
_sb("z16", [2, 8], U16)
_sb("nR", [RO, 32], F)
_sb("nF", [RO, 112], B)
_sb("nOff", [2, 120], U16)
for _k in range(8):
    SCRATCH["P%d" % _k] = ("psum", [128, 512], F)

SEMAPHORES = ["c_vector", "c_scalar", "c_tensor", "c_pool"] + ["d%d" % k for k in range(12)] + \
             ["ls%d" % k for k in range(9)] + ["ar%d" % k for k in range(9)]

CY = 0.83e-3 * 1.05
PCY = 0.42e-3 * 1.05
GA, SCA = 1.56, 3.5
PLAN = {}


def place(x, a, b):
    lo, hi = 0, len(b) - 1
    while lo < hi:
        mid = (lo + hi) // 2
        if b[mid] > x:
            hi = mid
        else:
            lo = mid + 1
    return lo


def plan(ops):
    n = len(ops)
    lat_x, lat_s = CFG["lat"]
    comp = [o["k"] == "c" for o in ops]
    pred = [[(d, 0) for d in sorted(o["deps"])] + [(d, 1) for d in sorted(o["order"] - o["deps"])] for o in ops]
    anc = [0] * n
    for i in range(n):
        far = 0
        for d, k in pred[i]:
            far |= anc[d]
        pred[i] = [(d, k) for d, k in pred[i] if not far >> d & 1]
        for d, k in pred[i]:
            far |= 1 << d
        anc[i] = far
    succ = [[] for _ in ops]
    for i in range(n):
        for d, k in pred[i]:
            succ[d].append((i, k))
    alts = [[(e, a[0], a[0] if comp[i] else (0.0 if e == "ext" else (0.1 if o["k"] == "dma" else 0.5))) for e, a in o["alt"].items()]
            for i, o in enumerate(ops)]
    seed = [CFG["seed"]]

    def draw():
        seed[0] = (seed[0] * 1103515245 + 12345) % 2 ** 31
        return seed[0] / 2.0 ** 31

    def lay(key, before, after, eng, back, free):
        key = list(key)
        for i in (range(n - 1, -1, -1) if back else range(n)):
            for p, k in before[i]:
                if key[p] >= key[i]:
                    key[i] = key[p] + 1e-6
        st, fin, eng, gaps = [0.0] * n, [0.0] * n, list(eng), {}
        for i in sorted(range(n), key=lambda i: key[i]):
            best = None
            for e, d, h in alts[i]:
                shy = 0.0
                if e != eng[i]:
                    if not free or not free[i]:
                        continue
                    shy = free[i] if e == "vector" else free[i] - CFG["pull"]
                r = 0.0
                for p, k in before[i]:
                    x = fin[p] + (0.0 if k else (lat_s if eng[p] == e and comp[i if back else p] else lat_x))
                    if x > r:
                        r = x
                at = -1
                if h:
                    if e not in gaps:
                        gaps[e] = ([0.0], [1e9])
                    a, b = gaps[e]
                    if back:
                        r += d - h
                    at = len(b) - 1 if r >= a[-1] else place(r, a, b)
                    while (a[at] if a[at] > r else r) + h > b[at] + 1e-9:
                        at += 1
                    if a[at] > r:
                        r = a[at]
                    if back:
                        r -= d - h
                if best is None or r + d + shy < best[0]:
                    best = (r + d + shy, e, r, d, h, at)
            _, e, r, d, h, at = best
            eng[i], st[i], fin[i] = e, r, r + d
            if h:
                a, b = gaps[e]
                x = r + d - h if back else r
                lo, hi = x - a[at] > 0.04, b[at] - x - h > 0.04
                if lo and hi:
                    a.insert(at + 1, x + h)
                    b.insert(at, x)
                elif lo:
                    b[at] = x
                elif hi:
                    a[at] = x + h
                else:
                    del a[at], b[at]
        return max(fin), st, fin, eng

    def both(key, eng, free):
        span, st, fin, eng = lay(key, pred, succ, eng, False, free)
        t, _, f2, _ = lay([-x for x in fin], succ, pred, eng, True, None)
        return [span, st, fin, eng, [t - x for x in f2]]

    def slow(o, d, speed):
        if o["k"] == "c":
            return d * speed[0] * (1.0, speed[1] / GA, speed[2] / SCA)[o["g"]]
        return d * (speed[3] if o["e"] == "pool" else 1.0)
    other = [(w, [{e: slow(o, a[0], speed) for e, a in o["alt"].items()} for o in ops]) for w, speed in CFG["other"]]

    def worth(x):
        order, eng, total = sorted(range(n), key=lambda i: (x[1][i], i)), x[3], x[0]
        for w, dur in other:
            fin, free = [0.0] * n, {}
            for i in order:
                e = eng[i]
                r = free.get(e, 0.0)
                for p, k in pred[i]:
                    y = fin[p] + (0.0 if k else (lat_s if eng[p] == e and comp[p] else lat_x))
                    if y > r:
                        r = y
                fin[i] = r + dur[i][e]
                if e != "ext":
                    free[e] = fin[i] if comp[i] else r + (0.1 if ops[i]["k"] == "dma" else 0.5)
            total += w * max(fin)
        return total / (1 + len(other))

    tail = [0.0] * n
    for i in range(n - 1, -1, -1):
        tail[i] = ops[i]["d"] + max([tail[s] + (0.0 if k else lat_x) for s, k in succ[i]] + [ops[i].get("due", 0.0)])
    kinds = sorted(set(o["w"] for o in ops))
    kind = [kinds.index(o["w"]) for o in ops]
    parts = sorted(set(o["p"] for o in ops))
    part = [parts.index(o["p"]) for o in ops]
    two = [i for i in range(n) if len(alts[i]) > 1]
    cur = both([-x - o["b"] for x, o in zip(tail, ops)], [o["e"] for o in ops], [o.get("lend", 0.0) + 1e-3 for o in ops])
    for _ in range(3):
        new = both(cur[4], cur[3], None)
        if new[0] <= cur[0]:
            cur = new
    cur.append(worth(cur))
    best, rounds, m = cur, CFG["rounds"], CFG["moves"]
    STATS["spans"] = [round(cur[0], 1)]
    for it in range(rounds):
        mix = draw()
        base = [mix * x + (1 - mix) * y for x, y in zip(cur[1], cur[4])] if draw() < 0.5 else cur[4]
        at, wide, amp = draw() * max(cur[2]), 3 + 20 * draw() ** 2, 0.2 + draw()
        r, key, free, eng = draw(), base, None, cur[3]
        if r < m[0]:
            sh = [amp * 3 * (draw() - 0.5) if draw() < 0.2 else 0.0 for _ in kinds]
            key = [x + sh[k] if at < x < at + wide else x for x, k in zip(base, kind)]
        elif r < m[1]:
            key = [x + amp * (draw() - 0.5) if at < x < at + wide else x for x in base]
        elif r < m[2]:
            sh = [amp * 8 * (draw() - 0.5) if draw() < 0.1 else 0.0 for _ in parts]
            key = [x + sh[k] for x, k in zip(base, part)]
        elif r < m[3]:
            bar = 2.0 * draw() ** 2 + 1e-3
            free = [bar if at < x < at + wide else 0.0 for x in base]
        else:
            eng = list(eng)
            off = "vector" if draw() < CFG["off"] else ""
            near = [i for i in two if at < base[i] < at + wide and (eng[i] == off or not off)]
            for _ in range(1 + int(2 * draw())):
                if near:
                    i = near[int(draw() * len(near))]
                    eng[i] = [a[0] for a in alts[i] if a[0] != eng[i]][0]
        new = both(key, eng, free)
        if new[0] <= cur[0] + 1.0:
            new.append(worth(new))
            if new[5] <= cur[5] + CFG["heat"] * (1 - it / rounds) * draw() ** 2:
                cur = new
                if new[5] < best[5]:
                    best = new
        if it % max(1, rounds // 8) == 0:
            STATS["spans"].append((round(cur[0], 1), round(cur[5], 1)))
    STATS.update({"span": max(best[2]), "n": n, "fin": best[2], "ops": ops})
    return sorted(range(n), key=lambda i: (best[1][i], i)), best[3]


def rank_program(g, core, T, topo):
    rank = T.rank_of(core)
    if rank is None:
        return
    cores = list(T.cores)
    n_r = len(cores)
    prev, nxt = cores[(rank - 1) % n_r], cores[(rank + 1) % n_r]

    def share(src):
        r = cores.index(src)
        nb = [cores[(r - 1) % n_r], cores[(r + 1) % n_r]]
        out, used = {}, []
        for d in sorted(nb, key=lambda d: len(topo.engines(src, d))):
            e = [x for x in topo.engines(src, d) if x not in used]
            e = e[:8] if used else e[:max(1, min(8, len(set(topo.engines(src, nb[0]) + topo.engines(src, nb[1]))) // 2))]
            out[d] = e
            used = used + e
        return out

    ops, log, tag, banks = [], {}, [0.0, ("start", -1)], {}
    S_ = slice
    ALL = S_(None)

    def v(name, *idx, p=None):
        ap = T[name][(ALL if p is None else p,) + idx]
        if name not in SCRATCH:
            return {"ap": ap, "r": []}
        m = np.zeros(SCRATCH[name][1][1:], bool)
        m[idx] = True
        return {"ap": ap, "r": [(name, int.from_bytes(np.packbits(m.reshape(-1)).tobytes(), "big"))]}

    def c(name, a, b, s=1, p=None):
        return v(name, S_(a, b, s), p=p)

    def ind(win, off):
        return {"ap": win["ap"].indirect(off["ap"]), "r": win["r"], "x": off["r"]}

    def op(eng, dur, fn, reads, writes, kind="c", extra=None, two=False):
        me = len(ops)
        who = me if two else eng
        deps, order_only = set(), set()
        acc = []
        for x in reads:
            if isinstance(x, dict):
                acc += [(r, False) for r in x["r"]] + [(r, False) for r in x.get("x", [])]
        for x in writes:
            acc += [(r, True) for r in x["r"]] + [(r, False) for r in x.get("x", [])]
        for name in sorted(set(r[0] for r, _ in acc if r[0] in SCRATCH and SCRATCH[r[0]][0] == "psum")):
            turn = banks.setdefault(name, [who, [], []])
            if turn[0] != who:
                turn[:] = [who, [], turn[1]]
            deps.update(turn[2])
            turn[1].append(me)
        for (name, m), wr in acc:
            for (m2, o, w2) in log.get(name, []):
                if o != me and (m & m2) and (wr or w2):
                    (order_only if eng == "tensor" and ops[o]["e"] == eng else deps).add(o)
        for (name, m), wr in acc:
            lst = log.setdefault(name, [])
            if wr:
                lst[:] = [(e[0] & ~m, e[1], e[2]) for e in lst if e[0] & ~m]
            lst.append((m, me, wr))
        if extra is not None:
            deps.add(extra)
        ops.append({"e": eng, "d": dur, "alt": {eng: (dur, fn)}, "deps": deps, "order": order_only, "k": kind, "b": tag[0], "p": tag[1],
                    "w": ([x["r"][0][0] for x in writes if x["r"]] + [""])[0],
                    "g": 2 if any("x" in x for x in writes) else int(any(isinstance(x, dict) and "x" in x for x in reads))})
        return me

    def part(name, t):
        tag[1] = (name, t)

    def a_(x):
        return x["ap"] if isinstance(x, dict) else x

    def vd(n, x=None, o=None):
        if o is not None and "x" in o:
            return 0.05 + SCA * n * CY
        if x is not None and "x" in x:
            return 0.05 + GA * n * CY
        return max(64, n) * CY

    def cp(o, x, n):
        op("vector", vd(n, x, o), lambda q: q.tensor_copy(o["ap"], x["ap"]), [x], [o])

    def tt(o, x, y, f, n):
        op("vector", vd(n, x, o), lambda q: q.tensor_tensor(o["ap"], x["ap"], y["ap"], f), [x, y], [o])

    def ts(o, x, s1, f1, n, s2=None, f2=None):
        if s2 is None:
            op("vector", vd(n, x), lambda q: q.tensor_scalar(o["ap"], x["ap"], a_(s1), None, f1), [x, s1], [o])
        else:
            op("vector", vd(n, x), lambda q: q.tensor_scalar(o["ap"], x["ap"], a_(s1), a_(s2), f1, f2), [x, s1, s2], [o])

    def scan(o, d0, d1, init, f0, f1, n):
        op("vector", vd(n), lambda q: q.tensor_tensor_scan(o["ap"], d0["ap"], d1["ap"], init, f0, f1), [d0, d1], [o])

    def red(o, x, n):
        op("vector", vd(n), lambda q: q.tensor_reduce(o["ap"], x["ap"], AxisListType.X, AL.add), [x], [o])

    def ms(o, val, n):
        op("vector", vd(n), lambda q: q.memset(o["ap"], val), [], [o])

    first_exp = []

    def act(o, x, n, f=AF.Copy, bias=None, scale=None, accum=None):
        k = {}
        if bias is not None:
            k["bias"] = a_(bias)
        if scale is not None:
            k["scale"] = a_(scale)
        if accum is not None:
            k["accum_out"] = accum["ap"]
        d = 0.07 + (GA * n if "x" in x else max(64, n)) * CY + (1.3 if f == AF.Exp and not first_exp else 0)
        if f == AF.Exp:
            first_exp.append(1)
        op("scalar", d, lambda q: q.activation(o["ap"], x["ap"], f, **k), [x, bias, scale], [o] + ([accum] if accum else []))

    def flex(first, o, x, n, scale=1.0, bias=None, relu=False, half=False, lend=None):
        k = {"scale": a_(scale)}
        if bias is not None:
            k["bias"] = a_(bias)
        f = AF.Relu if relu else (AF.Copy if bias is None else AF.Identity)
        if relu:
            on_v = lambda q: q.tensor_scalar(o["ap"], x["ap"], 0.0, None, AL.max)
        elif bias is None:
            on_v = lambda q: q.tensor_scalar(o["ap"], x["ap"], a_(scale), None, AL.mult)
        else:
            on_v = lambda q: q.tensor_scalar(o["ap"], x["ap"], a_(scale), a_(bias), AL.mult, AL.add)
        alt = {"scalar": (0.07 + (GA * n if "x" in x else max(64, n)) * CY, lambda q: q.activation(o["ap"], x["ap"], f, **k)),
               "vector": (vd(n // 2 if half else n, x), on_v)}
        op(first, alt[first][0], alt[first][1], [x, scale, bias], [o], two=True)
        ops[-1]["alt"] = alt
        ops[-1]["lend"] = CFG["lendc"] if lend is None else lend

    def put(o, x, either):
        cp(o, x, 128)
        if either:
            ops[-1]["alt"]["scalar"] = (0.07 + SCA * 128 * CY, lambda q: q.activation(o["ap"], x["ap"], AF.Silu))
            ops[-1]["lend"] = 0.3

    def fs(*a, **k):
        flex("scalar", *a, **k)

    def fv(*a, **k):
        flex("vector", *a, **k)

    def mm(lst):
        pieces, size = [[]], 0
        for x in lst:
            if pieces[-1] and (size + x[5] > CFG["piece"] or x[1].get("cut")):
                pieces.append([])
                size = 0
            pieces[-1].append(x)
            size += x[5]
        for piece in pieces:
            def f(q, piece=piece):
                for (o, l, r, st, sp, _) in piece:
                    ins = q.matmul(o["ap"], l["ap"], r["ap"], st, sp)
                return ins
            mark = [{"r": [(b + "g", 1)]} for b in sorted(set(x[0]["r"][0][0] for x in piece))]
            shut = piece[0][3] and piece[-1][4]
            op("tensor", 0.03 + sum(x[5] for x in piece) * PCY, f, [x[1] for x in piece] + [x[2] for x in piece] + (mark if shut else []),
               [x[0] for x in piece] + ([] if shut else mark))

    def cut(x):
        return dict(x, cut=True)

    def grp(o, pairs):
        return [(o, l, r, k == 0, k == len(pairs) - 1, n) for k, (l, r, n) in enumerate(pairs)]

    def iota(o, pat, base, cmul, n, flt=True):
        k = {"allow_small_or_imprecise_dtypes": True} if flt else {}
        op("pool", 0.13 + 2 * n * CY, lambda q: q.iota(o["ap"], pat, base, cmul, **k), [], [o])

    def fill(o, val, n):
        iota(o, [[0, n]], val, 0, n)
        ops[-1]["lend"] = 0.5
        ops[-1]["alt"]["vector"] = (vd(n), lambda q: q.memset(o["ap"], float(val)))

    def asel(o, x, pat, f, fill, base, cmul, n):
        op("pool", 0.17 + 2 * n * CY, lambda q: q.affine_select(o["ap"], x["ap"], pat, f, fill, base, cmul), [x], [o])

    def dma(queue, o, x, us):
        op(queue, us, lambda q: q.dma_start(o["ap"], x["ap"]), [x], [o], kind="dma")

    n_x = [0]

    def exchange(to_prev, to_next, us):
        k = n_x[0]
        n_x[0] += 1
        mine = share(core)
        trs = []
        for d, lst in ((prev, to_prev), (nxt, to_next)):
            rid, pid, _ = topo.addr(d)
            per = len(mine[d]) // len(lst)
            for i, (s, o) in enumerate(lst):
                mask = sum(1 << e for e in mine[d][i * per:(i + 1) * per])
                trs.append(RemoteDMATransfer(dst_ids=[DstId(rid=rid, pnc=pid)], dma_engine_mask=mask,
                                             remote_sem=T.sem["ar%d" % k], src=s["ap"], dst=o["ap"]))
        sent = len(mine[prev]) + len(mine[nxt])
        come = len(share(prev)[core]) + len(share(nxt)[core])
        s = op("pool", us, lambda q: q.remote_dma_fused(trs, local_sem=T.sem["ls%d" % k]),
               [x[0] for x in to_prev + to_next], [], kind=("ls%d" % k, sent))
        op("ext", 0.3, None, [], [x[1] for x in to_prev + to_next], kind=("ar%d" % k, come), extra=s)

    p32 = S_(0, 32)
    tag[0] = 1000.0
    dma("sync", c("VD", 0, V, p=S_(0, 8)), v("vol", ALL), 2.2)
    dma("scalar", {"ap": c("VD", 0, V, p=S_(8, 32))["ap"], "r": [("VDx", 1)]}, v("dv", ALL), 2.4)
    tag[0] = 500.0
    dma("sync", v("ntb"), v("nt", ALL), 5.5)
    tag[0] = 400.0
    dma("scalar", c("Wf", 0, V), v("u", ALL), 8.0)
    dma("scalar", c("wall", WT + 8, 2 * WT), v("wt", ALL), 8.5)
    tag[0] = 0.0

    ms(v("Cq", p=p32), 1.0, 215)
    asel(v("Cq", p=p32), v("Cq", p=p32), [[-16, 3], [-3, 143]], AL.is_equal, 0.0, -83, 16, 429)
    asel(v("Cq", 0, p=p32), v("Cq", 0, p=p32), [[-1, 143]], AL.not_equal, 1.0, 15, 16, 143)
    iota(c("pid", 0, 1), [[0, 1]], 0, 1, 1, False)
    iota(v("rows", 0), [[1, 128]], 0, 0, 128)
    iota(v("rows", 1), [[0, 8], [1, 16]], 0, 0, 128)
    iota(v("rows", 2), [[1, 8], [0, 16]], 0, 0, 128)
    iota(v("lane"), [[0, 5], [16, 8]], 0, 0, 40)
    ts(c("pid", 1, 2), c("pid", 0, 1), 15, AL.bitwise_and, 1)
    ts(c("pid", 2, 3), c("pid", 0, 1), 4, AL.arith_shift_right, 1)
    qc, gc, below, shc, alc, wc, pc, lnw, twice, less, most = [c("col", k, k + 1) for k in range(11)]
    cp(qc, c("pid", 1, 2), 1)
    cp(gc, c("pid", 2, 3), 1)
    cp(pc, c("pid", 0, 1), 1)
    ts(shc, pc, 111.5, AL.is_gt, 1, -128.0, AL.mult)
    ts(shc, shc, pc, AL.add, 1, 16.0, AL.add)
    lrow, qrow, grow = v("rows", 0), v("rows", 1), v("rows", 2)
    If = v("cf", 0)
    Ib, bo, up, negI, shm, I16, selV, selE, selQ = [v("cb", k) for k in range(9)]
    bo8 = v("cb", 1, S_(0, 128, 16))
    I8 = v("cb", 0, S_(0, 128, 16))
    ts(bo, grow, gc, AL.is_equal, 128)
    ts(v("cmpb"), qrow, qc, AL.is_lt, 128)
    tt(up, v("cmpb"), bo, AL.mult, 256)
    ts(v("lane"), v("lane"), qc, AL.add, 40)
    fv(v("biasL"), v("lane"), 40, -1.0, -0.5)
    ts(If, lrow, pc, AL.is_equal, 128)
    ts(Ib, lrow, pc, AL.is_equal, 128)
    ts(shm, lrow, shc, AL.is_equal, 128)
    negf = v("cf", 1)
    ts(v("Ih", 0), lrow, pc, AL.is_equal, 128)
    ts(v("Ih", 1), lrow, pc, AL.is_equal, 128, -16.0, AL.mult)
    for o, k in [(I16, 16.0), (negI, -2.0 ** 24)]:
        fs(o, Ib, 128, k, half=True)
    for o, k in [(negf, -1.0)] + [(v("cf", 1 + s), s / 8.0) for s in range(1, 5)]:
        fs(o, If, 128, k)
    fill(c("top", 0, 256, 2), 0, 128)
    iota(c("top", 1, 256, 2), [[0, 8], [-4096, 16]], int(TOP), 0, 128)
    fill(c("ne", 0, 8), 1, 8)
    ts(v("M16"), v("rows", 0, S_(0, 16)), qc, AL.is_equal, 16)
    ts(v("cm"), v("rows", 0, S_(0, 8)), gc, AL.is_equal, 8)
    row = lambda k: c("M16", k, k + 1)
    fill(v("cW"), -W, 8)
    iota(c("wb", 0, 24), [[WT, 3], [0, 8]], WT, 0, 24)
    fill(c("wb", 24, 32), WT, 8)
    fill(c("Pw", 96, 104), 10 ** 6, 8)
    fill(v("A2"), 0, 256)
    ts(v("hold"), qrow, 0.0, AL.mult, 128)
    ts(v("rmask"), qrow, 0.5, AL.is_gt, 128)
    ts(v("SC"), qrow, qc, AL.is_lt, 128)
    ts(v("wZ"), qrow, qc, AL.is_equal, 128, 2.0 ** 60, AL.mult)
    tt(v("SC"), v("SC"), v("wZ"), AL.add, 256)
    tt(v("qmask"), v("SC"), v("rmask"), AL.mult, 256)
    fv(c("qmask", 1, 128, 16), c("qmask", 1, 128, 16), 8, 2.0 ** -60)
    fv(most, row(0), 1, -984.0, 1000.0)
    fv(less, row(0), 1, 1.0, -1.0)
    cp(v("cmh", 0), v("cm"), 8)
    ts(v("cmh", 1), v("cm"), less, AL.mult, 8)
    fill(v("Dg"), 0, 144)
    cp(c("Dg", 15, 143, 16), v("cm"), 8)
    for q in range(16):
        fv(v("Rq", q), c("Dg", 15, 143), 128, row(q), half=True)
    fill(c("Dq", 0, 15), 0, 15)
    fv(c("Dq", 15, 143), Ib, 128, row(0), half=True)
    for t in range(RO):
        x0 = (STEP * t) % V // 16
        iota(v("xtab", t, S_(0, 96 - x0)), [[1, 96 - x0]], x0, 0, 96 - x0)
        if x0:
            iota(v("xtab", t, S_(96 - x0, 96)), [[1, x0]], 0, 0, x0)
        fill(v("xtab", t, S_(96, 112)), 0, 16)
    for a, x, n in RING:
        iota(c("ring", a, a + n), [[1, n]], x + 1, 0, n)
    if max(CFG["fast"]):
        fs(v("ring16"), v("ring"), 112, 16.0, half=True)
        iota(v("q16"), [[1, 16]], -16, 0, 16)
        fill(v("dig", 1), 1, 56)
        fill(v("dig", 1, S_(0, 56, 7)), 0, 8)
        fill(v("dig", 1, S_(3, 56, 7)), -1, 8)
        for x, val in ((1, BIG), (2, -BIG), (4, -7.5), (5, BIG / 256), (6, 16 - BIG / 256)):
            ms(v("dig", 0, S_(x, 56, 7)), val, 8)
    q16f = v("rows", 0, S_(0, 16))
    fv(v("rq", 0), q16f, 16, row(4), row(2))
    tt(v("rq", 1), v("rq", 0), q16f, AL.mult, 32)
    fv(v("rq", 2), v("rq", 1), 16, 1.0, row(3))
    for q in range(16):
        fv(c("St", q, W, 16), v("ring"), 112, row(1), v("rq", 2, S_(q, q + 1)), half=True)
    fs(selV, bo, 128, row(0), half=True)
    ts(selE, bo, row(3), AL.mult, 64, 0.0625, AL.mult)
    ts(v("raw"), qrow, row(3), AL.mult, 128, -1.0, AL.mult)
    fv(twice, row(2), 1, 2.0)
    fv(v("raw"), v("raw"), 128, 1.0, twice)
    tt(v("raw"), v("raw"), qrow, AL.mult, 256)
    ts(v("raw"), v("raw"), row(3), AL.add, 128, row(4), AL.subtract)
    ts(below, gc, 0.5, AL.is_lt, 1, 8.0, AL.mult)
    ts(below, below, gc, AL.add, 1, -1.0, AL.add)
    ts(v("Mm"), grow, below, AL.is_equal, 128)
    tt(selQ, v("raw"), v("Mm"), AL.mult, 256)
    fill(c("volE", W, W + 16), 0, 16)
    fill(c("Wf", W, UB), 0, UB - W)
    fill(c("wall", 0, 8), 1, 8)
    ms(c("wall", WT, WT + 8), 0.5, 8)
    fill(v("Z0"), 0, 96)
    fv(v("lane1"), v("lane"), 40, 1.0, 1.0)
    fv(v("dump"), v("lane"), 40, 1.0, W + 1.0)
    ln2 = math.log(2.0)
    fv(lnw, pc, 1, -ln2, 63 * ln2)
    act(wc, lnw, 1, AF.Exp)
    fv(v("t40"), v("lane"), 40, -ln2, 63 * ln2 + math.log(2.5))
    act(v("thr"), v("t40"), 40, AF.Exp)
    fv(alc, row(1), 1, 16.0, row(2))
    fv(v("aBf"), v("cm"), 8, alc)
    fv(c("hcm", 8, 16), v("aBf"), 8)
    fv(c("hcm", 0, 8), v("cm"), 8, row(1))
    for k in range(8):
        fs(v("selP", k), Ib, 128, 0.0, c("aBf", k, k + 1), half=True)
    fill(v("wpad"), 0, 240)
    fv(c("wpad", 112, 128), v("M16"), 16, 0.0, wc)
    for k in range(2):
        ms(c("un", k, 32, 2), UP * 256.0 ** k, 16)
    if max(CFG["stages"]) > 1:
        for k in range(8):
            ms(c("un8", k, 128, 8), UP * 256.0 ** k, 16)
            ms(c("lev", 16 * k, 16 * k + 16), 256.0 ** -k, 16)
        for a in (128, 256):
            fs(c("lev", a, 2 * a), c("lev", 0, a), a)
    for name, n in (("OL", 5), ("Zp", 8)):
        iota(v(name, ALL, ALL, 1), [[0, 4 * n], [0, 16]], 0, 0, 64 * n)
    data = (ALL, S_(0, 3, 2))

    def half(name, j, k):
        return v(name, j, k // 2, S_(k % 2, k % 2 + 2))

    def pair(bank, a, x, y):
        return c(bank, x, y, p=S_(32 * a, 32 * a + 32))

    def both(x):
        return {"ap": x["ap"], "r": x["r"] + [("VDx", 1), ("VDy", 1)]}
    for a in (0, 1408):
        for p in (S_(32, 64), S_(64, 128)):
            ms({"ap": c("VD", a, a + 128, p=p)["ap"], "r": [("VDy", 1)]}, 0, 128)
    exchange([(both(c("VD", 0, 128)), c("VD", 1664, W))], [(both(c("VD", 1408, V)), c("VD", V, 1664))], 4.0)
    for a, b in ((0, 768), (768, V), (V, W)):
        cp(c("Vg", a, b, p=p32), both(c("VD", a, b, p=p32)), b - a)

    def wrap(t, a, b):
        bank = "P%d" % (3 + t)
        mm(grp(c(bank, a, b), [(v("Cq", t, S_(15 - q, 143 - q), p=p32), c("Vg", 16 * a + q, 16 * b, 16, p=p32), max(64, b - a))
                               for q in range(16)]))
        if (t, a) == (0, 0):
            ts(v("smallR"), c(bank, 0, 96), 7.5, AL.is_lt, 96)
        for r, x, n in RING:
            if a <= x < b:
                cp(v("dvO", S_(r, r + n), t), c(bank, x, x + n), n)
    for t in range(RO):
        wrap(t, 0, 96)
    for bank, x, a, b, r in (("P6", 0, 128, 640, 512), ("P7", 0, 640, 1152, 1024), ("P6", 0, 1152, 1408, 1536), ("P7", 0, 0, 128, 256),
                             ("P6", 256, 1408, V, 128), ("P7", 128, V, 1664, 384), ("P7", 256, 1664, W, 0)):
        mm(grp(c(bank, x, x + b - a), [(Ib, c("St", r, r + b - a), b - a), (v("Cq", 0, S_(15, 143), p=p32), c("Vg", a, b, p=p32), b - a)]))
        if a != V:
            a, x = (V, 128) if a == 1664 else (a, x)
            ts(c("volE", a, b), c(bank, x, x + b - a), row(0), AL.max, b - a, most, AL.min)
    for t in range(RO):
        wrap(t, 96, 112)
    exchange([(c("Wf", 0, 128), c("Wf", 1664, W))], [(c("Wf", 1408, V), c("Wf", V, 1664))], 2.5)

    def scaled(a, b):
        fs(c("Wf", UB + a, UB + b), c("Wf", a, b), b - a, 1.0 / 256, lend=2.0)
    for a, b in ((0, 512), (512, 1024), (1024, V), (V, W)):
        scaled(a, b)
    fs(c("wall", 8, WT), c("wall", WT + 8, 2 * WT), 256, 1.0 / UP)
    fs(c("wall", WT + 8, 2 * WT), c("wall", WT + 8, 2 * WT), 256, 1.0 / UP)
    exchange([(c("wall", WT, 2 * WT), c("wall", 3 * WT, 4 * WT))], [(c("wall", WT, 2 * WT), c("wall", 2 * WT, 3 * WT))], 2.5)

    def spread_volumes(a, b, bank):
        n = 16 * (b - a)
        mm([(c(bank, 0, n), Ib, c("St", 16 * a, 16 * b), True, False, n)] +
           [(c(bank, q, n, 16), v("Rq", q), c("volN", a, b), False, q == 15, 64) for q in range(16)])
        if a:
            fs(c("volE", 16 * a - 384, 16 * b - 384), c(bank, 0, n), n, lend=1.0)
        else:
            for r, x, _ in RING[:4]:
                act(c("volE", 16 * x, 16 * x + 128), c(bank, 16 * r, 16 * r + 128), 128)

    def lanes(t):
        last = t == RO - 1
        e = t % 2
        x0 = (STEP * t) % V // 16
        if t:
            tt(c("smallR", 88 - x0, 104 - x0), v("nR", t - 1, S_(8, 24)), c("thB", 8, 24), AL.is_gt, 32)
        mm([(c("P0", 0, 96), bo, v("smallR"), True, True, 96), (c("P0", 128, 224), up, v("smallR"), True, True, 96)])
        scan(v("Cc"), c("P0", 0, 96), v("Z0"), 0.0, AL.add, AL.add, 96)
        na = CFG["acts"][t]
        for k in range(na):
            act(v("junk", k), v("Cc"), 96, AF.Sign, bias=c("biasL", k, k + 1), accum=c("acc", k, k + 1))
        for k in range(na, 8):
            ts(v("junk", k), v("Cc"), c("lane", k, k + 1), AL.is_gt, 96, 2.0, AL.mult)
        for k in range(na, 8):
            red(c("bo2", k, k + 1), v("junk", k), 96)
        tt(c("Pw", 0, 96), v("Cc"), c("P0", 128, 224), AL.subtract, 96)
        if na < 8:
            ts(c("acc", na, 8), c("bo2", na, 8), -96.0, AL.add, 8)
        ts(v("x16"), v("acc"), -0.5, AL.mult, 8, 48.0, AL.add)
        fv(c("xr", 0, 8), v("acc"), 8, -0.5, 48.0 + x0)
        if x0:
            ts(c("xr", 8, 16), v("acc"), 2.0 * x0 - 95.0, AL.is_lt, 8, -96.0, AL.mult)
        tt(v("cmpb"), ind(v("Pw"), v("x16")), lrow, AL.is_le, 128)
        fs(v("XE"), ind(v("xtab", t), v("x16")), 128)
        mm(grp(c("P0", 224, 232), [(I16, c("xr", 0, 8), 64)] + [(I16, c("xr", 8, 16), 64)] * (x0 > 0) + [(Ib, v("cW"), 64)] +
               [(c("Dg", 15 - q, 143 - q), c("cmpb", q, 128, 16), 64) for q in range(16)]) +
           grp(c("P0", 232, 240), [(v("cmpb"), bo8, 64), (v("XE"), bo8, 64)]))
        ts(v("o16", e, S_(0, 8)), c("P0", 224, 232), float(W), AL.add, 8)
        cp(c("hold", 0, 128, 16), c("P0", 232, 240), 8)
        scan(v("Bc", 0), v("rmask"), v("hold"), 0.0, AL.mult, AL.add, 128)
        ts(v("mm"), c("lane", 0, 32), c("Cc", 95, 96), AL.is_lt, 32)
        if t:
            ts(c("hh", 0, 32), v("nF", t - 1, S_(0, 32)), 3.0, AL.min, 32)
            tt(c("qu", 0, 32), c("qa", 0, 32), c("hh", 0, 32), AL.subtract, 64)
            ts(c("volN", 0, 32), c("qu", 0, 32), 1.0, AL.max, 32, 16.0, AL.min)
            spread_volumes(0, 32, "P1")
        else:
            ts(v("volN"), v("dvO", ALL, 0), 1.0, AL.max, 112, 16.0, AL.min)
        if not last:
            tt(v("qa"), v("volN"), v("dvO", ALL, t + 1), AL.add, 224)
            fv(c("P2", 112, 224), v("qa"), 112, 1000.0, -10500.0)
            fv(v("thr1"), v("qa"), 112, 1.0, -7.5)
            tt(v("thr1"), c("P2", 112, 224), v("thr1"), AL.max, 112)

    def lists(t):
        last = t == RO - 1
        e = t % 2
        sl = lambda name, a, b: v(name, e, S_(8 * a, 8 * b))
        Gj = lambda a, b: v("G", e, S_(128 * a, 128 * b))
        bo = lambda k: c("bo", 8 * k, 8 * k + 8)

        def names(j):
            ts(v("b16", e, j), ind(v("ntb"), sl("o16", j, j + 1)), 0.0625, AL.mult, 128, -0.46875, AL.add)

        def level(j):
            ts(v("b16", e, j, S_(1, 128, 2)), v("b16", e, j, S_(1, 128, 2)), float(UB), AL.add, 32)

        def present(a, b):
            tt(c("t40", 8 * a, 8 * b), sl("nW", a, b), sl("th", a, b), AL.mult, 16 * (b - a))
            ts(sl("nA16", a, b), c("t40", 8 * a, 8 * b), float(W), AL.add, 40)
            fs(Gj(a, b), ind(v("volE"), sl("nA16", a, b)), 128 * (b - a), lend=1.0)
            tt(sl("pre", a, b), c("t40", 8 * a, 8 * b), c("lane1", 8 * a, 8 * b), AL.subtract, 16 * (b - a))
            mm([(c("P2", 440 + 16 * (j - a), 456 + 16 * (j - a)), Gj(j, j + 1), v("hcm"), True, True, 64) for j in range(a, b)])
            fs(v("hc", S_(a, b)), c("P2", 440, 440 + 16 * (b - a)), 48)
            if a == 4 and CFG["fast"][t]:
                return
            mm([(c("P1", 128 * (j - a + 1), 128 * (j - a + 2)), Gj(j, j + 1), selQ, True, True, 128) for j in range(a, b)])
            fs(v("OL", S_(a, b), *data), c("P1", 128, 128 * (b - a + 1)), 128 * (b - a), relu=True)
            for k in range(8):
                for j in range(a, b):
                    ts(v("OH", 5 * k + j), v("ring"), v("hc", j, S_(k, k + 1)), AL.is_equal, 56)

        def tally(a, b, first=None):
            out = []
            for h in range(4):
                out += grp(pair("P2", h, 0, 112), ([(v("cb", 0, S_(32 * h, 32 * h + 32)), first, 112)] if first else []) +
                           [(half("OL", j, m), v("OH", 5 * ((m + 1) % 8) + j), 112) for j in range(a, b) for m in (2 * h, 2 * h + 1)])
            return out

        def equal(a, b):
            n = 128 * (b - a)
            per = 512 // n
            for k0 in range(0, 8, per):
                bank = "P%d" % (3 + (k0 // per) % 2)
                mm([(c(bank, n * (k - k0), n * (k - k0 + 1)), v("selP", k), Gj(a, b), True, True, n) for k in range(k0, k0 + per)])
                for k in range(k0, k0 + per):
                    for j in range(a, b):
                        x = n * (k - k0) + 128 * (j - a)
                        ts(v("EQ", k, S_(128 * j - 128, 128 * j)), c(bank, x, x + 128), v("hc", j, S_(8 + k, 9 + k)), AL.is_equal, 128)

        def first(a, b):
            n = 128 * (b - a)
            a0 = 0 if a == 1 else a
            mm(grp(c("P3", 0, n), [(c("wpad", 112 - 16 * k, 240 - 16 * k), v("EQ", k, S_(128 * a - 128, 128 * b - 128)), n) for k in range(8)]))
            fs(c("Wb", 128 * a - 128, 128 * b - 128), c("P3", 0, n), n)
            mm(grp(c("P4", 0, 8 * (b - a)), [(c("Dq", 15 - q, 143 - q), c("Wb", 128 * a - 128 + q, 128 * b - 128, 16), 64) for q in range(16)]))
            tt(c("ff", 8 * a, 8 * b), c("P4", 0, 8 * (b - a)), c("thr", 8 * a, 8 * b), AL.is_lt, 32)
            if a0 < a:
                fv(c("ff", 0, 8), sl("th", 0, 1), 8)
            f = c("ff", 8 * a0, 8 * b)
            tt(f, f, sl("pre", a0, b), AL.mult, 64)
            tt(f, f, c("dump", 8 * a0, 8 * b), AL.add, 64)
            cp(sl("off16", a0, b), f, 32)

        names(0)
        for j in range(1, 5):
            off = sl("o16", j - 1, j)
            fs(v("raw"), ind(v("ntb"), off), 128)
            ts(v("bn"), v("b16", e, j - 1), 1.0, AL.mult, 64)
            cuts = CFG["split"][t]
            for a, b in zip(cuts, cuts[1:]):
                fs(c("Vg", 16 * a, 16 * b), ind(v("volE"), v("b16", e, j - 1, S_(a, b))), 16 * (b - a), lend=CFG["lendv"][t])
            level(j - 1)
            named = c("P1", 128, 256) if CFG["eqlast"][j - 1] else c("P0", 0, 128)
            mm([(named, v("bn"), v("Ih", 0), True, True, 128)])
            mm(grp(c("P1", 0, 128), [(v("raw"), If, 512), (v("bn"), v("Ih", 1), 128)]))
            odd, late = c("P0", 129, 384, 2), bool(CFG["eqlast"][j - 1])
            listed = [(odd, negI, v("eq", i), False, late and i == j - 1, 128) for i in range(j)]
            turn = [(c("P0", 128 + 2 * k, 384, 32), c("Vg", k, 2048, 16), I8, False, not late and k == 15, 64) for k in range(16)]
            mm([(c("P0", 128, 384), Ib, v("top"), True, False, 256), (odd, v("bn"), v("Ih", 0), False, False, 128)])
            for i in range(j):
                tt(v("eq", i), named, v("Bc", i), AL.is_equal, 128)
            fs(c("A2", 1, 256, 2), c("P1", 0, 128), 128, 2.0 ** 16)
            if not late:
                mm(listed)
            held = v("Bc", j - 1, S_(0, 128, 16))
            if j == 4:
                fs(v("XE"), ind(v("volE"), off), 128)
                mm(grp(c("P2", 224, 232), [(Gj(i, i + 1), I8, 64) for i in range(3)] + [(v("XE"), I8, 64)]) +
                   [(c("P2", 232, 240), Gj(0, 1), I8, True, True, 64)])
                ts(bo(0), c("P2", 232, 240), 0.5, AL.is_lt, 8, 4095.0 * 4096, AL.mult)
                ts(bo(1), c("P2", 224, 232), 43.5, AL.is_gt, 8, 4095.0 * 4096, AL.mult)
                tt(bo(2), bo(0), bo(1), AL.add, 16)
                tt(bo(4), bo(2), held, AL.add, 16)
                if CFG["fast"][t]:
                    fv(bo(3), bo(2), 8, 1.0, 4095.5)
            cuts = CFG["batch"][t]
            part("marks", t)
            if j in cuts:
                a = cuts[cuts.index(j) - 1]
                if a < 3:
                    ts(sl("nW", a, min(j, 3)), sl("o16", a, min(j, 3)), -float(W), AL.add, 24)
                tt(c("ne", 8 * max(a, 1), 8 * j), sl("nW", max(a, 1), j), sl("nW", max(a, 1) - 1, j - 1), AL.not_equal, 32)
                tt(sl("th", a, j), c("ne", 8 * a, 8 * j), c("mm", 8 * a, 8 * j), AL.mult, 48)
                present(a, j)
                if j == 3 and CFG["early"][t]:
                    mm(tally(0, 3))
                    fs(v("nA"), c("P2", 0, 112), 112)
            part("step%d" % j, t)
            if j == 4:
                held = bo(4)
            mm(turn)
            if late:
                mm(listed)
            scan(v("KS"), v("A2"), c("P0", 128, 384), 0.0, AL.mult, AL.add, 256)
            scan(v("SC"), v("rmask"), c("KS", 1, 256, 2), 0.0, AL.mult, AL.max, 128)
            ka, won = v("ka"), c("SC", 15, 128, 16)
            tt(ka, won, held, AL.max, 16)
            ts(v("kb"), ka if j == 4 else won, BIG, AL.add, 8, -BIG, AL.add)
            tt(c("hold", 0, 128, 16), ka, v("kb"), AL.subtract, 16)
            if j == 4 and CFG["fast"][t]:
                for x in (0, 3):
                    tt(v("dig", 0, S_(x, 56, 7)), won, held, AL.max, 16)
                tt(bo(5), won, bo(3), AL.is_gt, 16)
                scan(v("dig", 2), v("dig", 1), v("dig", 0), 0.0, AL.mult, AL.add, 56)
                tt(bo(6), v("dig", 2, S_(3, 56, 7)), v("dig", 2, S_(6, 56, 7)), AL.subtract, 16)
                for k in range(8):
                    ts(v("OH", 5 * k + 4), v("ring16"), v("dig", 2, S_(7 * k + 6, 7 * k + 7)), AL.is_equal, 56)
                for k in range(8):
                    m = (k - 1) % 8
                    ts(v("OL", 4, m // 2, 2 * (m % 2)), v("q16"), c("bo", 48 + k, 49 + k), AL.is_equal, 16, c("bo", 40 + k, 41 + k), AL.mult)
            scan(v("MK"), v("qmask"), v("hold"), 0.0, AL.mult, AL.add, 128)
            if j < 4:
                scan(v("Bc", j), v("rmask"), v("hold"), 0.0, AL.mult, AL.add, 128)
            mm(grp(c("P0", 0, 8), [(Ib, v("cW"), 64), (v("hold"), v("cmh", 1), 64), (v("MK"), v("cmh", 0), 64)]))
            ts(sl("o16", j, j + 1), c("P0", 0, 8), float(W), AL.add, 8)
            ops[-1]["due"] = CFG["duel"][t] + (4 - j) * CFG["pace"][t]
            if j == 4:
                tt(sl("th", 4, 5), c("P0", 0, 8), sl("nW", 3, 4), AL.not_equal, 8)
            if j > 2:
                cp(sl("nW", j, j + 1), c("P0", 0, 8), 8)
            names(j)
        if CFG["stages"][t] == 1:
            level(4)
        mm(tally(3, 4, v("nA")) if CFG["early"][t] else tally(0, 4))
        fs(v("nA"), c("P2", 0, 112), 112)
        part("equal", t)
        cuts = CFG["ecut"][t]
        for a, b in zip(cuts, cuts[1:]):
            equal(a, b)
        first(1, 4)
        part("counts", t)
        if not CFG["fast"][t]:
            present(4, 5)
        mm(tally(4, 5, v("nA")))
        cp(v("nS"), c("P2", 0, 32), 32)
        exchange([(c("nS", 16, 32), v("nR", t, S_(0, 16)))], [(c("nS", 0, 16), v("nR", t, S_(16, 32)))], 2.2)
        cp(v("nF", t, S_(32, 112)), c("P2", 32, 112), 80)
        if not last:
            x0 = (STEP * (t + 1)) % V // 16
            tt(c("smallR", 0, 88 - x0), c("P2", 24 + x0, 112), c("thr1", 24 + x0, 112), AL.is_gt, 64)
            tt(c("smallR", 104 - x0, 96), c("P2", 32, 24 + x0), c("thr1", 32, 24 + x0), AL.is_gt, 80)
            ts(c("hh", 32, 112), c("P2", 32, 112), 3.0, AL.min, 80)
            tt(c("thB", 8, 24), c("thr1", 8, 24), c("nS", 8, 24), AL.subtract, 32)
            tt(c("qu", 32, 112), c("qa", 32, 112), c("hh", 32, 112), AL.subtract, 160)
        if CFG["fast"][t]:
            present(4, 5)
        part("equal4", t)
        equal(4, 5)
        first(4, 5)
        part("counts", t)
        if not last:
            ts(c("volN", 32, 112), c("qu", 32, 112), 1.0, AL.max, 80, 16.0, AL.min)
            for (a, b), bank in zip(((32, 64), (64, 96), (96, 112)), CFG["vbank"]):
                spread_volumes(a, b, bank)
        mm([(c("P2", 240, 320), shm, v("nF", t, S_(32, 112)), True, True, 80)])
        ts(v("nOff", e, S_(8, 88)), c("P2", 240, 320), 7.0, AL.add, 80)
        tt(v("nF", t, S_(0, 32)), v("nS"), v("nR", t), AL.add, 64)

    def border_counts(t):
        out = []
        for k, r in enumerate((8, 24, 0, 16)):
            out += grp(c("P2", 320 + 8 * k, 328 + 8 * k), [(shm, v("nF", t, S_(r, r + 8)), 64), (Ib, c("wb", 8 * k, 8 * k + 8), 64)])
        mm(out)
        ts(v("nOff", t % 2, S_(88, 120)), c("P2", 320, 352), 7.0, AL.add, 32)

    def fields(t):
        last = t == RO - 1
        e = t % 2
        uw = c("Wf", 0, W)
        sl = lambda name, a, b: v(name, e, S_(8 * a, 8 * b))
        part("mean", t)
        fs(c("um", 0, 512), ind(uw, sl("o16", 0, 4)), 512, lend=CFG["lend"][t])
        fs(c("um", 512, 640), ind(uw, sl("o16", 4, 5)), 128)
        mm(grp(c("P6", 256, 288), [(c("Dq", 15 - q, 143 - q), v("G", e, S_(q, 512, 16)), 64) for q in range(16)]))
        fs(c("Zq", 0, 32), c("P6", 256, 288), 32)
        mm(grp(c("P6", 288, 296), [(Ib, c("Zq", 8 * i, 8 * i + 8), 64) for i in range(4)] +
               [(c("Dq", 15 - q, 143 - q), v("G", e, S_(512 + q, 640, 16)), 64) for q in range(16)]))
        mm(grp(c("P6", 128, 256), [(selE, v("G", e, S_(128 * j, 128 * j + 128)), 128) for j in range(1, 5)]))
        ts(v("z16", e), c("P6", 288, 296), 7.0, AL.add, 8)
        fs(v("wZ"), ind(c("wall", 0, WT), v("z16", e)), 128, UP * UP)
        mm([(v("P5"), selV, v("G", e, S_(0, 512)), True, True, 512)])
        for a in (0, 256):
            tt(c("prod", a, a + 256), c("P5", a, a + 256), c("um", a, a + 256), AL.mult, 256)
        mm([(c("P7", 128, 256), selV, v("G", e, S_(512, 640)), True, True, 128)] +
           grp(c("P7", 256, 384), [(negf, c("um", 0, 128), 512), (If, c("um", 512, 640), 512)]))
        tt(c("prod", 512, 640), c("P7", 128, 256), c("um", 512, 640), AL.mult, 128)
        fs(v("Dd"), c("P7", 256, 384), 128, UP)
        mm(grp(c("P7", 384, 512), [(If, c("prod", 128 * j, 128 * j + 128), 512) for j in range(5)]))
        tt(v("De"), c("P6", 128, 256), v("Dd"), AL.mult, 128)
        tt(v("Mm"), c("P7", 384, 512), v("wZ"), AL.mult, 128)
        if CFG["est"]:
            tt(v("Mm"), v("Mm"), v("De"), AL.subtract, 256)
        for j in (1, 2, 0, 3, 4):
            mm(grp(c("P5", 128 * j - 128, 128 * j) if j else c("P7", 0, 128),
                   [(v("cf", 1 + j), v("Dd"), 512)] * (j > 0) + [(negf, v("De"), 512)] * (1 - CFG["est"]) + [(If, v("Mm"), 512)]))
        back = lambda a, b, s=1: S_(b - 1, a - 1 if a else None, -s)

        def bound(a, n, o):
            scan(c("Omin", o, o + n), c("Ug", a, a + 2 * n, 2), c("Ug", a + 1, a + 2 * n, 2), 1e29, AL.min, AL.min, n)
            scan(v("Omax", back(o, o + n)), v("Ug", back(a, a + 2 * n - 1, 2)), v("Ug", back(a + 1, a + 2 * n, 2)), 0.0, AL.max, AL.max, n)

        part("bounds", t)
        m = 6 - CFG["stages"][t]
        for j in range(m):
            cuts = CFG["per"][t]
            for a, b in zip(cuts, cuts[1:]):
                fs(c("Ug", 16 * m * a + j, 16 * m * b, m), ind(v("Wf"), v("b16", e, j, S_(a, b))), 16 * (b - a), lend=CFG["lend"][t])
        part("scans", t)
        for i in range(0, 128, 2):
            bound(16 * m * i, 16 * m, 8 * m * (i % 32))
            if i % 32 == 30 and CFG["unS"][t]:
                for h in range(2):
                    fs(c("Rlo", i - 30 + h, i + 2, 2), c("Omin", 8 * m * (h + 1) - 1, 256 * m, 16 * m), 16, UP * 256.0 ** h)
                    fs(c("Rhi", i - 30 + h, i + 2, 2), c("Omax", 8 * m * h, 256 * m, 16 * m), 16, UP * 256.0 ** h)
            elif i % 32 == 30:
                tt(c("Rlo", i - 30, i + 2), c("Omin", 8 * m - 1, 256 * m, 8 * m), v("un"), AL.mult, 64)
                tt(c("Rhi", i - 30, i + 2), c("Omax", 0, 256 * m, 8 * m), v("un"), AL.mult, 64)
        if m == 4:
            part("late", t)
            for a in range(0, 128, 32):
                tt(c("Ug", 8192 + 16 * a, 8704 + 16 * a), ind(uw, v("b16", e, 4, S_(a, a + 32))), v("lev"), AL.mult, 512)
            for i in range(0, 128, 8):
                bound(8192 + 16 * i, 64, 1280 + 8 * i)
            for o, src, x, y, f in (("Rlo", "Omin", 1287, 256, AL.min), ("Rhi", "Omax", 1280, 384, AL.max)):
                tt(c("P6", y, y + 128), c(src, x, 2304, 8), v("un8"), AL.mult, 256)
                tt(v(o), c("P6", y, y + 128), v(o), f, 128)
        part("sums", t)
        sw = c("Wf", 0, UB)
        for j in (1, 2, 0, 3, 4):
            x = c("P5", 128 * j - 128, 128 * j) if j else c("P7", 0, 128)
            tt(x, x, v("Rlo"), AL.max, 128)
            tt(c("ec", 128 * j, 128 * j + 128), x, v("Rhi"), AL.min, 128)
        for two, bank in zip(((1, 2), (3, 4)), ("P0", "P1") if last else ("P3", "P4")):
            turned = lambda j: c(bank, 128 * (j % 2), 128 * (j % 2) + 128)
            for j in two:
                mm([(turned(j), c("ec", 128 * j, 128 * j + 128), If, True, True, 512)])
            for j in two:
                (cp if CFG["hiV"][t] else act)(v("Zp", 2 * j - 2, *data), turned(j), 128)
            for j in two:
                tt(v("Zp", 2 * j - 1, *data), turned(j), v("Zp", 2 * j - 2, *data), AL.subtract, 128)
        for j in range(1, 5):
            zh, zl, bank = 2 * j - 2, 2 * j - 1, "P%d" % (7 - j % 2)
            for h in range(4):
                mm(grp(pair(bank, h, 0, 128), [(half("Zp", z, k), v("EQ", k, S_(128 * j - 128, 128 * j)), 128)
                                               for z in (zh, zl) for k in (2 * h, 2 * h + 1)]))
            fs(v("Ss", j - 1), c(bank, 0, 128), 128)
        for j in range(5):
            off = sl("off16", j, j + 1)
            if j:
                tt(v("tg", j - 1), ind(sw, off), v("Ss", j - 1), AL.add, 128)
            put(ind(sw, off), v("tg", j - 1) if j else c("ec", 0, 128), CFG["silu"][t])
        Rb = "Rb%d" % t
        if last:
            exchange([(c("Wf", V, 1664), c(Rb, 128, 256))], [(c("Wf", 1664, W), c(Rb, 0, 128))], 2.6)
        else:
            exchange([(c("Wf", V, 1664), c(Rb, 128, 256)), (c("Wf", 0, 128), c(Rb, 384, 512))],
                     [(c("Wf", 1664, W), c(Rb, 0, 128)), (c("Wf", 1408, V), c(Rb, 256, 384))], 3.0)
        end = 96 if last else 112
        part("weigh", t)

        def weigh(a, b, src, x):
            tt(c("Wf", 16 * a, 16 * b), ind(v("wall"), v("nOff", e, S_(x, x + b - a))), src, AL.mult, 16 * (b - a))
            ops[-1]["due"] = CFG["due"][t]
            if last:
                dma("sync", v("y", S_(16 * a, 16 * b)), c("Wf", 16 * a, 16 * b), 2.0 + (b - a) * 0.03)
            else:
                scaled(16 * a, 16 * b)
        n = 16 * end - 1280
        mm([(c("P5", 0, 128), If, c("Wf", 0, 128), True, True, 512)] +
           [(c("P5", a, a + 128), If, c("Wf", 1280 + a, 1408 + a), True, True, 512) for a in range(128, n, 128)])
        cuts = CFG["weigh"]
        for a, b in zip(cuts, cuts[1:]):
            weigh(a, b, c("Wf", 16 * a, 16 * b), a)
        tt(c(Rb, 0, n), c("P5", 0, n), c(Rb, 0, n), AL.add, n)
        weigh(88, end, c(Rb, 128, n), 88)
        weigh(0, 8, c(Rb, 0, 128), 112)

    for f, t in [(lanes, 0), (lists, 0), (lanes, 1), (fields, 0), (lists, 1), (lanes, 2), (fields, 1), (lists, 2), (fields, 2)]:
        part("lanes" if f is lanes else "step0" if f is lists else "start", t)
        if f is fields:
            border_counts(t)
        f(t)

    if "order" not in PLAN:
        PLAN["order"], PLAN["eng"] = plan(ops)
    queue = {"pool": g, "vector": g.vector, "scalar": g.scalar, "tensor": g.tensor, "sync": g.sync}
    token, count, seen, n_d = {}, {}, {}, 0
    for i in PLAN["order"]:
        o = ops[i]
        e = PLAN["eng"][i]
        if e == "ext":
            token[i] = o["k"]
            continue
        need = {}
        for d in o["deps"]:
            s, val = token[d]
            need[s] = max(need.get(s, 0), val)
        for s in sorted(need):
            if seen.get((e, s), 0) < need[s]:
                queue[e].wait_ge(T.sem[s], need[s])
                seen[(e, s)] = need[s]
        ins = o["alt"][e][1](queue[e])
        if o["k"] == "c":
            count[e] = count.get(e, 0) + 1
            token[i] = ("c_" + e, count[e])
            ins.then_inc(T.sem["c_" + e], 1)
        elif o["k"] == "dma":
            token[i] = ("d%d" % n_d, 16)
            ins.then_inc(T.sem["d%d" % n_d], 16)
            n_d += 1
        else:
            token[i] = o["k"]
    most_ = {}
    for s, val in token.values():
        most_[s] = max(most_.get(s, 0), val)
    for s in sorted(most_):
        if seen.get(("pool", s), 0) < most_[s]:
            g.wait_ge(T.sem[s], most_[s])
